import numpy as np
import ml_dtypes


def mxq(x, axis, fmt="e4m3"):
    dtype, down = {"e4m3": (ml_dtypes.float8_e4m3fn, 7), "e5m2": (ml_dtypes.float8_e5m2, 14)}[fmt]
    v = np.moveaxis(np.asarray(x, np.float32).astype(ml_dtypes.bfloat16).astype(np.float64), axis, -1)
    blocks = v.reshape(v.shape[:-1] + (-1, 32))
    amax = np.abs(blocks).max(-1, keepdims=True)
    byte = np.maximum(np.where(amax > 0, np.frexp(amax)[1] - 1 + 127, 0) - down, 1)
    scale = np.exp2(byte - 127.0)
    codes = (blocks / scale).astype(np.float32).astype(dtype).astype(np.float64)
    return np.moveaxis((codes * scale).reshape(v.shape), -1, axis)


WIDE = False


def mx_kscale(k):
    if not WIDE:
        return np.ones(k)
    levels = np.array([10, -10, 5, -5, 0])
    if k % 512:
        return np.exp2(np.random.permutation(np.resize(levels, k // 32))).repeat(32)
    a = np.empty((k // 512, 16))
    for p in range(k // 512):
        a[p, :8] = np.random.permutation(np.resize(levels, 8))
        for g in range(8):
            far = levels[np.abs(levels - a[p, g]) >= 10]
            a[p, g + 8] = far[np.random.randint(len(far))]
    return np.exp2(a.ravel()).repeat(32)


def f64(x):
    return np.asarray(x).astype(np.float64)


def striped(idx):
    return np.tile(idx.reshape(-1, 16).T, (8, 1)).astype(np.uint16)


def unstriped(offs):
    return offs[:16].T.reshape(-1).astype(np.int64)


E2M1 = np.array([0.0, 0.5, 1.0, 1.5, 2.0, 3.0, 4.0, 6.0, -0.0, -0.5, -1.0, -1.5, -2.0, -3.0, -4.0, -6.0])


def pack_weight(w, fmt):
    k, n = w.shape
    w = f64(np.asarray(w, np.float32).astype(ml_dtypes.bfloat16)).reshape(k // 32, 32, n)
    amax = np.abs(w).max(1)
    if fmt == "e4m3":
        byte = np.frexp(amax)[1] - 1 + 127 - 7
    else:
        mant, ex = np.frexp(amax / 6.0)
        byte = np.where(mant > 0.5, ex, ex - 1) + 127
    byte = np.clip(np.where(amax > 0, byte, 1), 1, 254)
    scaled = (w * np.exp2(127.0 - byte)[:, None, :]).reshape(k, n).astype(np.float32)
    by_word = np.ascontiguousarray(scaled.reshape(k // 512, 128, 4, n).transpose(0, 1, 3, 2))
    if fmt == "e4m3":
        words = by_word.astype(ml_dtypes.float8_e4m3fn).view(np.uint8)
    else:
        c = by_word.astype(ml_dtypes.float4_e2m1fn).view(np.uint8) & 0xF
        words = (c[..., 0::2] | (c[..., 1::2] << 4)).reshape(k // 512, 128, 2 * n)
    return np.ascontiguousarray(words), np.ascontiguousarray(byte.astype(np.uint8).reshape(k // 512, 16, n))


def unpack_weight(words, scales, fmt):
    g, _, n = scales.shape
    words = np.ascontiguousarray(words).reshape(g, 128, n, -1)
    if fmt == "e4m3":
        vals = words.view(ml_dtypes.float8_e4m3fn).astype(np.float64)
    else:
        nib = np.empty((g, 128, n, 4), np.uint8)
        nib[..., 0::2] = words & 0xF
        nib[..., 1::2] = words >> 4
        vals = E2M1[nib]
    vals = vals * np.repeat(np.exp2(scales.astype(np.float64) - 127.0), 8, axis=1)[..., None]
    return vals.transpose(0, 1, 3, 2).reshape(g * 512, n)


def gelu(v):
    return 0.5 * v * (1.0 + np.tanh(np.sqrt(2.0 / np.pi) * (v + 0.044715 * v**3)))


K, T, S, P, P2, H, N = 1024, 2048, 1024, 512, 256, 1024, 512

def setup_inputs():
    n = np.random.standard_normal
    s = mx_kscale(K)[:, None]
    u = mx_kscale(H)[:, None]
    tab_words, tab_scales = pack_weight(n((K, T)) * s, "e4m3")
    w2_words, w2_scales = pack_weight(n((H, N)) / np.sqrt(H) / u, "e2m1")
    perm = np.random.permutation(S)
    perm2 = np.random.permutation(P)
    return {
        "tab_words": tab_words,
        "tab_scales": tab_scales,
        "offs": striped(np.random.permutation(T)[:S]),
        "w1": (n((K, H)) / np.sqrt(K) / s * u.T).astype(np.float32),
        "pos1": striped(perm[:P]),
        "pos2": striped(perm[P:]),
        "w2_words": w2_words,
        "w2_scales": w2_scales,
        "pos3": striped(perm2[:P2]),
        "pos4": striped(perm2[P2:]),
        "w": n(N).astype(np.float32),
    }

def reference(tab_words, tab_scales, offs, w1, pos1, pos2, w2_words, w2_scales, pos3, pos4, w):
    v = unpack_weight(tab_words, tab_scales, "e4m3")[:, unstriped(offs)]
    h = mxq(f64(w1), 0, "e4m3").T @ v
    z = np.maximum(h[:, unstriped(pos1)], h[:, unstriped(pos2)])
    w2 = unpack_weight(w2_words, w2_scales, "e2m1")
    y = w2.T @ mxq(z, 0, "e4m3")
    left = y[:, unstriped(pos3)]
    right = y[:, unstriped(pos4)]
    gate = 1.0 / (1.0 + np.exp(-right))
    out = left + gate * (f64(w)[:, None] - left)
    return out

@@ -1,0 +1,251 @@
+from contextlib import ExitStack
+
+import concourse.mybir as mybir
+
+K, T, S, PAIRS, DOCS, H, N = 1024, 2048, 1024, 512, 256, 1024, 512
+FLOPS = 2 * K * H * S + 2 * H * N * PAIRS
+
+F32 = mybir.dt.float32
+BF16 = mybir.dt.bfloat16
+I32 = mybir.dt.int32
+U32 = mybir.dt.uint32
+U16 = mybir.dt.uint16
+U8 = mybir.dt.uint8
+FP8X4 = mybir.dt.float8_e4m3fn_x4
+FP4X4 = mybir.dt.float4_e2m1fn_x4
+ALU = mybir.AluOpType
+ACT = mybir.ActivationFunctionType
+
+P = 128
+PACK = 4
+K_PASS = P * PACK
+BANK = 512
+
+
+def tile_list_passage_document_coarsening_kernel(
+    tc, tab_words, tab_scales, offs, w1, pos1, pos2, w2_words, w2_scales, pos3, pos4, w, out
+):
+    nc = tc.nc
+    with ExitStack() as ctx:
+        keep = ctx.enter_context(tc.tile_pool(name="keep", bufs=1))
+        psum = ctx.enter_context(tc.psum_pool(name="psum", bufs=1))
+
+        def load_list(name, src, entries):
+            tile = keep.tile([P, entries // 16], U16, name=name)
+            nc.sync.dma_start(tile[:], src)
+            return tile
+
+        def load_w1(b, a, parts=1):
+            tiles = []
+            width = K_PASS // parts
+            for part in range(parts):
+                tile = keep.tile([P, PACK, width], F32, name=f"w1_raw_{b}_{a}_{part}")
+                start = b * K_PASS + part * width
+                rows = w1[a * K_PASS : (a + 1) * K_PASS, start : start + width]
+                nc.sync.dma_start(tile[:], rows.rearrange("(p j) c -> p j c", j=PACK))
+                tiles.append(tile)
+            return tiles
+
+        def load_table(a):
+            words = keep.tile([P, T], U32, name=f"table_{a}")
+            nc.sync.dma_start(words[:].bitcast(I32), tab_words[a].rearrange("p t i -> p (t i)").bitcast(I32))
+            return words
+
+        table_scales = keep.tile([P, T], U8, name="table_scales")
+        w2_planes = keep.tile([P, 2, N], U8, name="w2_planes", align_bytes=64)
+        warm_in = keep.tile([P, 1], F32, name="warm_in")
+        warm_out = keep.tile([P, 1], F32, name="warm_out")
+        nc.vector.memset(table_scales[:].bitcast(I32), 0)
+        nc.vector.memset(warm_in[:], 0.0)
+        nc.vector.memset(w2_planes[:].bitcast(I32), 0)
+
+        offs_t = load_list("offs_t", offs, S)
+        nc.scalar.activation(warm_out[:], warm_in[:], ACT.Sigmoid)
+        raw = {}
+        table = [load_table(0)]
+        pos1_t = load_list("pos1_t", pos1, PAIRS)
+        pos2_t = load_list("pos2_t", pos2, PAIRS)
+        for q in range(4):
+            nc.sync.dma_start(
+                table_scales[32 * q : 32 * q + 8, :].bitcast(I32), tab_scales[:, 4 * q : 4 * q + 4, :].bitcast(I32)
+            )
+        raw[0, 0] = load_w1(0, 0)
+        table.append(load_table(1))
+        raw[0, 1] = load_w1(0, 1, parts=2)
+        raw[1, 0] = load_w1(1, 0)
+        raw[1, 1] = load_w1(1, 1)
+        w2_codes = keep.tile([P, 2, 2 * N], U8, name="w2_codes", align_bytes=64)
+        nc.sync.dma_start(w2_codes[:].bitcast(I32), w2_words.rearrange("a p c -> p a c").bitcast(I32))
+        for q in range(4):
+            nc.sync.dma_start(
+                w2_planes[32 * q : 32 * q + 4, :, :].bitcast(I32),
+                w2_scales[:, 4 * q : 4 * q + 4, :].rearrange("a r c -> r a c").bitcast(I32),
+            )
+        pos3_t = load_list("pos3_t", pos3, DOCS)
+        pos4_t = load_list("pos4_t", pos4, DOCS)
+        w_col = keep.tile([P, N // P], F32, name="w_col")
+        with nc.allow_non_contiguous_dma(reason="one value of w for each partition"):
+            nc.sync.dma_start(w_col[:], w.rearrange("(c p) -> p c", p=P))
+
+        w1_codes = {}
+        w1_planes = {}
+        w1_bf16 = {}
+        for b in range(2):
+            for u in range(2):
+                w1_bf16[b, u] = keep.tile([P, 4 * K_PASS], BF16, name=f"w1_bf16_{b}_{u}", align_bytes=64)
+                w1_codes[b, u] = keep.tile([P, 4 * P], U32, name=f"w1_codes_{b}_{u}", align_bytes=64)
+                w1_planes[b, u] = keep.tile([P, 4 * P], U8, name=f"w1_plane_{b}_{u}", align_bytes=64)
+
+        def round_w1(b, a, u):
+            width = P // len(raw[b, a])
+            grouped = w1_bf16[b, u][:, 2 * a * K_PASS : 2 * (a + 1) * K_PASS].rearrange("p (t m j) -> p m j t", t=2, j=PACK)
+            for part, tile in enumerate(raw[b, a]):
+                src = tile[:].rearrange("p j (m t) -> p m j t", t=PACK)[:, :, :, 2 * u : 2 * u + 2]
+                nc.scalar.copy(grouped[:, part * width : (part + 1) * width, :, :], src)
+
+        def quantize_w1(b, u, start, stop):
+            nc.vector.quantize_mx(
+                out=w1_codes[b, u][:, start * P : stop * P].bitcast(FP8X4),
+                scales=w1_planes[b, u][:, start * P : stop * P],
+                in_=w1_bf16[b, u][:, start * K_PASS : stop * K_PASS],
+            )
+
+        v_scales = keep.tile([P, S], U8, name="v_scales", align_bytes=64)
+        v_codes = [keep.tile([P, S], U32, name=f"v_codes_{a}", align_bytes=64) for a in range(2)]
+
+        nc.vector.tensor_copy(v_codes[0][:], table[0][:].indirect(offs_t[:]))
+        nc.vector.tensor_copy(v_scales[:], table_scales[:].indirect(offs_t[:]))
+        round_w1(0, 0, 0)
+        round_w1(0, 0, 1)
+        quantize_w1(0, 0, 0, 2)
+        nc.vector.tensor_copy(v_codes[1][:], table[1][:].indirect(offs_t[:]))
+        round_w1(0, 1, 0)
+        quantize_w1(0, 0, 2, 3)
+        quantize_w1(0, 0, 3, 4)
+        round_w1(0, 1, 1)
+        quantize_w1(0, 1, 0, 4)
+
+        h = {}
+
+        def make_h(b, t):
+            ht = keep.tile([P, S], F32, name=f"h_{b}_{t}")
+            u, e = divmod(t, 2)
+            banks = [psum.tile([P, BANK], F32, name=f"h_bank_{b}_{t}_{half}", tag=f"bank_{2 * t + half}") for half in range(2)]
+            for a in range(2):
+                rows = slice((2 * a + e) * P, (2 * a + e + 1) * P)
+                for half in range(2):
+                    cols = slice(half * BANK, (half + 1) * BANK)
+                    nc.tensor.matmul_mx(
+                        out=banks[half][:],
+                        lhsT=w1_codes[b, u][:, rows].bitcast(FP8X4),
+                        lhsT_scale=w1_planes[b, u][:, rows],
+                        rhs=v_codes[a][:, cols].bitcast(FP8X4),
+                        rhs_scale=v_scales[4 * a : P, cols],
+                        start=(a == 0),
+                        stop=(a == 1),
+                    )
+            nc.scalar.copy(ht[:, 0:BANK], banks[0][:])
+            if (b, t) == (0, 0):
+                nc.vector.tensor_copy(ht[:, BANK:S], banks[1][:])
+            else:
+                nc.scalar.copy(ht[:, BANK:S], banks[1][:])
+            h[b, t] = ht
+
+        first = [keep.tile([P, PACK, PAIRS], F32, name=f"first_{b}") for b in range(2)]
+        second = [keep.tile([P, PACK, PAIRS], F32, name=f"second_{b}") for b in range(2)]
+
+        def pick_h(b, t, start=0, stop=PAIRS):
+            entries = slice(start // 16, stop // 16)
+            nc.vector.tensor_copy(first[b][:, t, start:stop], h[b, t][:].indirect(pos1_t[:, entries]))
+            nc.vector.tensor_copy(second[b][:, t, start:stop], h[b, t][:].indirect(pos2_t[:, entries]))
+
+        z_bf16 = [keep.tile([P, PAIRS * PACK], BF16, name=f"z_bf16_{b}", align_bytes=64) for b in range(2)]
+        z_codes = [keep.tile([P, PAIRS], U32, name=f"z_codes_{b}", align_bytes=64) for b in range(2)]
+        z_planes = [keep.tile([P, PAIRS], U8, name=f"z_plane_{b}", align_bytes=64) for b in range(2)]
+
+        def pair_max(b, start, stop):
+            nc.vector.tensor_tensor(
+                z_bf16[b][:, start * PACK : stop * PACK].rearrange("p (c i t) -> p c t i", i=4, t=PACK),
+                first[b][:, :, start:stop].rearrange("p t (c i) -> p c t i", i=4),
+                second[b][:, :, start:stop].rearrange("p t (c i) -> p c t i", i=4),
+                ALU.max,
+            )
+
+        def quantize_z(b, start, stop):
+            nc.vector.quantize_mx(
+                out=z_codes[b][:, start:stop].bitcast(FP8X4),
+                scales=z_planes[b][:, start:stop],
+                in_=z_bf16[b][:, start * PACK : stop * PACK],
+            )
+
+        EARLY = PAIRS - P
+
+        def multiply_z(b, c, bank, start, stop):
+            for m in range(start, stop, P):
+                nc.tensor.matmul_mx(
+                    out=bank[:, m - start : m - start + P],
+                    lhsT=w2_codes[:, b, 2 * c * P : 2 * (c + 1) * P].bitcast(FP4X4),
+                    lhsT_scale=w2_planes[:, b, c * P : (c + 1) * P],
+                    rhs=z_codes[b][:, m : m + P].bitcast(FP8X4),
+                    rhs_scale=z_planes[b][:, m : m + P],
+                    start=(b == 0 and m == start),
+                    stop=(b == 1 and m == stop - P),
+                )
+
+        make_h(0, 0)
+        make_h(0, 1)
+        pick_h(0, 0)
+        round_w1(1, 0, 0)
+        make_h(0, 2)
+        pick_h(0, 1)
+        round_w1(1, 1, 0)
+        make_h(0, 3)
+        pick_h(0, 2)
+        round_w1(1, 0, 1)
+        round_w1(1, 1, 1)
+        quantize_w1(1, 0, 0, 4)
+        make_h(1, 0)
+        pick_h(0, 3)
+        quantize_w1(1, 1, 0, 4)
+        make_h(1, 1)
+        pair_max(0, 0, PAIRS)
+        pick_h(1, 0)
+        quantize_z(0, 0, PAIRS)
+        make_h(1, 2)
+        make_h(1, 3)
+        early = [psum.tile([P, EARLY], F32, name=f"y_early_{c}", tag=f"bank_{2 * c}") for c in range(N // P)]
+        late = [psum.tile([P, P], F32, name=f"y_late_{c}", tag=f"bank_{2 * c + 1}") for c in range(N // P)]
+        for c in range(N // P):
+            multiply_z(0, c, early[c], 0, EARLY)
+            multiply_z(0, c, late[c], EARLY, PAIRS)
+        pick_h(1, 1)
+        pick_h(1, 2)
+        pick_h(1, 3, 0, EARLY)
+        pair_max(1, 0, EARLY)
+        pick_h(1, 3, EARLY, PAIRS)
+        quantize_z(1, 0, 2 * P)
+        quantize_z(1, 2 * P, EARLY)
+        pair_max(1, EARLY, PAIRS)
+        quantize_z(1, EARLY, PAIRS)
+        y = [keep.tile([P, PAIRS], F32, name=f"y_{c}") for c in range(N // P)]
+        for c in range(N // P):
+            multiply_z(1, c, early[c], 0, EARLY)
+            multiply_z(1, c, late[c], EARLY, PAIRS)
+            nc.scalar.copy(y[c][:, 0:EARLY], early[c][:])
+            if c == 0:
+                nc.vector.tensor_copy(y[c][:, EARLY:PAIRS], late[c][:])
+            else:
+                nc.scalar.copy(y[c][:, EARLY:PAIRS], late[c][:])
+
+        for c in range(N // P):
+            right = keep.tile([P, DOCS], F32, name=f"right_{c}")
+            left = keep.tile([P, DOCS], F32, name=f"left_{c}")
+            nc.vector.tensor_copy(right[:], y[c][:].indirect(pos4_t[:]))
+            nc.vector.tensor_copy(left[:], y[c][:].indirect(pos3_t[:]))
+            stay = keep.tile([P, DOCS], F32, name=f"stay_{c}")
+            nc.scalar.activation(stay[:], right[:], ACT.Sigmoid, scale=-1.0)
+            rest = keep.tile([P, DOCS], F32, name=f"rest_{c}")
+            nc.vector.scalar_tensor_tensor(rest[:], left[:], w_col[:, c : c + 1], stay[:], ALU.subtract, ALU.mult)
+            doc = keep.tile([P, DOCS], F32, name=f"doc_{c}")
+            nc.scalar.activation(doc[:], rest[:], ACT.Identity, bias=w_col[:, c : c + 1])
+            nc.sync.dma_start(out[c * P : (c + 1) * P, :], doc[:])

@@ -71,7 +71,7 @@ def tile_list_passage_document_coarsening_kernel(
             )
         raw[0, 0] = load_w1(0, 0)
         table.append(load_table(1))
-        raw[0, 1] = load_w1(0, 1, parts=2)
+        raw[0, 1] = load_w1(0, 1)
         raw[1, 0] = load_w1(1, 0)
         raw[1, 1] = load_w1(1, 1)
         w2_codes = keep.tile([P, 2, 2 * N], U8, name="w2_codes", align_bytes=64)
@@ -96,12 +96,12 @@ def tile_list_passage_document_coarsening_kernel(
                 w1_codes[b, u] = keep.tile([P, 4 * P], U32, name=f"w1_codes_{b}_{u}", align_bytes=64)
                 w1_planes[b, u] = keep.tile([P, 4 * P], U8, name=f"w1_plane_{b}_{u}", align_bytes=64)
 
-        def round_w1(b, a, u):
+        def round_w1(b, a, u, copy=nc.scalar.copy):
             width = P // len(raw[b, a])
             grouped = w1_bf16[b, u][:, 2 * a * K_PASS : 2 * (a + 1) * K_PASS].rearrange("p (t m j) -> p m j t", t=2, j=PACK)
             for part, tile in enumerate(raw[b, a]):
                 src = tile[:].rearrange("p j (m t) -> p m j t", t=PACK)[:, :, :, 2 * u : 2 * u + 2]
-                nc.scalar.copy(grouped[:, part * width : (part + 1) * width, :, :], src)
+                copy(grouped[:, part * width : (part + 1) * width, :, :], src)
 
         def quantize_w1(b, u, start, stop):
             nc.vector.quantize_mx(
@@ -119,7 +119,7 @@ def tile_list_passage_document_coarsening_kernel(
         round_w1(0, 0, 1)
         quantize_w1(0, 0, 0, 2)
         nc.vector.tensor_copy(v_codes[1][:], table[1][:].indirect(offs_t[:]))
-        round_w1(0, 1, 0)
+        round_w1(0, 1, 0, nc.vector.tensor_copy)
         quantize_w1(0, 0, 2, 3)
         quantize_w1(0, 0, 3, 4)
         round_w1(0, 1, 1)
@@ -165,9 +165,9 @@ def tile_list_passage_document_coarsening_kernel(
 
         def pair_max(b, start, stop):
             nc.vector.tensor_tensor(
-                z_bf16[b][:, start * PACK : stop * PACK].rearrange("p (c i t) -> p c t i", i=4, t=PACK),
-                first[b][:, :, start:stop].rearrange("p t (c i) -> p c t i", i=4),
-                second[b][:, :, start:stop].rearrange("p t (c i) -> p c t i", i=4),
+                z_bf16[b][:, start * PACK : stop * PACK].rearrange("p (c i t) -> p c t i", i=2, t=PACK),
+                first[b][:, :, start:stop].rearrange("p t (c i) -> p c t i", i=2),
+                second[b][:, :, start:stop].rearrange("p t (c i) -> p c t i", i=2),
                 ALU.max,
             )
 

@@ -71,7 +71,7 @@ def tile_list_passage_document_coarsening_kernel(
             )
         raw[0, 0] = load_w1(0, 0)
         table.append(load_table(1))
-        raw[0, 1] = load_w1(0, 1)
+        raw[0, 1] = load_w1(0, 1, parts=2)
         raw[1, 0] = load_w1(1, 0)
         raw[1, 1] = load_w1(1, 1)
         w2_codes = keep.tile([P, 2, 2 * N], U8, name="w2_codes", align_bytes=64)
@@ -93,14 +93,17 @@ def tile_list_passage_document_coarsening_kernel(
         for b in range(2):
             for u in range(2):
                 w1_bf16[b, u] = keep.tile([P, 4 * K_PASS], BF16, name=f"w1_bf16_{b}_{u}", align_bytes=64)
-                w1_codes[b, u] = keep.tile([P, 4 * P], U32, name=f"w1_codes_{b}_{u}", align_bytes=64)
+                w1_codes[b, u] = keep.tile(
+                    [P, 4 * P], U32, name=f"w1_codes_{b}_{u}", tag=f"w1_codes_{b}_{u}", align_bytes=64
+                )
                 w1_planes[b, u] = keep.tile([P, 4 * P], U8, name=f"w1_plane_{b}_{u}", align_bytes=64)
 
-        def round_w1(b, a, u, copy=nc.scalar.copy):
+        def round_w1(b, a, u, last_copy=nc.scalar.copy):
             width = P // len(raw[b, a])
             grouped = w1_bf16[b, u][:, 2 * a * K_PASS : 2 * (a + 1) * K_PASS].rearrange("p (t m j) -> p m j t", t=2, j=PACK)
             for part, tile in enumerate(raw[b, a]):
                 src = tile[:].rearrange("p j (m t) -> p m j t", t=PACK)[:, :, :, 2 * u : 2 * u + 2]
+                copy = last_copy if part == len(raw[b, a]) - 1 else nc.scalar.copy
                 copy(grouped[:, part * width : (part + 1) * width, :, :], src)
 
         def quantize_w1(b, u, start, stop):
@@ -127,8 +130,7 @@ def tile_list_passage_document_coarsening_kernel(
 
         h = {}
 
-        def make_h(b, t):
-            ht = keep.tile([P, S], F32, name=f"h_{b}_{t}")
+        def multiply_h(b, t):
             u, e = divmod(t, 2)
             banks = [psum.tile([P, BANK], F32, name=f"h_bank_{b}_{t}_{half}", tag=f"bank_{2 * t + half}") for half in range(2)]
             for a in range(2):
@@ -144,12 +146,19 @@ def tile_list_passage_document_coarsening_kernel(
                         start=(a == 0),
                         stop=(a == 1),
                     )
+            return banks
+
+        def evacuate_h(b, t, banks, tag):
+            ht = keep.tile([P, S], F32, name=f"h_{b}_{t}", tag=tag, align_bytes=64)
             nc.scalar.copy(ht[:, 0:BANK], banks[0][:])
             if (b, t) == (0, 0):
                 nc.vector.tensor_copy(ht[:, BANK:S], banks[1][:])
             else:
                 nc.scalar.copy(ht[:, BANK:S], banks[1][:])
             h[b, t] = ht
+
+        def make_h(b, t):
+            evacuate_h(b, t, multiply_h(b, t), f"h_{b}_{t}")
 
         first = [keep.tile([P, PACK, PAIRS], F32, name=f"first_{b}") for b in range(2)]
         second = [keep.tile([P, PACK, PAIRS], F32, name=f"second_{b}") for b in range(2)]
@@ -159,7 +168,7 @@ def tile_list_passage_document_coarsening_kernel(
             nc.vector.tensor_copy(first[b][:, t, start:stop], h[b, t][:].indirect(pos1_t[:, entries]))
             nc.vector.tensor_copy(second[b][:, t, start:stop], h[b, t][:].indirect(pos2_t[:, entries]))
 
-        z_bf16 = [keep.tile([P, PAIRS * PACK], BF16, name=f"z_bf16_{b}", align_bytes=64) for b in range(2)]
+        z_bf16 = {1: keep.tile([P, PAIRS * PACK], BF16, name="z_bf16_1", align_bytes=64)}
         z_codes = [keep.tile([P, PAIRS], U32, name=f"z_codes_{b}", align_bytes=64) for b in range(2)]
         z_planes = [keep.tile([P, PAIRS], U8, name=f"z_plane_{b}", align_bytes=64) for b in range(2)]
 
@@ -208,18 +217,25 @@ def tile_list_passage_document_coarsening_kernel(
         pick_h(0, 3)
         quantize_w1(1, 1, 0, 4)
         make_h(1, 1)
-        pair_max(0, 0, PAIRS)
+        z_rows = keep.tile([P, PACK, PAIRS], BF16, name="z_rows", tag="z_rows", align_bytes=64)
+        nc.vector.tensor_tensor(z_rows[:], first[0][:], second[0][:], ALU.max)
         pick_h(1, 0)
-        quantize_z(0, 0, PAIRS)
         make_h(1, 2)
-        make_h(1, 3)
+        last_banks = multiply_h(1, 3)
+        z_bf16[0] = keep.tile([P, PAIRS * PACK], BF16, name="z_bf16_0", tag="w1_codes_1_1", align_bytes=64)
+        nc.scalar.copy(
+            z_bf16[0][:].rearrange("p (c i t) -> p c t i", i=4, t=PACK),
+            z_rows[:].rearrange("p t (c i) -> p c t i", i=4),
+        )
+        evacuate_h(1, 3, last_banks, "z_rows")
+        pick_h(1, 1)
+        pick_h(1, 2)
+        quantize_z(0, 0, PAIRS)
         early = [psum.tile([P, EARLY], F32, name=f"y_early_{c}", tag=f"bank_{2 * c}") for c in range(N // P)]
         late = [psum.tile([P, P], F32, name=f"y_late_{c}", tag=f"bank_{2 * c + 1}") for c in range(N // P)]
         for c in range(N // P):
             multiply_z(0, c, early[c], 0, EARLY)
             multiply_z(0, c, late[c], EARLY, PAIRS)
-        pick_h(1, 1)
-        pick_h(1, 2)
         pick_h(1, 3, 0, EARLY)
         pair_max(1, 0, EARLY)
         pick_h(1, 3, EARLY, PAIRS)

@@ -35,16 +35,11 @@ def tile_list_passage_document_coarsening_kernel(
             nc.sync.dma_start(tile[:], src)
             return tile
 
-        def load_w1(b, a, parts=1):
-            tiles = []
-            width = K_PASS // parts
-            for part in range(parts):
-                tile = keep.tile([P, PACK, width], F32, name=f"w1_raw_{b}_{a}_{part}")
-                start = b * K_PASS + part * width
-                rows = w1[a * K_PASS : (a + 1) * K_PASS, start : start + width]
-                nc.sync.dma_start(tile[:], rows.rearrange("(p j) c -> p j c", j=PACK))
-                tiles.append(tile)
-            return tiles
+        def load_w1(a, start, width):
+            tile = keep.tile([P, PACK, width], F32, name=f"w1_raw_{a}_{start}", tag=f"w1_raw_{a}_{start}", align_bytes=64)
+            rows = w1[a * K_PASS : (a + 1) * K_PASS, start : start + width]
+            nc.sync.dma_start(tile[:], rows.rearrange("(p j) c -> p j c", j=PACK))
+            return tile
 
         def load_table(a):
             words = keep.tile([P, T], U32, name=f"table_{a}")
@@ -61,19 +56,21 @@ def tile_list_passage_document_coarsening_kernel(
 
         offs_t = load_list("offs_t", offs, S)
         nc.scalar.activation(warm_out[:], warm_in[:], ACT.Sigmoid)
-        raw = {}
         table = [load_table(0)]
+        near_raw = {}
+        for a in range(2):
+            near_raw[0, a] = load_w1(a, 0, P)[:]
         pos1_t = load_list("pos1_t", pos1, PAIRS)
-        pos2_t = load_list("pos2_t", pos2, PAIRS)
         for q in range(4):
             nc.sync.dma_start(
                 table_scales[32 * q : 32 * q + 8, :].bitcast(I32), tab_scales[:, 4 * q : 4 * q + 4, :].bitcast(I32)
             )
-        raw[0, 0] = load_w1(0, 0)
         table.append(load_table(1))
-        raw[0, 1] = load_w1(0, 1, parts=2)
-        raw[1, 0] = load_w1(1, 0)
-        raw[1, 1] = load_w1(1, 1)
+        pos2_t = load_list("pos2_t", pos2, PAIRS)
+        for t in range(1, PACK):
+            for a in range(2):
+                near_raw[t, a] = load_w1(a, t * P, P)[:]
+        far_raw = [load_w1(a, K_PASS, K_PASS) for a in range(2)]
         w2_codes = keep.tile([P, 2, 2 * N], U8, name="w2_codes", align_bytes=64)
         nc.sync.dma_start(w2_codes[:].bitcast(I32), w2_words.rearrange("a p c -> p a c").bitcast(I32))
         for q in range(4):
@@ -87,96 +84,125 @@ def tile_list_passage_document_coarsening_kernel(
         with nc.allow_non_contiguous_dma(reason="one value of w for each partition"):
             nc.sync.dma_start(w_col[:], w.rearrange("(c p) -> p c", p=P))
 
-        w1_codes = {}
-        w1_planes = {}
-        w1_bf16 = {}
-        for b in range(2):
-            for u in range(2):
-                w1_bf16[b, u] = keep.tile([P, 4 * K_PASS], BF16, name=f"w1_bf16_{b}_{u}", align_bytes=64)
-                w1_codes[b, u] = keep.tile(
-                    [P, 4 * P], U32, name=f"w1_codes_{b}_{u}", tag=f"w1_codes_{b}_{u}", align_bytes=64
+        near_bf16 = {}
+        near_codes = {}
+        near_planes = {}
+        far_bf16 = {}
+        far_codes = {}
+        far_planes = {}
+
+        def round_near(t):
+            near_bf16[t] = keep.tile([P, 2 * K_PASS], BF16, name=f"near_bf16_{t}", align_bytes=64)
+            for a in range(2):
+                nc.scalar.copy(
+                    near_bf16[t][:, a * K_PASS : (a + 1) * K_PASS].rearrange("p (c i j) -> p c j i", i=4, j=PACK),
+                    near_raw[t, a].rearrange("p j (c i) -> p c j i", i=4),
                 )
-                w1_planes[b, u] = keep.tile([P, 4 * P], U8, name=f"w1_plane_{b}_{u}", align_bytes=64)
 
-        def round_w1(b, a, u, last_copy=nc.scalar.copy):
-            width = P // len(raw[b, a])
-            grouped = w1_bf16[b, u][:, 2 * a * K_PASS : 2 * (a + 1) * K_PASS].rearrange("p (t m j) -> p m j t", t=2, j=PACK)
-            for part, tile in enumerate(raw[b, a]):
-                src = tile[:].rearrange("p j (m t) -> p m j t", t=PACK)[:, :, :, 2 * u : 2 * u + 2]
-                copy = last_copy if part == len(raw[b, a]) - 1 else nc.scalar.copy
-                copy(grouped[:, part * width : (part + 1) * width, :, :], src)
+        def quantize_near(t):
+            near_codes[t] = keep.tile([P, 2 * P], U32, name=f"near_codes_{t}", align_bytes=64)
+            near_planes[t] = keep.tile([P, 2 * P], U8, name=f"near_plane_{t}", align_bytes=64)
+            nc.vector.quantize_mx(out=near_codes[t][:].bitcast(FP8X4), scales=near_planes[t][:], in_=near_bf16[t][:])
 
-        def quantize_w1(b, u, start, stop):
-            nc.vector.quantize_mx(
-                out=w1_codes[b, u][:, start * P : stop * P].bitcast(FP8X4),
-                scales=w1_planes[b, u][:, start * P : stop * P],
-                in_=w1_bf16[b, u][:, start * K_PASS : stop * K_PASS],
-            )
+        def round_far(u):
+            far_bf16[u] = keep.tile([P, 4 * K_PASS], BF16, name=f"far_bf16_{u}", tag=f"far_bf16_{u}", align_bytes=64)
+            for a in range(2):
+                nc.scalar.copy(
+                    far_bf16[u][:, 2 * a * K_PASS : 2 * (a + 1) * K_PASS].rearrange("p (t m j) -> p m j t", t=2, j=PACK),
+                    far_raw[a][:].rearrange("p j (m t) -> p m j t", t=PACK)[:, :, :, 2 * u : 2 * u + 2],
+                )
+
+        def quantize_far(u):
+            far_codes[u] = keep.tile([P, 4 * P], U32, name=f"far_codes_{u}", tag=f"far_codes_{u}", align_bytes=64)
+            far_planes[u] = keep.tile([P, 4 * P], U8, name=f"far_plane_{u}", align_bytes=64)
+            nc.vector.quantize_mx(out=far_codes[u][:].bitcast(FP8X4), scales=far_planes[u][:], in_=far_bf16[u][:])
 
         v_scales = keep.tile([P, S], U8, name="v_scales", align_bytes=64)
         v_codes = [keep.tile([P, S], U32, name=f"v_codes_{a}", align_bytes=64) for a in range(2)]
+        HALVES = [(0, BANK), (BANK, S)]
+        FIRST_RANGES = [(0, BANK), (BANK, BANK + 2 * P), (BANK + 2 * P, S)]
 
         nc.vector.tensor_copy(v_codes[0][:], table[0][:].indirect(offs_t[:]))
+        round_near(0)
+        quantize_near(0)
         nc.vector.tensor_copy(v_scales[:], table_scales[:].indirect(offs_t[:]))
-        round_w1(0, 0, 0)
-        round_w1(0, 0, 1)
-        quantize_w1(0, 0, 0, 2)
-        nc.vector.tensor_copy(v_codes[1][:], table[1][:].indirect(offs_t[:]))
-        round_w1(0, 1, 0, nc.vector.tensor_copy)
-        quantize_w1(0, 0, 2, 3)
-        quantize_w1(0, 0, 3, 4)
-        round_w1(0, 1, 1)
-        quantize_w1(0, 1, 0, 4)
+        for start, stop in FIRST_RANGES:
+            nc.vector.tensor_copy(v_codes[1][:, start:stop], table[1][:].indirect(offs_t[:, start // 16 : stop // 16]))
 
         h = {}
 
         def multiply_h(b, t):
-            u, e = divmod(t, 2)
-            banks = [psum.tile([P, BANK], F32, name=f"h_bank_{b}_{t}_{half}", tag=f"bank_{2 * t + half}") for half in range(2)]
-            for a in range(2):
-                rows = slice((2 * a + e) * P, (2 * a + e + 1) * P)
-                for half in range(2):
-                    cols = slice(half * BANK, (half + 1) * BANK)
+            if b == 0:
+                codes, planes = near_codes[t], near_planes[t]
+                first_col = [a * P for a in range(2)]
+            else:
+                u, e = divmod(t, 2)
+                codes, planes = far_codes[u], far_planes[u]
+                first_col = [(2 * a + e) * P for a in range(2)]
+            ranges = FIRST_RANGES if (b, t) == (0, 0) else HALVES
+            tags = [2 * t, 2 * t + 1, 7]
+            banks = [
+                psum.tile([P, stop - start], F32, name=f"h_bank_{b}_{t}_{n}", tag=f"bank_{tags[n]}")
+                for n, (start, stop) in enumerate(ranges)
+            ]
+            order = [(a, n) for n in range(len(ranges)) for a in range(2)]
+            if (b, t) == (0, 0):
+                order = sorted(order)
+            for a, n in order:
+                rows = slice(first_col[a], first_col[a] + P)
+                for bank, (start, stop) in [(banks[n], ranges[n])]:
                     nc.tensor.matmul_mx(
-                        out=banks[half][:],
-                        lhsT=w1_codes[b, u][:, rows].bitcast(FP8X4),
-                        lhsT_scale=w1_planes[b, u][:, rows],
-                        rhs=v_codes[a][:, cols].bitcast(FP8X4),
-                        rhs_scale=v_scales[4 * a : P, cols],
+                        out=bank[:],
+                        lhsT=codes[:, rows].bitcast(FP8X4),
+                        lhsT_scale=planes[:, rows],
+                        rhs=v_codes[a][:, start:stop].bitcast(FP8X4),
+                        rhs_scale=v_scales[4 * a : P, start:stop],
                         start=(a == 0),
                         stop=(a == 1),
                     )
-            return banks
+            return list(zip(banks, ranges))
 
         def evacuate_h(b, t, banks, tag):
             ht = keep.tile([P, S], F32, name=f"h_{b}_{t}", tag=tag, align_bytes=64)
-            nc.scalar.copy(ht[:, 0:BANK], banks[0][:])
-            if (b, t) == (0, 0):
-                nc.vector.tensor_copy(ht[:, BANK:S], banks[1][:])
-            else:
-                nc.scalar.copy(ht[:, BANK:S], banks[1][:])
+            for bank, (start, stop) in banks:
+                nc.scalar.copy(ht[:, start:stop], bank[:])
             h[b, t] = ht
 
-        def make_h(b, t):
-            evacuate_h(b, t, multiply_h(b, t), f"h_{b}_{t}")
+        def make_h(b, t, tag=None):
+            evacuate_h(b, t, multiply_h(b, t), tag or f"h_{b}_{t}")
 
-        first = [keep.tile([P, PACK, PAIRS], F32, name=f"first_{b}") for b in range(2)]
-        second = [keep.tile([P, PACK, PAIRS], F32, name=f"second_{b}") for b in range(2)]
+        z_slots = keep.tile([P, PACK * PAIRS], BF16, name="z_slots", tag="z_slots", align_bytes=64)
+        near_first = {}
+        near_second = {}
 
-        def pick_h(b, t, start=0, stop=PAIRS):
+        def pick_near(t, tag=None):
+            both = keep.tile([P, 2, PAIRS], F32, name=f"near_picks_{t}", tag=tag or f"near_picks_{t}", align_bytes=64)
+            near_first[t] = both[:, 0, :]
+            near_second[t] = both[:, 1, :]
+            nc.vector.tensor_copy(near_first[t], h[0, t][:].indirect(pos1_t[:]))
+            nc.vector.tensor_copy(near_second[t], h[0, t][:].indirect(pos2_t[:]))
+
+        def max_near(t):
+            z_rows = keep.tile([P, PAIRS], BF16, name=f"z_rows_{t}")
+            nc.vector.tensor_tensor(z_rows[:], near_first[t], near_second[t], ALU.max)
+            nc.sync.dma_start(z_slots[32 * t : 32 * (t + 1), :], z_rows[:])
+
+        second = keep.tile([P, PACK, PAIRS], F32, name="second")
+
+        def pick_far(t, start=0, stop=PAIRS):
             entries = slice(start // 16, stop // 16)
-            nc.vector.tensor_copy(first[b][:, t, start:stop], h[b, t][:].indirect(pos1_t[:, entries]))
-            nc.vector.tensor_copy(second[b][:, t, start:stop], h[b, t][:].indirect(pos2_t[:, entries]))
+            nc.vector.tensor_copy(first[:, t, start:stop], h[1, t][:].indirect(pos1_t[:, entries]))
+            nc.vector.tensor_copy(second[:, t, start:stop], h[1, t][:].indirect(pos2_t[:, entries]))
 
         z_bf16 = {1: keep.tile([P, PAIRS * PACK], BF16, name="z_bf16_1", align_bytes=64)}
         z_codes = [keep.tile([P, PAIRS], U32, name=f"z_codes_{b}", align_bytes=64) for b in range(2)]
         z_planes = [keep.tile([P, PAIRS], U8, name=f"z_plane_{b}", align_bytes=64) for b in range(2)]
 
-        def pair_max(b, start, stop):
+        def max_far(start, stop):
             nc.vector.tensor_tensor(
-                z_bf16[b][:, start * PACK : stop * PACK].rearrange("p (c i t) -> p c t i", i=2, t=PACK),
-                first[b][:, :, start:stop].rearrange("p t (c i) -> p c t i", i=2),
-                second[b][:, :, start:stop].rearrange("p t (c i) -> p c t i", i=2),
+                z_bf16[1][:, start * PACK : stop * PACK].rearrange("p (c i t) -> p c t i", i=2, t=PACK),
+                first[:, :, start:stop].rearrange("p t (c i) -> p c t i", i=2),
+                second[:, :, start:stop].rearrange("p t (c i) -> p c t i", i=2),
                 ALU.max,
             )
 
@@ -201,47 +227,54 @@ def tile_list_passage_document_coarsening_kernel(
                     stop=(b == 1 and m == stop - P),
                 )
 
-        make_h(0, 0)
-        make_h(0, 1)
-        pick_h(0, 0)
-        round_w1(1, 0, 0)
+        round_near(1)
+        quantize_near(1)
+        round_near(2)
+        quantize_near(2)
+        make_h(0, 0, f"w1_raw_1_{2 * P}")
+        pick_near(0)
+        max_near(0)
+        round_near(3)
+        quantize_near(3)
+        make_h(0, 1, f"w1_raw_1_{3 * P}")
+        pick_near(1)
+        max_near(1)
         make_h(0, 2)
-        pick_h(0, 1)
-        round_w1(1, 1, 0)
+        pick_near(2)
+        max_near(2)
         make_h(0, 3)
-        pick_h(0, 2)
-        round_w1(1, 0, 1)
-        round_w1(1, 1, 1)
-        quantize_w1(1, 0, 0, 4)
+        round_far(0)
+        quantize_far(0)
+        pick_near(3, "far_bf16_0")
+        max_near(3)
+        round_far(1)
+        quantize_far(1)
         make_h(1, 0)
-        pick_h(0, 3)
-        quantize_w1(1, 1, 0, 4)
         make_h(1, 1)
-        z_rows = keep.tile([P, PACK, PAIRS], BF16, name="z_rows", tag="z_rows", align_bytes=64)
-        nc.vector.tensor_tensor(z_rows[:], first[0][:], second[0][:], ALU.max)
-        pick_h(1, 0)
+        first = keep.tile([P, PACK, PAIRS], F32, name="first")
+        pick_far(0)
         make_h(1, 2)
         last_banks = multiply_h(1, 3)
-        z_bf16[0] = keep.tile([P, PAIRS * PACK], BF16, name="z_bf16_0", tag="w1_codes_1_1", align_bytes=64)
+        z_bf16[0] = keep.tile([P, PAIRS * PACK], BF16, name="z_bf16_0", tag="far_codes_1", align_bytes=64)
         nc.scalar.copy(
             z_bf16[0][:].rearrange("p (c i t) -> p c t i", i=4, t=PACK),
-            z_rows[:].rearrange("p t (c i) -> p c t i", i=4),
+            z_slots[:].rearrange("p (t c i) -> p c t i", i=4, t=PACK),
         )
-        evacuate_h(1, 3, last_banks, "z_rows")
-        pick_h(1, 1)
-        pick_h(1, 2)
+        evacuate_h(1, 3, last_banks, "z_slots")
+        pick_far(1)
+        pick_far(2)
         quantize_z(0, 0, PAIRS)
         early = [psum.tile([P, EARLY], F32, name=f"y_early_{c}", tag=f"bank_{2 * c}") for c in range(N // P)]
         late = [psum.tile([P, P], F32, name=f"y_late_{c}", tag=f"bank_{2 * c + 1}") for c in range(N // P)]
         for c in range(N // P):
             multiply_z(0, c, early[c], 0, EARLY)
             multiply_z(0, c, late[c], EARLY, PAIRS)
-        pick_h(1, 3, 0, EARLY)
-        pair_max(1, 0, EARLY)
-        pick_h(1, 3, EARLY, PAIRS)
+        pick_far(3, 0, EARLY)
+        max_far(0, EARLY)
+        pick_far(3, EARLY, PAIRS)
         quantize_z(1, 0, 2 * P)
         quantize_z(1, 2 * P, EARLY)
-        pair_max(1, EARLY, PAIRS)
+        max_far(EARLY, PAIRS)
         quantize_z(1, EARLY, PAIRS)
         y = [keep.tile([P, PAIRS], F32, name=f"y_{c}") for c in range(N // P)]
         for c in range(N // P):
@@ -253,15 +286,26 @@ def tile_list_passage_document_coarsening_kernel(
             else:
                 nc.scalar.copy(y[c][:, EARLY:PAIRS], late[c][:])
 
-        for c in range(N // P):
-            right = keep.tile([P, DOCS], F32, name=f"right_{c}")
-            left = keep.tile([P, DOCS], F32, name=f"left_{c}")
+        gate = {}
+        kept = {}
+
+        def pick_y(c):
+            right = keep.tile([P, DOCS], F32, name=f"right_{c}", tag=f"right_{c}")
             nc.vector.tensor_copy(right[:], y[c][:].indirect(pos4_t[:]))
-            nc.vector.tensor_copy(left[:], y[c][:].indirect(pos3_t[:]))
             stay = keep.tile([P, DOCS], F32, name=f"stay_{c}")
+            gate[c] = keep.tile([P, DOCS], F32, name=f"gate_{c}")
             nc.scalar.activation(stay[:], right[:], ACT.Sigmoid, scale=-1.0)
-            rest = keep.tile([P, DOCS], F32, name=f"rest_{c}")
-            nc.vector.scalar_tensor_tensor(rest[:], left[:], w_col[:, c : c + 1], stay[:], ALU.subtract, ALU.mult)
-            doc = keep.tile([P, DOCS], F32, name=f"doc_{c}")
-            nc.scalar.activation(doc[:], rest[:], ACT.Identity, bias=w_col[:, c : c + 1])
+            nc.scalar.activation(gate[c][:], right[:], ACT.Sigmoid)
+            kept[c] = keep.tile([P, DOCS], F32, name=f"kept_{c}")
+            nc.vector.tensor_tensor(kept[c][:], y[c][:].indirect(pos3_t[:]), stay[:], ALU.mult)
+
+        def store_doc(c):
+            doc = keep.tile([P, DOCS], F32, name=f"doc_{c}", tag=f"right_{c + 1}")
+            nc.vector.scalar_tensor_tensor(doc[:], gate[c][:], w_col[:, c : c + 1], kept[c][:], ALU.mult, ALU.add)
             nc.sync.dma_start(out[c * P : (c + 1) * P, :], doc[:])
+
+        pick_y(0)
+        for c in range(1, N // P):
+            pick_y(c)
+            store_doc(c - 1)
+        store_doc(N // P - 1)

@@ -58,18 +58,23 @@ def tile_list_passage_document_coarsening_kernel(
         nc.scalar.activation(warm_out[:], warm_in[:], ACT.Sigmoid)
         table = [load_table(0)]
         near_raw = {}
-        for a in range(2):
-            near_raw[0, a] = load_w1(a, 0, P)[:]
+
+        def load_near(a, t):
+            both = load_w1(a, t * P, 2 * P)
+            near_raw[t, a] = both[:, :, 0:P]
+            near_raw[t + 1, a] = both[:, :, P : 2 * P]
+
+        load_near(0, 0)
         pos1_t = load_list("pos1_t", pos1, PAIRS)
+        pos2_t = load_list("pos2_t", pos2, PAIRS)
         for q in range(4):
             nc.sync.dma_start(
                 table_scales[32 * q : 32 * q + 8, :].bitcast(I32), tab_scales[:, 4 * q : 4 * q + 4, :].bitcast(I32)
             )
         table.append(load_table(1))
-        pos2_t = load_list("pos2_t", pos2, PAIRS)
-        for t in range(1, PACK):
-            for a in range(2):
-                near_raw[t, a] = load_w1(a, t * P, P)[:]
+        load_near(1, 0)
+        load_near(0, 2)
+        load_near(1, 2)
         far_raw = [load_w1(a, K_PASS, K_PASS) for a in range(2)]
         w2_codes = keep.tile([P, 2, 2 * N], U8, name="w2_codes", align_bytes=64)
         nc.sync.dma_start(w2_codes[:].bitcast(I32), w2_words.rearrange("a p c -> p a c").bitcast(I32))
@@ -91,13 +96,16 @@ def tile_list_passage_document_coarsening_kernel(
         far_codes = {}
         far_planes = {}
 
+        def round_pass(dst, t, a):
+            nc.scalar.copy(
+                dst.rearrange("p (c i j) -> p c j i", i=4, j=PACK),
+                near_raw[t, a].rearrange("p j (c i) -> p c j i", i=4),
+            )
+
         def round_near(t):
-            near_bf16[t] = keep.tile([P, 2 * K_PASS], BF16, name=f"near_bf16_{t}", align_bytes=64)
+            near_bf16[t] = keep.tile([P, 2 * K_PASS], BF16, name=f"near_bf16_{t}", tag=f"near_bf16_{t}", align_bytes=64)
             for a in range(2):
-                nc.scalar.copy(
-                    near_bf16[t][:, a * K_PASS : (a + 1) * K_PASS].rearrange("p (c i j) -> p c j i", i=4, j=PACK),
-                    near_raw[t, a].rearrange("p j (c i) -> p c j i", i=4),
-                )
+                round_pass(near_bf16[t][:, a * K_PASS : (a + 1) * K_PASS], t, a)
 
         def quantize_near(t):
             near_codes[t] = keep.tile([P, 2 * P], U32, name=f"near_codes_{t}", align_bytes=64)
@@ -118,16 +126,37 @@ def tile_list_passage_document_coarsening_kernel(
             nc.vector.quantize_mx(out=far_codes[u][:].bitcast(FP8X4), scales=far_planes[u][:], in_=far_bf16[u][:])
 
         v_scales = keep.tile([P, S], U8, name="v_scales", align_bytes=64)
-        v_codes = [keep.tile([P, S], U32, name=f"v_codes_{a}", align_bytes=64) for a in range(2)]
         HALVES = [(0, BANK), (BANK, S)]
         FIRST_RANGES = [(0, BANK), (BANK, BANK + 2 * P), (BANK + 2 * P, S)]
+        v_first = keep.tile([P, S], U32, name="v_first", align_bytes=64)
+        v_low = keep.tile([P, BANK], U32, name="v_low", align_bytes=64)
 
-        nc.vector.tensor_copy(v_codes[0][:], table[0][:].indirect(offs_t[:]))
-        round_near(0)
-        quantize_near(0)
+        near_codes[0] = keep.tile([P, 2 * P], U32, name="near_codes_0", align_bytes=64)
+        near_planes[0] = keep.tile([P, 2 * P], U8, name="near_plane_0", align_bytes=64)
+
+        def quantize_first(a):
+            stage = keep.tile([P, K_PASS], BF16, name=f"first_bf16_{a}", tag=f"first_bf16_{a}", align_bytes=64)
+            round_pass(stage[:], 0, a)
+            cols = slice(a * P, (a + 1) * P)
+            nc.vector.quantize_mx(out=near_codes[0][:, cols].bitcast(FP8X4), scales=near_planes[0][:, cols], in_=stage[:])
+
+        nc.vector.tensor_copy(v_first[:], table[0][:].indirect(offs_t[:]))
+        quantize_first(0)
         nc.vector.tensor_copy(v_scales[:], table_scales[:].indirect(offs_t[:]))
-        for start, stop in FIRST_RANGES:
-            nc.vector.tensor_copy(v_codes[1][:, start:stop], table[1][:].indirect(offs_t[:, start // 16 : stop // 16]))
+        nc.vector.tensor_copy(v_low[:], table[1][:].indirect(offs_t[:, 0 : BANK // 16]))
+        quantize_first(1)
+        v_high = keep.tile([P, BANK], U32, name="v_high", tag="first_bf16_1", align_bytes=64)
+        for start, stop in FIRST_RANGES[1:]:
+            nc.vector.tensor_copy(
+                v_high[:, start - BANK : stop - BANK], table[1][:].indirect(offs_t[:, start // 16 : stop // 16])
+            )
+
+        def v_codes(a, start, stop):
+            if a == 0:
+                return v_first[:, start:stop]
+            if start < BANK:
+                return v_low[:, start:stop]
+            return v_high[:, start - BANK : stop - BANK]
 
         h = {}
 
@@ -155,7 +184,7 @@ def tile_list_passage_document_coarsening_kernel(
                         out=bank[:],
                         lhsT=codes[:, rows].bitcast(FP8X4),
                         lhsT_scale=planes[:, rows],
-                        rhs=v_codes[a][:, start:stop].bitcast(FP8X4),
+                        rhs=v_codes(a, start, stop).bitcast(FP8X4),
                         rhs_scale=v_scales[4 * a : P, start:stop],
                         start=(a == 0),
                         stop=(a == 1),
@@ -172,20 +201,16 @@ def tile_list_passage_document_coarsening_kernel(
             evacuate_h(b, t, multiply_h(b, t), tag or f"h_{b}_{t}")
 
         z_slots = keep.tile([P, PACK * PAIRS], BF16, name="z_slots", tag="z_slots", align_bytes=64)
-        near_first = {}
-        near_second = {}
 
-        def pick_near(t, tag=None):
-            both = keep.tile([P, 2, PAIRS], F32, name=f"near_picks_{t}", tag=tag or f"near_picks_{t}", align_bytes=64)
-            near_first[t] = both[:, 0, :]
-            near_second[t] = both[:, 1, :]
-            nc.vector.tensor_copy(near_first[t], h[0, t][:].indirect(pos1_t[:]))
-            nc.vector.tensor_copy(near_second[t], h[0, t][:].indirect(pos2_t[:]))
+        def pick_near(t, picks, slot):
+            nc.vector.tensor_copy(picks[0][:, slot, :], h[0, t][:].indirect(pos1_t[:]))
+            nc.vector.tensor_copy(picks[1][:, slot, :], h[0, t][:].indirect(pos2_t[:]))
 
-        def max_near(t):
-            z_rows = keep.tile([P, PAIRS], BF16, name=f"z_rows_{t}")
-            nc.vector.tensor_tensor(z_rows[:], near_first[t], near_second[t], ALU.max)
-            nc.sync.dma_start(z_slots[32 * t : 32 * (t + 1), :], z_rows[:])
+        def max_near(tiles, picks, tag):
+            z_rows = keep.tile([P, len(tiles), PAIRS], BF16, name=f"z_rows_{tiles[0]}", tag=tag, align_bytes=64)
+            nc.vector.tensor_tensor(z_rows[:], picks[0][:], picks[1][:], ALU.max)
+            for slot, t in enumerate(tiles):
+                nc.sync.dma_start(z_slots[32 * t : 32 * (t + 1), :], z_rows[:, slot, :])
 
         second = keep.tile([P, PACK, PAIRS], F32, name="second")
 
@@ -229,26 +254,32 @@ def tile_list_passage_document_coarsening_kernel(
 
         round_near(1)
         quantize_near(1)
+        make_h(0, 0, "w1_raw_1_0")
         round_near(2)
         quantize_near(2)
-        make_h(0, 0, f"w1_raw_1_{2 * P}")
-        pick_near(0)
-        max_near(0)
+        picks_a = [
+            keep.tile([P, 1, PAIRS], F32, name="first_a"),
+            keep.tile([P, 1, PAIRS], F32, name="second_a", tag="near_bf16_2", align_bytes=64),
+        ]
+        pick_near(0, picks_a, 0)
+        make_h(0, 1)
         round_near(3)
         quantize_near(3)
-        make_h(0, 1, f"w1_raw_1_{3 * P}")
-        pick_near(1)
-        max_near(1)
+        picks_b = [
+            keep.tile([P, 3, PAIRS], F32, name="first_b"),
+            keep.tile([P, 3, PAIRS], F32, name="second_b", tag="near_bf16_3", align_bytes=64),
+        ]
+        pick_near(1, picks_b, 0)
         make_h(0, 2)
-        pick_near(2)
-        max_near(2)
-        make_h(0, 3)
+        pick_near(2, picks_b, 1)
         round_far(0)
         quantize_far(0)
-        pick_near(3, "far_bf16_0")
-        max_near(3)
+        make_h(0, 3)
+        max_near([0], picks_a, "far_bf16_0")
+        pick_near(3, picks_b, 2)
         round_far(1)
         quantize_far(1)
+        max_near([1, 2, 3], picks_b, "far_bf16_1")
         make_h(1, 0)
         make_h(1, 1)
         first = keep.tile([P, PACK, PAIRS], F32, name="first")

@@ -1,6 +1,7 @@
 from contextlib import ExitStack
 
 import concourse.mybir as mybir
+from concourse.masks import make_identity
 
 K, T, S, PAIRS, DOCS, H, N = 1024, 2048, 1024, 512, 256, 1024, 512
 FLOPS = 2 * K * H * S + 2 * H * N * PAIRS
@@ -200,17 +201,13 @@ def tile_list_passage_document_coarsening_kernel(
         def make_h(b, t, tag=None):
             evacuate_h(b, t, multiply_h(b, t), tag or f"h_{b}_{t}")
 
-        z_slots = keep.tile([P, PACK * PAIRS], BF16, name="z_slots", tag="z_slots", align_bytes=64)
+        identity = keep.tile([P, P], F32, name="identity")
+        make_identity(nc, identity[:])
+        near_first = keep.tile([P, PACK, PAIRS], F32, name="near_first")
 
-        def pick_near(t, picks, slot):
-            nc.vector.tensor_copy(picks[0][:, slot, :], h[0, t][:].indirect(pos1_t[:]))
-            nc.vector.tensor_copy(picks[1][:, slot, :], h[0, t][:].indirect(pos2_t[:]))
-
-        def max_near(tiles, picks, tag):
-            z_rows = keep.tile([P, len(tiles), PAIRS], BF16, name=f"z_rows_{tiles[0]}", tag=tag, align_bytes=64)
-            nc.vector.tensor_tensor(z_rows[:], picks[0][:], picks[1][:], ALU.max)
-            for slot, t in enumerate(tiles):
-                nc.sync.dma_start(z_slots[32 * t : 32 * (t + 1), :], z_rows[:, slot, :])
+        def pick_near(t, excess):
+            nc.vector.tensor_copy(near_first[:, t, :], h[0, t][:].indirect(pos1_t[:]))
+            nc.vector.tensor_tensor(excess, h[0, t][:].indirect(pos2_t[:]), near_first[:, t, :], ALU.subtract)
 
         second = keep.tile([P, PACK, PAIRS], F32, name="second")
 
@@ -219,7 +216,7 @@ def tile_list_passage_document_coarsening_kernel(
             nc.vector.tensor_copy(first[:, t, start:stop], h[1, t][:].indirect(pos1_t[:, entries]))
             nc.vector.tensor_copy(second[:, t, start:stop], h[1, t][:].indirect(pos2_t[:, entries]))
 
-        z_bf16 = {1: keep.tile([P, PAIRS * PACK], BF16, name="z_bf16_1", align_bytes=64)}
+        z_bf16 = {}
         z_codes = [keep.tile([P, PAIRS], U32, name=f"z_codes_{b}", align_bytes=64) for b in range(2)]
         z_planes = [keep.tile([P, PAIRS], U8, name=f"z_plane_{b}", align_bytes=64) for b in range(2)]
 
@@ -257,50 +254,73 @@ def tile_list_passage_document_coarsening_kernel(
         make_h(0, 0, "w1_raw_1_0")
         round_near(2)
         quantize_near(2)
-        picks_a = [
-            keep.tile([P, 1, PAIRS], F32, name="first_a"),
-            keep.tile([P, 1, PAIRS], F32, name="second_a", tag="near_bf16_2", align_bytes=64),
-        ]
-        pick_near(0, picks_a, 0)
+        excess_a = keep.tile([P, 1, PAIRS], F32, name="excess_a", tag="near_bf16_2", align_bytes=64)
+        pick_near(0, excess_a[:, 0, :])
         make_h(0, 1)
         round_near(3)
         quantize_near(3)
-        picks_b = [
-            keep.tile([P, 3, PAIRS], F32, name="first_b"),
-            keep.tile([P, 3, PAIRS], F32, name="second_b", tag="near_bf16_3", align_bytes=64),
-        ]
-        pick_near(1, picks_b, 0)
+        excess_b = keep.tile([P, 3, PAIRS], F32, name="excess_b", tag="near_bf16_3", align_bytes=64)
+        pick_near(1, excess_b[:, 0, :])
         make_h(0, 2)
-        pick_near(2, picks_b, 1)
+        pick_near(2, excess_b[:, 1, :])
         round_far(0)
         quantize_far(0)
         make_h(0, 3)
-        max_near([0], picks_a, "far_bf16_0")
-        pick_near(3, picks_b, 2)
+        pick_near(3, excess_b[:, 2, :])
         round_far(1)
         quantize_far(1)
-        max_near([1, 2, 3], picks_b, "far_bf16_1")
         make_h(1, 0)
         make_h(1, 1)
         first = keep.tile([P, PACK, PAIRS], F32, name="first")
         pick_far(0)
         make_h(1, 2)
-        last_banks = multiply_h(1, 3)
-        z_bf16[0] = keep.tile([P, PAIRS * PACK], BF16, name="z_bf16_0", tag="far_codes_1", align_bytes=64)
-        nc.scalar.copy(
-            z_bf16[0][:].rearrange("p (c i t) -> p c t i", i=4, t=PACK),
-            z_slots[:].rearrange("p (t c i) -> p c t i", i=4, t=PACK),
-        )
-        evacuate_h(1, 3, last_banks, "z_slots")
+        make_h(1, 3)
+        turned = []
+        rise = keep.tile([P, PACK, PAIRS], F32, name="rise", tag="far_codes_1", align_bytes=64)
+        for j in range(PAIRS // P):
+            cols = slice(j * P, (j + 1) * P)
+            if j % 2 == 0:
+                two = slice(j * P, (j + 2) * P)
+                nc.scalar.activation(rise[:, 0:1, two], excess_a[:, :, two], ACT.Relu)
+                nc.scalar.activation(rise[:, 1:PACK, two], excess_b[:, :, two], ACT.Relu)
+            bank = psum.tile([P, K_PASS], F32, name=f"z_turned_bank_{j}", tag=f"bank_{j}")
+            for t in range(PACK):
+                for part, src in enumerate([near_first, rise]):
+                    nc.tensor.matmul(
+                        bank[:, t * P : (t + 1) * P],
+                        lhsT=src[:, t, cols],
+                        rhs=identity[:],
+                        is_transpose=True,
+                        start=(part == 0),
+                        stop=(part == 1),
+                    )
+            tile = keep.tile([P, K_PASS], BF16, name=f"z_turned_{j}", align_bytes=64)
+            nc.scalar.copy(
+                tile[:].rearrange("m (u p e) -> m u p e", u=2, e=2),
+                bank[:].rearrange("m (p u e) -> m u p e", u=2, e=2),
+            )
+            turned.append(tile)
+        z_bf16[0] = keep.tile([P, PAIRS * PACK], BF16, name="z_bf16_0", tag="z_bf16", align_bytes=64)
+        for half in range(2):
+            bank = psum.tile([P, 2, 2, P], F32, name=f"z_back_bank_{half}", tag=f"bank_{4 + half}")
+            for jj in range(2):
+                words = turned[2 * half + jj][:].bitcast(F32)
+                for u in range(2):
+                    nc.tensor.transpose(bank[:, jj, u, :], words[:, u * P : (u + 1) * P], identity[:])
+            nc.scalar.copy(
+                z_bf16[0][:, half * 2 * K_PASS : (half + 1) * 2 * K_PASS].bitcast(F32).rearrange("p (j m u) -> p j m u", j=2, u=2),
+                bank[:].rearrange("p j u m -> p j m u"),
+            )
         pick_far(1)
         pick_far(2)
+        pick_far(3, 0, EARLY)
         quantize_z(0, 0, PAIRS)
+        z_bf16[1] = keep.tile([P, PAIRS * PACK], BF16, name="z_bf16_1", tag="z_bf16", align_bytes=64)
         early = [psum.tile([P, EARLY], F32, name=f"y_early_{c}", tag=f"bank_{2 * c}") for c in range(N // P)]
         late = [psum.tile([P, P], F32, name=f"y_late_{c}", tag=f"bank_{2 * c + 1}") for c in range(N // P)]
         for c in range(N // P):
             multiply_z(0, c, early[c], 0, EARLY)
             multiply_z(0, c, late[c], EARLY, PAIRS)
-        pick_far(3, 0, EARLY)
         max_far(0, EARLY)
         pick_far(3, EARLY, PAIRS)
         quantize_z(1, 0, 2 * P)

@@ -57,25 +57,28 @@ def tile_list_passage_document_coarsening_kernel(
 
         offs_t = load_list("offs_t", offs, S)
         nc.scalar.activation(warm_out[:], warm_in[:], ACT.Sigmoid)
-        table = [load_table(0)]
         near_raw = {}
 
-        def load_near(a, t):
-            both = load_w1(a, t * P, 2 * P)
-            near_raw[t, a] = both[:, :, 0:P]
-            near_raw[t + 1, a] = both[:, :, P : 2 * P]
+        def load_near(a, tiles):
+            chunk = load_w1(a, tiles[0] * P, len(tiles) * P)
+            for slot, t in enumerate(tiles):
+                near_raw[t, a] = chunk[:, :, slot * P : (slot + 1) * P]
 
-        load_near(0, 0)
         pos1_t = load_list("pos1_t", pos1, PAIRS)
         pos2_t = load_list("pos2_t", pos2, PAIRS)
         for q in range(4):
             nc.sync.dma_start(
                 table_scales[32 * q : 32 * q + 8, :].bitcast(I32), tab_scales[:, 4 * q : 4 * q + 4, :].bitcast(I32)
             )
+        table = [load_table(0)]
+        load_near(0, [0])
         table.append(load_table(1))
-        load_near(1, 0)
-        load_near(0, 2)
-        load_near(1, 2)
+        load_near(1, [0])
+        load_near(0, [1])
+        load_near(1, [1])
+        load_near(0, [2, 3])
+        load_near(1, [2])
+        load_near(1, [3])
         far_raw = [load_w1(a, K_PASS, K_PASS) for a in range(2)]
         w2_codes = keep.tile([P, 2, 2 * N], U8, name="w2_codes", align_bytes=64)
         nc.sync.dma_start(w2_codes[:].bitcast(I32), w2_words.rearrange("a p c -> p a c").bitcast(I32))
@@ -141,9 +144,9 @@ def tile_list_passage_document_coarsening_kernel(
             cols = slice(a * P, (a + 1) * P)
             nc.vector.quantize_mx(out=near_codes[0][:, cols].bitcast(FP8X4), scales=near_planes[0][:, cols], in_=stage[:])
 
+        nc.vector.tensor_copy(v_scales[:], table_scales[:].indirect(offs_t[:]))
         nc.vector.tensor_copy(v_first[:], table[0][:].indirect(offs_t[:]))
         quantize_first(0)
-        nc.vector.tensor_copy(v_scales[:], table_scales[:].indirect(offs_t[:]))
         nc.vector.tensor_copy(v_low[:], table[1][:].indirect(offs_t[:, 0 : BANK // 16]))
         quantize_first(1)
         v_high = keep.tile([P, BANK], U32, name="v_high", tag="first_bf16_1", align_bytes=64)
@@ -251,17 +254,17 @@ def tile_list_passage_document_coarsening_kernel(
 
         round_near(1)
         quantize_near(1)
-        make_h(0, 0, "w1_raw_1_0")
+        make_h(0, 0, f"w1_raw_1_{P}")
         round_near(2)
         quantize_near(2)
         excess_a = keep.tile([P, 1, PAIRS], F32, name="excess_a", tag="near_bf16_2", align_bytes=64)
         pick_near(0, excess_a[:, 0, :])
-        make_h(0, 1)
+        make_h(0, 1, f"w1_raw_1_{2 * P}")
         round_near(3)
         quantize_near(3)
         excess_b = keep.tile([P, 3, PAIRS], F32, name="excess_b", tag="near_bf16_3", align_bytes=64)
         pick_near(1, excess_b[:, 0, :])
-        make_h(0, 2)
+        make_h(0, 2, f"w1_raw_1_{3 * P}")
         pick_near(2, excess_b[:, 1, :])
         round_far(0)
         quantize_far(0)
@@ -275,25 +278,28 @@ def tile_list_passage_document_coarsening_kernel(
         pick_far(0)
         make_h(1, 2)
         make_h(1, 3)
+        def turn(src, j, bank, opens):
+            for t in range(PACK):
+                nc.tensor.matmul(
+                    bank[:, t * P : (t + 1) * P],
+                    lhsT=src[:, t, j * P : (j + 1) * P],
+                    rhs=identity[:],
+                    is_transpose=True,
+                    start=(opens and t == 0),
+                    stop=(not opens and t == PACK - 1),
+                )
+
+        turn_banks = [psum.tile([P, K_PASS], F32, name=f"z_turned_bank_{j}", tag=f"bank_{j}") for j in range(PAIRS // P)]
+        for j, bank in enumerate(turn_banks):
+            turn(near_first, j, bank, True)
         turned = []
         rise = keep.tile([P, PACK, PAIRS], F32, name="rise", tag="far_codes_1", align_bytes=64)
-        for j in range(PAIRS // P):
-            cols = slice(j * P, (j + 1) * P)
+        for j, bank in enumerate(turn_banks):
             if j % 2 == 0:
                 two = slice(j * P, (j + 2) * P)
                 nc.scalar.activation(rise[:, 0:1, two], excess_a[:, :, two], ACT.Relu)
                 nc.scalar.activation(rise[:, 1:PACK, two], excess_b[:, :, two], ACT.Relu)
-            bank = psum.tile([P, K_PASS], F32, name=f"z_turned_bank_{j}", tag=f"bank_{j}")
-            for t in range(PACK):
-                for part, src in enumerate([near_first, rise]):
-                    nc.tensor.matmul(
-                        bank[:, t * P : (t + 1) * P],
-                        lhsT=src[:, t, cols],
-                        rhs=identity[:],
-                        is_transpose=True,
-                        start=(part == 0),
-                        stop=(part == 1),
-                    )
+            turn(rise, j, bank, False)
             tile = keep.tile([P, K_PASS], BF16, name=f"z_turned_{j}", align_bytes=64)
             nc.scalar.copy(
                 tile[:].rearrange("m (u p e) -> m u p e", u=2, e=2),

@@ -54,6 +54,9 @@ def tile_list_passage_document_coarsening_kernel(
         nc.vector.memset(table_scales[:].bitcast(I32), 0)
         nc.vector.memset(warm_in[:], 0.0)
         nc.vector.memset(w2_planes[:].bitcast(I32), 0)
+        identity = keep.tile([P, P], F32, name="identity")
+        nc.vector.memset(identity[:], 0.0)
+        make_identity(nc, identity[:], nomemset=True)
 
         offs_t = load_list("offs_t", offs, S)
         nc.scalar.activation(warm_out[:], warm_in[:], ACT.Sigmoid)
@@ -204,13 +207,19 @@ def tile_list_passage_document_coarsening_kernel(
         def make_h(b, t, tag=None):
             evacuate_h(b, t, multiply_h(b, t), tag or f"h_{b}_{t}")
 
-        identity = keep.tile([P, P], F32, name="identity")
-        make_identity(nc, identity[:])
         near_first = keep.tile([P, PACK, PAIRS], F32, name="near_first")
 
         def pick_near(t, excess):
-            nc.vector.tensor_copy(near_first[:, t, :], h[0, t][:].indirect(pos1_t[:]))
-            nc.vector.tensor_tensor(excess, h[0, t][:].indirect(pos2_t[:]), near_first[:, t, :], ALU.subtract)
+            parts = 1 if t < 2 else 2
+            pieces = [slice(n * PAIRS // parts, (n + 1) * PAIRS // parts) for n in range(parts)]
+            for cols in pieces:
+                entries = slice(cols.start // 16, cols.stop // 16)
+                nc.vector.tensor_copy(near_first[:, t, cols], h[0, t][:].indirect(pos1_t[:, entries]))
+            for cols in pieces:
+                entries = slice(cols.start // 16, cols.stop // 16)
+                nc.vector.tensor_tensor(
+                    excess[:, cols], h[0, t][:].indirect(pos2_t[:, entries]), near_first[:, t, cols], ALU.subtract
+                )
 
         second = keep.tile([P, PACK, PAIRS], F32, name="second")
 
@@ -240,16 +249,16 @@ def tile_list_passage_document_coarsening_kernel(
 
         EARLY = PAIRS - P
 
-        def multiply_z(b, c, bank, start, stop):
-            for m in range(start, stop, P):
+        def multiply_z(b, c, bank, start, stop, width=P):
+            for m in range(start, stop, width):
                 nc.tensor.matmul_mx(
-                    out=bank[:, m - start : m - start + P],
+                    out=bank[:, m - start : m - start + width],
                     lhsT=w2_codes[:, b, 2 * c * P : 2 * (c + 1) * P].bitcast(FP4X4),
                     lhsT_scale=w2_planes[:, b, c * P : (c + 1) * P],
-                    rhs=z_codes[b][:, m : m + P].bitcast(FP8X4),
-                    rhs_scale=z_planes[b][:, m : m + P],
+                    rhs=z_codes[b][:, m : m + width].bitcast(FP8X4),
+                    rhs_scale=z_planes[b][:, m : m + width],
                     start=(b == 0 and m == start),
-                    stop=(b == 1 and m == stop - P),
+                    stop=(b == 1 and m == stop - width),
                 )
 
         round_near(1)
@@ -322,11 +331,15 @@ def tile_list_passage_document_coarsening_kernel(
         pick_far(3, 0, EARLY)
         quantize_z(0, 0, PAIRS)
         z_bf16[1] = keep.tile([P, PAIRS * PACK], BF16, name="z_bf16_1", tag="z_bf16", align_bytes=64)
-        early = [psum.tile([P, EARLY], F32, name=f"y_early_{c}", tag=f"bank_{2 * c}") for c in range(N // P)]
-        late = [psum.tile([P, P], F32, name=f"y_late_{c}", tag=f"bank_{2 * c + 1}") for c in range(N // P)]
-        for c in range(N // P):
+        SPLIT = 2
+        early = [psum.tile([P, EARLY], F32, name=f"y_early_{c}", tag=f"bank_{2 * c}") for c in range(SPLIT)]
+        late = [psum.tile([P, P], F32, name=f"y_late_{c}", tag=f"bank_{2 * c + 1}") for c in range(SPLIT)]
+        whole = {c: psum.tile([P, PAIRS], F32, name=f"y_whole_{c}", tag=f"bank_{4 + c}") for c in range(SPLIT, N // P)}
+        for c in range(SPLIT):
             multiply_z(0, c, early[c], 0, EARLY)
             multiply_z(0, c, late[c], EARLY, PAIRS)
+        for c in whole:
+            multiply_z(0, c, whole[c], 0, PAIRS, PAIRS)
         max_far(0, EARLY)
         pick_far(3, EARLY, PAIRS)
         quantize_z(1, 0, 2 * P)
@@ -334,7 +347,7 @@ def tile_list_passage_document_coarsening_kernel(
         max_far(EARLY, PAIRS)
         quantize_z(1, EARLY, PAIRS)
         y = [keep.tile([P, PAIRS], F32, name=f"y_{c}") for c in range(N // P)]
-        for c in range(N // P):
+        for c in range(SPLIT):
             multiply_z(1, c, early[c], 0, EARLY)
             multiply_z(1, c, late[c], EARLY, PAIRS)
             nc.scalar.copy(y[c][:, 0:EARLY], early[c][:])
@@ -342,6 +355,9 @@ def tile_list_passage_document_coarsening_kernel(
                 nc.vector.tensor_copy(y[c][:, EARLY:PAIRS], late[c][:])
             else:
                 nc.scalar.copy(y[c][:, EARLY:PAIRS], late[c][:])
+        for c in whole:
+            multiply_z(1, c, whole[c], 0, PAIRS, PAIRS)
+            nc.scalar.copy(y[c][:], whole[c][:])
 
         gate = {}
         kept = {}

@@ -29,6 +29,7 @@ def tile_list_passage_document_coarsening_kernel(
     nc = tc.nc
     with ExitStack() as ctx:
         keep = ctx.enter_context(tc.tile_pool(name="keep", bufs=1))
+        laid = ctx.enter_context(tc.tile_pool(name="laid", bufs=1))
         psum = ctx.enter_context(tc.psum_pool(name="psum", bufs=1))
 
         def load_list(name, src, entries):
@@ -36,8 +37,14 @@ def tile_list_passage_document_coarsening_kernel(
             nc.sync.dma_start(tile[:], src)
             return tile
 
+        KIB = 1024
+        RAW_AT = {(1, 2 * P): 3 * KIB, (1, 3 * P): 9 * KIB}
+
         def load_w1(a, start, width):
-            tile = keep.tile([P, PACK, width], F32, name=f"w1_raw_{a}_{start}", tag=f"w1_raw_{a}_{start}", align_bytes=64)
+            if (a, start) in RAW_AT:
+                tile = laid.tile([P, PACK, width], F32, name=f"w1_raw_{a}_{start}", offset=RAW_AT[a, start])
+            else:
+                tile = keep.tile([P, PACK, width], F32, name=f"w1_raw_{a}_{start}", tag=f"w1_raw_{a}_{start}", align_bytes=64)
             rows = w1[a * K_PASS : (a + 1) * K_PASS, start : start + width]
             nc.sync.dma_start(tile[:], rows.rearrange("(p j) c -> p j c", j=PACK))
             return tile
@@ -116,7 +123,7 @@ def tile_list_passage_document_coarsening_kernel(
 
         def quantize_near(t):
             near_codes[t] = keep.tile([P, 2 * P], U32, name=f"near_codes_{t}", align_bytes=64)
-            near_planes[t] = keep.tile([P, 2 * P], U8, name=f"near_plane_{t}", align_bytes=64)
+            near_planes[t] = keep.tile([P, 2 * P], U8, name=f"near_plane_{t}", tag=f"near_plane_{max(t - 1, 0) if t < 2 else t}", align_bytes=64)
             nc.vector.quantize_mx(out=near_codes[t][:].bitcast(FP8X4), scales=near_planes[t][:], in_=near_bf16[t][:])
 
         def round_far(u):
@@ -134,12 +141,14 @@ def tile_list_passage_document_coarsening_kernel(
 
         v_scales = keep.tile([P, S], U8, name="v_scales", align_bytes=64)
         HALVES = [(0, BANK), (BANK, S)]
-        FIRST_RANGES = [(0, BANK), (BANK, BANK + 2 * P), (BANK + 2 * P, S)]
+        TOP = BANK + P
+        FIRST_RANGES = [(0, BANK), (BANK, S - 2 * P), (S - 2 * P, S - P), (S - P, S)]
+        UPPER_PIECES = [(TOP, S - 2 * P), (S - 2 * P, S - P), (S - P, S)]
         v_first = keep.tile([P, S], U32, name="v_first", align_bytes=64)
-        v_low = keep.tile([P, BANK], U32, name="v_low", align_bytes=64)
+        v_low = keep.tile([P, TOP], U32, name="v_low", align_bytes=64)
 
         near_codes[0] = keep.tile([P, 2 * P], U32, name="near_codes_0", align_bytes=64)
-        near_planes[0] = keep.tile([P, 2 * P], U8, name="near_plane_0", align_bytes=64)
+        near_planes[0] = keep.tile([P, 2 * P], U8, name="near_plane_0", tag="near_plane_0", align_bytes=64)
 
         def quantize_first(a):
             stage = keep.tile([P, K_PASS], BF16, name=f"first_bf16_{a}", tag=f"first_bf16_{a}", align_bytes=64)
@@ -150,20 +159,20 @@ def tile_list_passage_document_coarsening_kernel(
         nc.vector.tensor_copy(v_scales[:], table_scales[:].indirect(offs_t[:]))
         nc.vector.tensor_copy(v_first[:], table[0][:].indirect(offs_t[:]))
         quantize_first(0)
-        nc.vector.tensor_copy(v_low[:], table[1][:].indirect(offs_t[:, 0 : BANK // 16]))
+        nc.vector.tensor_copy(v_low[:], table[1][:].indirect(offs_t[:, 0 : TOP // 16]))
         quantize_first(1)
-        v_high = keep.tile([P, BANK], U32, name="v_high", tag="first_bf16_1", align_bytes=64)
-        for start, stop in FIRST_RANGES[1:]:
+        v_high = keep.tile([P, S - TOP], U32, name="v_high", tag="w1_raw_1_0", align_bytes=64)
+        for start, stop in UPPER_PIECES:
             nc.vector.tensor_copy(
-                v_high[:, start - BANK : stop - BANK], table[1][:].indirect(offs_t[:, start // 16 : stop // 16])
+                v_high[:, start - TOP : stop - TOP], table[1][:].indirect(offs_t[:, start // 16 : stop // 16])
             )
 
         def v_codes(a, start, stop):
             if a == 0:
                 return v_first[:, start:stop]
-            if start < BANK:
+            if start < TOP:
                 return v_low[:, start:stop]
-            return v_high[:, start - BANK : stop - BANK]
+            return v_high[:, start - TOP : stop - TOP]
 
         h = {}
 
@@ -176,7 +185,7 @@ def tile_list_passage_document_coarsening_kernel(
                 codes, planes = far_codes[u], far_planes[u]
                 first_col = [(2 * a + e) * P for a in range(2)]
             ranges = FIRST_RANGES if (b, t) == (0, 0) else HALVES
-            tags = [2 * t, 2 * t + 1, 7]
+            tags = [2 * t, 2 * t + 1, 7, 6]
             banks = [
                 psum.tile([P, stop - start], F32, name=f"h_bank_{b}_{t}_{n}", tag=f"bank_{tags[n]}")
                 for n, (start, stop) in enumerate(ranges)
@@ -186,22 +195,32 @@ def tile_list_passage_document_coarsening_kernel(
                 order = sorted(order)
             for a, n in order:
                 rows = slice(first_col[a], first_col[a] + P)
-                for bank, (start, stop) in [(banks[n], ranges[n])]:
+                first, last = ranges[n]
+                cuts = [first, last]
+                if a == 1 and first < TOP < last:
+                    cuts = sorted({first, TOP, min(TOP + 2 * P, last), last})
+                for start, stop in zip(cuts, cuts[1:]):
                     nc.tensor.matmul_mx(
-                        out=bank[:],
+                        out=banks[n][:, start - first : stop - first],
                         lhsT=codes[:, rows].bitcast(FP8X4),
                         lhsT_scale=planes[:, rows],
                         rhs=v_codes(a, start, stop).bitcast(FP8X4),
                         rhs_scale=v_scales[4 * a : P, start:stop],
                         start=(a == 0),
-                        stop=(a == 1),
+                        stop=(a == 1 and stop == last),
                     )
             return list(zip(banks, ranges))
 
         def evacuate_h(b, t, banks, tag):
-            ht = keep.tile([P, S], F32, name=f"h_{b}_{t}", tag=tag, align_bytes=64)
-            for bank, (start, stop) in banks:
-                nc.scalar.copy(ht[:, start:stop], bank[:])
+            if b == 0 and t in (1, 2):
+                ht = laid.tile([P, S], F32, name=f"h_{b}_{t}", offset=6 * (t - 1) * KIB)
+            else:
+                ht = keep.tile([P, S], F32, name=f"h_{b}_{t}", tag=tag, align_bytes=64)
+            for n, (bank, (start, stop)) in enumerate(banks):
+                if n < 2:
+                    nc.scalar.copy(ht[:, start:stop], bank[:])
+                else:
+                    nc.vector.tensor_copy(ht[:, start:stop], bank[:])
             h[b, t] = ht
 
         def make_h(b, t, tag=None):
@@ -262,18 +281,18 @@ def tile_list_passage_document_coarsening_kernel(
                 )
 
         round_near(1)
-        quantize_near(1)
         make_h(0, 0, f"w1_raw_1_{P}")
+        quantize_near(1)
         round_near(2)
         quantize_near(2)
-        excess_a = keep.tile([P, 1, PAIRS], F32, name="excess_a", tag="near_bf16_2", align_bytes=64)
+        excess_a = laid.tile([P, 1, PAIRS], F32, name="excess_a", offset=4 * KIB)
         pick_near(0, excess_a[:, 0, :])
-        make_h(0, 1, f"w1_raw_1_{2 * P}")
+        make_h(0, 1)
         round_near(3)
         quantize_near(3)
-        excess_b = keep.tile([P, 3, PAIRS], F32, name="excess_b", tag="near_bf16_3", align_bytes=64)
+        excess_b = laid.tile([P, 3, PAIRS], F32, name="excess_b", offset=10 * KIB)
         pick_near(1, excess_b[:, 0, :])
-        make_h(0, 2, f"w1_raw_1_{3 * P}")
+        make_h(0, 2)
         pick_near(2, excess_b[:, 1, :])
         round_far(0)
         quantize_far(0)
@@ -309,15 +328,15 @@ def tile_list_passage_document_coarsening_kernel(
                 nc.scalar.activation(rise[:, 0:1, two], excess_a[:, :, two], ACT.Relu)
                 nc.scalar.activation(rise[:, 1:PACK, two], excess_b[:, :, two], ACT.Relu)
             turn(rise, j, bank, False)
-            tile = keep.tile([P, K_PASS], BF16, name=f"z_turned_{j}", align_bytes=64)
+            tile = keep.tile([P, K_PASS], BF16, name=f"z_turned_{j}", tag=f"z_turned_{j}", align_bytes=64)
             nc.scalar.copy(
                 tile[:].rearrange("m (u p e) -> m u p e", u=2, e=2),
                 bank[:].rearrange("m (p u e) -> m u p e", u=2, e=2),
             )
             turned.append(tile)
-        z_bf16[0] = keep.tile([P, PAIRS * PACK], BF16, name="z_bf16_0", tag="z_bf16", align_bytes=64)
+        z_bf16[0] = keep.tile([P, PAIRS * PACK], BF16, name="z_bf16_0", align_bytes=64)
         for half in range(2):
-            bank = psum.tile([P, 2, 2, P], F32, name=f"z_back_bank_{half}", tag=f"bank_{4 + half}")
+            bank = psum.tile([P, 2, 2, P], F32, name=f"z_back_bank_{half}", tag="bank_4")
             for jj in range(2):
                 words = turned[2 * half + jj][:].bitcast(F32)
                 for u in range(2):
@@ -328,9 +347,10 @@ def tile_list_passage_document_coarsening_kernel(
             )
         pick_far(1)
         pick_far(2)
-        pick_far(3, 0, EARLY)
-        quantize_z(0, 0, PAIRS)
-        z_bf16[1] = keep.tile([P, PAIRS * PACK], BF16, name="z_bf16_1", tag="z_bf16", align_bytes=64)
+        pick_far(3)
+        quantize_z(0, 0, 2 * P)
+        quantize_z(0, 2 * P, PAIRS)
+        z_bf16[1] = keep.tile([P, PAIRS * PACK], BF16, name="z_bf16_1", tag="z_turned_3", align_bytes=64)
         SPLIT = 2
         early = [psum.tile([P, EARLY], F32, name=f"y_early_{c}", tag=f"bank_{2 * c}") for c in range(SPLIT)]
         late = [psum.tile([P, P], F32, name=f"y_late_{c}", tag=f"bank_{2 * c + 1}") for c in range(SPLIT)]
@@ -339,22 +359,19 @@ def tile_list_passage_document_coarsening_kernel(
             multiply_z(0, c, early[c], 0, EARLY)
             multiply_z(0, c, late[c], EARLY, PAIRS)
         for c in whole:
-            multiply_z(0, c, whole[c], 0, PAIRS, PAIRS)
-        max_far(0, EARLY)
-        pick_far(3, EARLY, PAIRS)
+            multiply_z(0, c, whole[c], 0, PAIRS, 2 * P)
+        max_far(0, 2 * P)
+        max_far(2 * P, EARLY)
         quantize_z(1, 0, 2 * P)
-        quantize_z(1, 2 * P, EARLY)
         max_far(EARLY, PAIRS)
+        quantize_z(1, 2 * P, EARLY)
         quantize_z(1, EARLY, PAIRS)
         y = [keep.tile([P, PAIRS], F32, name=f"y_{c}") for c in range(N // P)]
         for c in range(SPLIT):
             multiply_z(1, c, early[c], 0, EARLY)
             multiply_z(1, c, late[c], EARLY, PAIRS)
             nc.scalar.copy(y[c][:, 0:EARLY], early[c][:])
-            if c == 0:
-                nc.vector.tensor_copy(y[c][:, EARLY:PAIRS], late[c][:])
-            else:
-                nc.scalar.copy(y[c][:, EARLY:PAIRS], late[c][:])
+            nc.vector.tensor_copy(y[c][:, EARLY:PAIRS], late[c][:])
         for c in whole:
             multiply_z(1, c, whole[c], 0, PAIRS, PAIRS)
             nc.scalar.copy(y[c][:], whole[c][:])

@@ -21,6 +21,26 @@ P = 128
 PACK = 4
 K_PASS = P * PACK
 BANK = 512
+GROUP = 16
+QUADRANTS = 4
+KIB = 1024
+
+RAW_AT = {(1, 2 * P): 3 * KIB, (1, 3 * P): 9 * KIB}
+H_AT = {(0, 1): 0, (0, 2): 6 * KIB}
+FIRST_EXCESS_AT = 4 * KIB
+LATER_EXCESS_AT = 10 * KIB
+
+LOWER = BANK + P
+UPPER_PIECES = [(start, start + P) for start in range(LOWER, S, P)]
+HALVES = [(0, BANK), (BANK, S)]
+FIRST_RANGES = [(0, BANK), (BANK, S - 2 * P), (S - 2 * P, S - P), (S - P, S)]
+Z_CUTS = (2 * P, 3 * P)
+Y_RANGES = [
+    [(0, Z_CUTS[0], 0), (Z_CUTS[0], Z_CUTS[1], 5), (Z_CUTS[1], PAIRS, 1)],
+    [(0, Z_CUTS[1], 2), (Z_CUTS[1], PAIRS, 3)],
+    [(0, PAIRS, 6)],
+    [(0, PAIRS, 7)],
+]
 
 
 def tile_list_passage_document_coarsening_kernel(
@@ -32,19 +52,21 @@ def tile_list_passage_document_coarsening_kernel(
         laid = ctx.enter_context(tc.tile_pool(name="laid", bufs=1))
         psum = ctx.enter_context(tc.psum_pool(name="psum", bufs=1))
 
+
         def load_list(name, src, entries):
-            tile = keep.tile([P, entries // 16], U16, name=name)
+            tile = keep.tile([P, entries // GROUP], U16, name=name)
             nc.sync.dma_start(tile[:], src)
             return tile
 
-        KIB = 1024
-        RAW_AT = {(1, 2 * P): 3 * KIB, (1, 3 * P): 9 * KIB}
+        def entries_of(list_tile, start, stop):
+            return list_tile[:, start // GROUP : stop // GROUP]
 
         def load_w1(a, start, width):
+            name = f"w1_raw_{a}_{start}"
             if (a, start) in RAW_AT:
-                tile = laid.tile([P, PACK, width], F32, name=f"w1_raw_{a}_{start}", offset=RAW_AT[a, start])
+                tile = laid.tile([P, PACK, width], F32, name=name, offset=RAW_AT[a, start])
             else:
-                tile = keep.tile([P, PACK, width], F32, name=f"w1_raw_{a}_{start}", tag=f"w1_raw_{a}_{start}", align_bytes=64)
+                tile = keep.tile([P, PACK, width], F32, name=name, tag=name, align_bytes=64)
             rows = w1[a * K_PASS : (a + 1) * K_PASS, start : start + width]
             nc.sync.dma_start(tile[:], rows.rearrange("(p j) c -> p j c", j=PACK))
             return tile
@@ -71,12 +93,12 @@ def tile_list_passage_document_coarsening_kernel(
 
         def load_near(a, tiles):
             chunk = load_w1(a, tiles[0] * P, len(tiles) * P)
-            for slot, t in enumerate(tiles):
-                near_raw[t, a] = chunk[:, :, slot * P : (slot + 1) * P]
+            for place, t in enumerate(tiles):
+                near_raw[t, a] = chunk[:, :, place * P : (place + 1) * P]
 
         pos1_t = load_list("pos1_t", pos1, PAIRS)
         pos2_t = load_list("pos2_t", pos2, PAIRS)
-        for q in range(4):
+        for q in range(QUADRANTS):
             nc.sync.dma_start(
                 table_scales[32 * q : 32 * q + 8, :].bitcast(I32), tab_scales[:, 4 * q : 4 * q + 4, :].bitcast(I32)
             )
@@ -92,7 +114,7 @@ def tile_list_passage_document_coarsening_kernel(
         far_raw = [load_w1(a, K_PASS, K_PASS) for a in range(2)]
         w2_codes = keep.tile([P, 2, 2 * N], U8, name="w2_codes", align_bytes=64)
         nc.sync.dma_start(w2_codes[:].bitcast(I32), w2_words.rearrange("a p c -> p a c").bitcast(I32))
-        for q in range(4):
+        for q in range(QUADRANTS):
             nc.sync.dma_start(
                 w2_planes[32 * q : 32 * q + 4, :, :].bitcast(I32),
                 w2_scales[:, 4 * q : 4 * q + 4, :].rearrange("a r c -> r a c").bitcast(I32),
@@ -102,6 +124,7 @@ def tile_list_passage_document_coarsening_kernel(
         w_col = keep.tile([P, N // P], F32, name="w_col")
         with nc.allow_non_contiguous_dma(reason="one value of w for each partition"):
             nc.sync.dma_start(w_col[:], w.rearrange("(c p) -> p c", p=P))
+
 
         near_bf16 = {}
         near_codes = {}
@@ -117,17 +140,17 @@ def tile_list_passage_document_coarsening_kernel(
             )
 
         def round_near(t):
-            near_bf16[t] = keep.tile([P, 2 * K_PASS], BF16, name=f"near_bf16_{t}", tag=f"near_bf16_{t}", align_bytes=64)
+            near_bf16[t] = keep.tile([P, 2 * K_PASS], BF16, name=f"near_bf16_{t}", align_bytes=64)
             for a in range(2):
                 round_pass(near_bf16[t][:, a * K_PASS : (a + 1) * K_PASS], t, a)
 
-        def quantize_near(t):
+        def quantize_near(t, plane_tag):
             near_codes[t] = keep.tile([P, 2 * P], U32, name=f"near_codes_{t}", align_bytes=64)
-            near_planes[t] = keep.tile([P, 2 * P], U8, name=f"near_plane_{t}", tag=f"near_plane_{max(t - 1, 0) if t < 2 else t}", align_bytes=64)
+            near_planes[t] = keep.tile([P, 2 * P], U8, name=f"near_plane_{t}", tag=plane_tag, align_bytes=64)
             nc.vector.quantize_mx(out=near_codes[t][:].bitcast(FP8X4), scales=near_planes[t][:], in_=near_bf16[t][:])
 
         def round_far(u):
-            far_bf16[u] = keep.tile([P, 4 * K_PASS], BF16, name=f"far_bf16_{u}", tag=f"far_bf16_{u}", align_bytes=64)
+            far_bf16[u] = keep.tile([P, 4 * K_PASS], BF16, name=f"far_bf16_{u}", align_bytes=64)
             for a in range(2):
                 nc.scalar.copy(
                     far_bf16[u][:, 2 * a * K_PASS : 2 * (a + 1) * K_PASS].rearrange("p (t m j) -> p m j t", t=2, j=PACK),
@@ -139,19 +162,15 @@ def tile_list_passage_document_coarsening_kernel(
             far_planes[u] = keep.tile([P, 4 * P], U8, name=f"far_plane_{u}", align_bytes=64)
             nc.vector.quantize_mx(out=far_codes[u][:].bitcast(FP8X4), scales=far_planes[u][:], in_=far_bf16[u][:])
 
-        v_scales = keep.tile([P, S], U8, name="v_scales", align_bytes=64)
-        HALVES = [(0, BANK), (BANK, S)]
-        TOP = BANK + P
-        FIRST_RANGES = [(0, BANK), (BANK, S - 2 * P), (S - 2 * P, S - P), (S - P, S)]
-        UPPER_PIECES = [(TOP, S - 2 * P), (S - 2 * P, S - P), (S - P, S)]
-        v_first = keep.tile([P, S], U32, name="v_first", align_bytes=64)
-        v_low = keep.tile([P, TOP], U32, name="v_low", align_bytes=64)
 
+        v_scales = keep.tile([P, S], U8, name="v_scales", align_bytes=64)
+        v_first = keep.tile([P, S], U32, name="v_first", align_bytes=64)
+        v_lower = keep.tile([P, LOWER], U32, name="v_lower", align_bytes=64)
         near_codes[0] = keep.tile([P, 2 * P], U32, name="near_codes_0", align_bytes=64)
         near_planes[0] = keep.tile([P, 2 * P], U8, name="near_plane_0", tag="near_plane_0", align_bytes=64)
 
         def quantize_first(a):
-            stage = keep.tile([P, K_PASS], BF16, name=f"first_bf16_{a}", tag=f"first_bf16_{a}", align_bytes=64)
+            stage = keep.tile([P, K_PASS], BF16, name=f"first_bf16_{a}", align_bytes=64)
             round_pass(stage[:], 0, a)
             cols = slice(a * P, (a + 1) * P)
             nc.vector.quantize_mx(out=near_codes[0][:, cols].bitcast(FP8X4), scales=near_planes[0][:, cols], in_=stage[:])
@@ -159,20 +178,21 @@ def tile_list_passage_document_coarsening_kernel(
         nc.vector.tensor_copy(v_scales[:], table_scales[:].indirect(offs_t[:]))
         nc.vector.tensor_copy(v_first[:], table[0][:].indirect(offs_t[:]))
         quantize_first(0)
-        nc.vector.tensor_copy(v_low[:], table[1][:].indirect(offs_t[:, 0 : TOP // 16]))
+        nc.vector.tensor_copy(v_lower[:], table[1][:].indirect(entries_of(offs_t, 0, LOWER)))
         quantize_first(1)
-        v_high = keep.tile([P, S - TOP], U32, name="v_high", tag="w1_raw_1_0", align_bytes=64)
+        v_upper = keep.tile([P, S - LOWER], U32, name="v_upper", tag="w1_raw_1_0", align_bytes=64)
         for start, stop in UPPER_PIECES:
             nc.vector.tensor_copy(
-                v_high[:, start - TOP : stop - TOP], table[1][:].indirect(offs_t[:, start // 16 : stop // 16])
+                v_upper[:, start - LOWER : stop - LOWER], table[1][:].indirect(entries_of(offs_t, start, stop))
             )
 
         def v_codes(a, start, stop):
             if a == 0:
                 return v_first[:, start:stop]
-            if start < TOP:
-                return v_low[:, start:stop]
-            return v_high[:, start - TOP : stop - TOP]
+            if start < LOWER:
+                return v_lower[:, start:stop]
+            return v_upper[:, start - LOWER : stop - LOWER]
+
 
         h = {}
 
@@ -185,67 +205,63 @@ def tile_list_passage_document_coarsening_kernel(
                 codes, planes = far_codes[u], far_planes[u]
                 first_col = [(2 * a + e) * P for a in range(2)]
             ranges = FIRST_RANGES if (b, t) == (0, 0) else HALVES
-            tags = [2 * t, 2 * t + 1, 7, 6]
+            bank_numbers = [2 * t, 2 * t + 1, 7, 6]
             banks = [
-                psum.tile([P, stop - start], F32, name=f"h_bank_{b}_{t}_{n}", tag=f"bank_{tags[n]}")
+                psum.tile([P, stop - start], F32, name=f"h_bank_{b}_{t}_{n}", tag=f"bank_{bank_numbers[n]}")
                 for n, (start, stop) in enumerate(ranges)
             ]
             order = [(a, n) for n in range(len(ranges)) for a in range(2)]
             if (b, t) == (0, 0):
                 order = sorted(order)
             for a, n in order:
-                rows = slice(first_col[a], first_col[a] + P)
-                first, last = ranges[n]
-                cuts = [first, last]
-                if a == 1 and first < TOP < last:
-                    cuts = sorted({first, TOP, min(TOP + 2 * P, last), last})
+                weights = slice(first_col[a], first_col[a] + P)
+                begin, end = ranges[n]
+                cuts = [begin, end]
+                if a == 1 and begin < LOWER < end:
+                    cuts = sorted({begin, LOWER, min(LOWER + 2 * P, end), end})
                 for start, stop in zip(cuts, cuts[1:]):
                     nc.tensor.matmul_mx(
-                        out=banks[n][:, start - first : stop - first],
-                        lhsT=codes[:, rows].bitcast(FP8X4),
-                        lhsT_scale=planes[:, rows],
+                        out=banks[n][:, start - begin : stop - begin],
+                        lhsT=codes[:, weights].bitcast(FP8X4),
+                        lhsT_scale=planes[:, weights],
                         rhs=v_codes(a, start, stop).bitcast(FP8X4),
                         rhs_scale=v_scales[4 * a : P, start:stop],
                         start=(a == 0),
-                        stop=(a == 1 and stop == last),
+                        stop=(a == 1 and stop == end),
                     )
             return list(zip(banks, ranges))
 
-        def evacuate_h(b, t, banks, tag):
-            if b == 0 and t in (1, 2):
-                ht = laid.tile([P, S], F32, name=f"h_{b}_{t}", offset=6 * (t - 1) * KIB)
-            else:
-                ht = keep.tile([P, S], F32, name=f"h_{b}_{t}", tag=tag, align_bytes=64)
-            for n, (bank, (start, stop)) in enumerate(banks):
-                if n < 2:
-                    nc.scalar.copy(ht[:, start:stop], bank[:])
-                else:
-                    nc.vector.tensor_copy(ht[:, start:stop], bank[:])
-            h[b, t] = ht
-
         def make_h(b, t, tag=None):
-            evacuate_h(b, t, multiply_h(b, t), tag or f"h_{b}_{t}")
+            banks = multiply_h(b, t)
+            name = f"h_{b}_{t}"
+            if (b, t) in H_AT:
+                h[b, t] = laid.tile([P, S], F32, name=name, offset=H_AT[b, t])
+            else:
+                h[b, t] = keep.tile([P, S], F32, name=name, tag=tag or name, align_bytes=64)
+            for n, (bank, (start, stop)) in enumerate(banks):
+                copy_out = nc.scalar.copy if n < len(HALVES) else nc.vector.tensor_copy
+                copy_out(h[b, t][:, start:stop], bank[:])
 
         near_first = keep.tile([P, PACK, PAIRS], F32, name="near_first")
 
-        def pick_near(t, excess):
-            parts = 1 if t < 2 else 2
-            pieces = [slice(n * PAIRS // parts, (n + 1) * PAIRS // parts) for n in range(parts)]
-            for cols in pieces:
-                entries = slice(cols.start // 16, cols.stop // 16)
-                nc.vector.tensor_copy(near_first[:, t, cols], h[0, t][:].indirect(pos1_t[:, entries]))
-            for cols in pieces:
-                entries = slice(cols.start // 16, cols.stop // 16)
+        def pick_near(t, excess, parts):
+            pieces = [(n * PAIRS // parts, (n + 1) * PAIRS // parts) for n in range(parts)]
+            for start, stop in pieces:
+                nc.vector.tensor_copy(near_first[:, t, start:stop], h[0, t][:].indirect(entries_of(pos1_t, start, stop)))
+            for start, stop in pieces:
                 nc.vector.tensor_tensor(
-                    excess[:, cols], h[0, t][:].indirect(pos2_t[:, entries]), near_first[:, t, cols], ALU.subtract
+                    excess[:, start:stop],
+                    h[0, t][:].indirect(entries_of(pos2_t, start, stop)),
+                    near_first[:, t, start:stop],
+                    ALU.subtract,
                 )
 
-        second = keep.tile([P, PACK, PAIRS], F32, name="second")
+        far_second = keep.tile([P, PACK, PAIRS], F32, name="far_second")
 
-        def pick_far(t, start=0, stop=PAIRS):
-            entries = slice(start // 16, stop // 16)
-            nc.vector.tensor_copy(first[:, t, start:stop], h[1, t][:].indirect(pos1_t[:, entries]))
-            nc.vector.tensor_copy(second[:, t, start:stop], h[1, t][:].indirect(pos2_t[:, entries]))
+        def pick_far(t):
+            nc.vector.tensor_copy(far_first[:, t, :], h[1, t][:].indirect(pos1_t[:]))
+            nc.vector.tensor_copy(far_second[:, t, :], h[1, t][:].indirect(pos2_t[:]))
+
 
         z_bf16 = {}
         z_codes = [keep.tile([P, PAIRS], U32, name=f"z_codes_{b}", align_bytes=64) for b in range(2)]
@@ -254,8 +270,8 @@ def tile_list_passage_document_coarsening_kernel(
         def max_far(start, stop):
             nc.vector.tensor_tensor(
                 z_bf16[1][:, start * PACK : stop * PACK].rearrange("p (c i t) -> p c t i", i=2, t=PACK),
-                first[:, :, start:stop].rearrange("p t (c i) -> p c t i", i=2),
-                second[:, :, start:stop].rearrange("p t (c i) -> p c t i", i=2),
+                far_first[:, :, start:stop].rearrange("p t (c i) -> p c t i", i=2),
+                far_second[:, :, start:stop].rearrange("p t (c i) -> p c t i", i=2),
                 ALU.max,
             )
 
@@ -266,9 +282,7 @@ def tile_list_passage_document_coarsening_kernel(
                 in_=z_bf16[b][:, start * PACK : stop * PACK],
             )
 
-        EARLY = PAIRS - P
-
-        def multiply_z(b, c, bank, start, stop, width=P):
+        def multiply_z(b, c, bank, start, stop, width):
             for m in range(start, stop, width):
                 nc.tensor.matmul_mx(
                     out=bank[:, m - start : m - start + width],
@@ -282,30 +296,31 @@ def tile_list_passage_document_coarsening_kernel(
 
         round_near(1)
         make_h(0, 0, f"w1_raw_1_{P}")
-        quantize_near(1)
+        quantize_near(1, "near_plane_0")
         round_near(2)
-        quantize_near(2)
-        excess_a = laid.tile([P, 1, PAIRS], F32, name="excess_a", offset=4 * KIB)
-        pick_near(0, excess_a[:, 0, :])
+        quantize_near(2, "near_plane_2")
+        first_excess = laid.tile([P, 1, PAIRS], F32, name="first_excess", offset=FIRST_EXCESS_AT)
+        pick_near(0, first_excess[:, 0, :], 1)
         make_h(0, 1)
         round_near(3)
-        quantize_near(3)
-        excess_b = laid.tile([P, 3, PAIRS], F32, name="excess_b", offset=10 * KIB)
-        pick_near(1, excess_b[:, 0, :])
+        quantize_near(3, "near_plane_3")
+        later_excess = laid.tile([P, PACK - 1, PAIRS], F32, name="later_excess", offset=LATER_EXCESS_AT)
+        pick_near(1, later_excess[:, 0, :], 1)
         make_h(0, 2)
-        pick_near(2, excess_b[:, 1, :])
+        pick_near(2, later_excess[:, 1, :], 2)
         round_far(0)
         quantize_far(0)
         make_h(0, 3)
-        pick_near(3, excess_b[:, 2, :])
+        pick_near(3, later_excess[:, 2, :], 2)
         round_far(1)
         quantize_far(1)
         make_h(1, 0)
         make_h(1, 1)
-        first = keep.tile([P, PACK, PAIRS], F32, name="first")
+        far_first = keep.tile([P, PACK, PAIRS], F32, name="far_first")
         pick_far(0)
         make_h(1, 2)
         make_h(1, 3)
+
         def turn(src, j, bank, opens):
             for t in range(PACK):
                 nc.tensor.matmul(
@@ -324,9 +339,9 @@ def tile_list_passage_document_coarsening_kernel(
         rise = keep.tile([P, PACK, PAIRS], F32, name="rise", tag="far_codes_1", align_bytes=64)
         for j, bank in enumerate(turn_banks):
             if j % 2 == 0:
-                two = slice(j * P, (j + 2) * P)
-                nc.scalar.activation(rise[:, 0:1, two], excess_a[:, :, two], ACT.Relu)
-                nc.scalar.activation(rise[:, 1:PACK, two], excess_b[:, :, two], ACT.Relu)
+                two_blocks = slice(j * P, (j + 2) * P)
+                nc.scalar.activation(rise[:, 0:1, two_blocks], first_excess[:, :, two_blocks], ACT.Relu)
+                nc.scalar.activation(rise[:, 1:PACK, two_blocks], later_excess[:, :, two_blocks], ACT.Relu)
             turn(rise, j, bank, False)
             tile = keep.tile([P, K_PASS], BF16, name=f"z_turned_{j}", tag=f"z_turned_{j}", align_bytes=64)
             nc.scalar.copy(
@@ -337,44 +352,37 @@ def tile_list_passage_document_coarsening_kernel(
         z_bf16[0] = keep.tile([P, PAIRS * PACK], BF16, name="z_bf16_0", align_bytes=64)
         for half in range(2):
             bank = psum.tile([P, 2, 2, P], F32, name=f"z_back_bank_{half}", tag="bank_4")
-            for jj in range(2):
-                words = turned[2 * half + jj][:].bitcast(F32)
+            for block in range(2):
+                words = turned[2 * half + block][:].bitcast(F32)
                 for u in range(2):
-                    nc.tensor.transpose(bank[:, jj, u, :], words[:, u * P : (u + 1) * P], identity[:])
-            nc.scalar.copy(
-                z_bf16[0][:, half * 2 * K_PASS : (half + 1) * 2 * K_PASS].bitcast(F32).rearrange("p (j m u) -> p j m u", j=2, u=2),
-                bank[:].rearrange("p j u m -> p j m u"),
-            )
-        pick_far(1)
-        pick_far(2)
-        pick_far(3)
-        quantize_z(0, 0, 2 * P)
-        quantize_z(0, 2 * P, PAIRS)
+                    nc.tensor.transpose(bank[:, block, u, :], words[:, u * P : (u + 1) * P], identity[:])
+            z_words = z_bf16[0][:, half * 2 * K_PASS : (half + 1) * 2 * K_PASS].bitcast(F32)
+            nc.scalar.copy(z_words.rearrange("p (j m u) -> p j m u", j=2, u=2), bank[:].rearrange("p j u m -> p j m u"))
+        for t in range(1, PACK):
+            pick_far(t)
+        quantize_z(0, 0, PAIRS // 2)
+        quantize_z(0, PAIRS // 2, PAIRS)
         z_bf16[1] = keep.tile([P, PAIRS * PACK], BF16, name="z_bf16_1", tag="z_turned_3", align_bytes=64)
-        SPLIT = 2
-        early = [psum.tile([P, EARLY], F32, name=f"y_early_{c}", tag=f"bank_{2 * c}") for c in range(SPLIT)]
-        late = [psum.tile([P, P], F32, name=f"y_late_{c}", tag=f"bank_{2 * c + 1}") for c in range(SPLIT)]
-        whole = {c: psum.tile([P, PAIRS], F32, name=f"y_whole_{c}", tag=f"bank_{4 + c}") for c in range(SPLIT, N // P)}
-        for c in range(SPLIT):
-            multiply_z(0, c, early[c], 0, EARLY)
-            multiply_z(0, c, late[c], EARLY, PAIRS)
-        for c in whole:
-            multiply_z(0, c, whole[c], 0, PAIRS, 2 * P)
-        max_far(0, 2 * P)
-        max_far(2 * P, EARLY)
-        quantize_z(1, 0, 2 * P)
-        max_far(EARLY, PAIRS)
-        quantize_z(1, 2 * P, EARLY)
-        quantize_z(1, EARLY, PAIRS)
+
+
+        y_banks = {}
+        for c, ranges in enumerate(Y_RANGES):
+            for start, stop, n in ranges:
+                y_banks[c, start] = psum.tile([P, stop - start], F32, name=f"y_bank_{c}_{start}", tag=f"bank_{n}")
+                multiply_z(0, c, y_banks[c, start], start, stop, P if (stop - start) % (2 * P) else 2 * P)
+        max_far(0, Z_CUTS[0])
+        max_far(Z_CUTS[0], Z_CUTS[1])
+        quantize_z(1, 0, Z_CUTS[0])
+        max_far(Z_CUTS[1], PAIRS)
+        quantize_z(1, Z_CUTS[0], Z_CUTS[1])
+        quantize_z(1, Z_CUTS[1], PAIRS)
         y = [keep.tile([P, PAIRS], F32, name=f"y_{c}") for c in range(N // P)]
-        for c in range(SPLIT):
-            multiply_z(1, c, early[c], 0, EARLY)
-            multiply_z(1, c, late[c], EARLY, PAIRS)
-            nc.scalar.copy(y[c][:, 0:EARLY], early[c][:])
-            nc.vector.tensor_copy(y[c][:, EARLY:PAIRS], late[c][:])
-        for c in whole:
-            multiply_z(1, c, whole[c], 0, PAIRS, PAIRS)
-            nc.scalar.copy(y[c][:], whole[c][:])
+        for c, ranges in enumerate(Y_RANGES):
+            copy_out = nc.vector.tensor_copy if c == 1 else nc.scalar.copy
+            for start, stop, n in ranges:
+                multiply_z(1, c, y_banks[c, start], start, stop, P if (stop - start) % (2 * P) else stop - start)
+                copy_out(y[c][:, start:stop], y_banks[c, start][:])
+
 
         gate = {}
         kept = {}

@@ -387,6 +387,9 @@ def tile_list_passage_document_coarsening_kernel(
         gate = {}
         kept = {}
 
+        def doc_pieces(c):
+            return [(0, DOCS // 2), (DOCS // 2, DOCS)] if c == N // P - 1 else [(0, DOCS)]
+
         def pick_y(c):
             right = keep.tile([P, DOCS], F32, name=f"right_{c}", tag=f"right_{c}")
             nc.vector.tensor_copy(right[:], y[c][:].indirect(pos4_t[:]))
@@ -395,12 +398,18 @@ def tile_list_passage_document_coarsening_kernel(
             nc.scalar.activation(stay[:], right[:], ACT.Sigmoid, scale=-1.0)
             nc.scalar.activation(gate[c][:], right[:], ACT.Sigmoid)
             kept[c] = keep.tile([P, DOCS], F32, name=f"kept_{c}")
-            nc.vector.tensor_tensor(kept[c][:], y[c][:].indirect(pos3_t[:]), stay[:], ALU.mult)
+            for start, stop in doc_pieces(c):
+                nc.vector.tensor_tensor(
+                    kept[c][:, start:stop], y[c][:].indirect(entries_of(pos3_t, start, stop)), stay[:, start:stop], ALU.mult
+                )
 
         def store_doc(c):
             doc = keep.tile([P, DOCS], F32, name=f"doc_{c}", tag=f"right_{c + 1}")
-            nc.vector.scalar_tensor_tensor(doc[:], gate[c][:], w_col[:, c : c + 1], kept[c][:], ALU.mult, ALU.add)
-            nc.sync.dma_start(out[c * P : (c + 1) * P, :], doc[:])
+            for start, stop in doc_pieces(c):
+                nc.vector.scalar_tensor_tensor(
+                    doc[:, start:stop], gate[c][:, start:stop], w_col[:, c : c + 1], kept[c][:, start:stop], ALU.mult, ALU.add
+                )
+                nc.sync.dma_start(out[c * P : (c + 1) * P, start:stop], doc[:, start:stop])
 
         pick_y(0)
         for c in range(1, N // P):

@@ -23,6 +23,7 @@ K_PASS = P * PACK
 BANK = 512
 GROUP = 16
 QUADRANTS = 4
+F32_MAX = 3.4028234663852886e38
 KIB = 1024
 
 RAW_AT = {(1, 2 * P): 3 * KIB, (1, 3 * P): 9 * KIB}
@@ -318,8 +319,21 @@ def tile_list_passage_document_coarsening_kernel(
         make_h(1, 1)
         far_first = keep.tile([P, PACK, PAIRS], F32, name="far_first")
         pick_far(0)
+        rise = {}
+
+        def relu_near(half, tag):
+            rise[half] = keep.tile([P, PACK, 2 * P], F32, name=f"rise_{half}", tag=tag, align_bytes=64)
+            two_blocks = slice(2 * half * P, 2 * (half + 1) * P)
+            for dst, src in ((rise[half][:, 0:1, :], first_excess), (rise[half][:, 1:PACK, :], later_excess)):
+                if half == 0:
+                    nc.scalar.activation(dst, src[:, :, two_blocks], ACT.Relu)
+                else:
+                    nc.gpsimd.tensor_scalar(dst, src[:, :, two_blocks], F32_MAX, 0.0, ALU.min, ALU.max)
+
+        relu_near(0, "far_codes_0")
         make_h(1, 2)
         make_h(1, 3)
+        relu_near(1, "far_codes_1")
 
         def turn(src, j, bank, opens):
             for t in range(PACK):
@@ -333,16 +347,10 @@ def tile_list_passage_document_coarsening_kernel(
                 )
 
         turn_banks = [psum.tile([P, K_PASS], F32, name=f"z_turned_bank_{j}", tag=f"bank_{j}") for j in range(PAIRS // P)]
+        turned = []
         for j, bank in enumerate(turn_banks):
             turn(near_first, j, bank, True)
-        turned = []
-        rise = keep.tile([P, PACK, PAIRS], F32, name="rise", tag="far_codes_1", align_bytes=64)
-        for j, bank in enumerate(turn_banks):
-            if j % 2 == 0:
-                two_blocks = slice(j * P, (j + 2) * P)
-                nc.scalar.activation(rise[:, 0:1, two_blocks], first_excess[:, :, two_blocks], ACT.Relu)
-                nc.scalar.activation(rise[:, 1:PACK, two_blocks], later_excess[:, :, two_blocks], ACT.Relu)
-            turn(rise, j, bank, False)
+            turn(rise[j // 2], j % 2, bank, False)
             tile = keep.tile([P, K_PASS], BF16, name=f"z_turned_{j}", tag=f"z_turned_{j}", align_bytes=64)
             nc.scalar.copy(
                 tile[:].rearrange("m (u p e) -> m u p e", u=2, e=2),

@@ -35,13 +35,15 @@ LOWER = BANK + P
 UPPER_PIECES = [(start, start + P) for start in range(LOWER, S, P)]
 HALVES = [(0, BANK), (BANK, S)]
 FIRST_RANGES = [(0, BANK), (BANK, S - 2 * P), (S - 2 * P, S - P), (S - P, S)]
-Z_CUTS = (2 * P, 3 * P)
+KEPT = 2 * P
 Y_RANGES = [
-    [(0, Z_CUTS[0], 0), (Z_CUTS[0], Z_CUTS[1], 5), (Z_CUTS[1], PAIRS, 1)],
-    [(0, Z_CUTS[1], 2), (Z_CUTS[1], PAIRS, 3)],
-    [(0, PAIRS, 6)],
+    [(0, KEPT, 0), (KEPT, 3 * P, 2), (3 * P, PAIRS, 6)],
+    [(0, 3 * P, 1), (3 * P, PAIRS, 4)],
+    [(0, PAIRS, 3)],
     [(0, PAIRS, 7)],
 ]
+LATE_AT = 16 * KIB
+LAST_TURNED_AT = 17 * KIB
 
 
 def tile_list_passage_document_coarsening_kernel(
@@ -206,7 +208,8 @@ def tile_list_passage_document_coarsening_kernel(
                 codes, planes = far_codes[u], far_planes[u]
                 first_col = [(2 * a + e) * P for a in range(2)]
             ranges = FIRST_RANGES if (b, t) == (0, 0) else HALVES
-            bank_numbers = [2 * t, 2 * t + 1, 7, 6]
+            first_bank = 2 * t if b == 0 else 6 * (t % 2)
+            bank_numbers = [first_bank, first_bank + 1, 7, 6]
             banks = [
                 psum.tile([P, stop - start], F32, name=f"h_bank_{b}_{t}_{n}", tag=f"bank_{bank_numbers[n]}")
                 for n, (start, stop) in enumerate(ranges)
@@ -257,43 +260,61 @@ def tile_list_passage_document_coarsening_kernel(
                     ALU.subtract,
                 )
 
-        far_second = keep.tile([P, PACK, PAIRS], F32, name="far_second")
+        def relu_beside(dst, src):
+            nc.gpsimd.tensor_scalar(dst, src, F32_MAX, 0.0, ALU.min, ALU.max)
+
+        def add_turned(dst, src, start, stop):
+            nc.tensor.matmul(dst, lhsT=src, rhs=identity[:], is_transpose=True, start=start, stop=stop)
+
+        near_rise = {}
+
+        def relu_near(t, excess, tag=None):
+            name = f"near_rise_{t}"
+            near_rise[t] = keep.tile([P, PAIRS], F32, name=name, tag=tag or name, align_bytes=64)
+            relu_beside(near_rise[t][:], excess)
+
+        def turn_near(t, src, opens, closes):
+            for j, bank in enumerate(turn_banks):
+                add_turned(bank[:, t * P : (t + 1) * P], src[:, j * P : (j + 1) * P], opens, closes)
+
+        far_first = {}
+        far_excess = {}
+        far_rise = {}
+        kept_first = keep.tile([P, PACK, KEPT], F32, name="kept_first")
+
+        def pick_kept(dst, t, list_tile, start=0, stop=KEPT):
+            nc.vector.tensor_copy(dst[:, t, start:stop], h[1, t][:].indirect(entries_of(list_tile, start, stop)))
 
         def pick_far(t):
-            nc.vector.tensor_copy(far_first[:, t, :], h[1, t][:].indirect(pos1_t[:]))
-            nc.vector.tensor_copy(far_second[:, t, :], h[1, t][:].indirect(pos2_t[:]))
-
-
-        z_bf16 = {}
-        z_codes = [keep.tile([P, PAIRS], U32, name=f"z_codes_{b}", align_bytes=64) for b in range(2)]
-        z_planes = [keep.tile([P, PAIRS], U8, name=f"z_plane_{b}", align_bytes=64) for b in range(2)]
-
-        def max_far(start, stop):
+            far_first[t] = keep.tile([P, PAIRS - KEPT], F32, name=f"far_first_{t}", tag=f"far_first_{t}")
+            far_excess[t] = keep.tile([P, PAIRS - KEPT], F32, name=f"far_excess_{t}")
+            nc.vector.tensor_copy(far_first[t][:], h[1, t][:].indirect(entries_of(pos1_t, KEPT, PAIRS)))
+            pick_kept(kept_first, t, pos1_t)
             nc.vector.tensor_tensor(
-                z_bf16[1][:, start * PACK : stop * PACK].rearrange("p (c i t) -> p c t i", i=2, t=PACK),
-                far_first[:, :, start:stop].rearrange("p t (c i) -> p c t i", i=2),
-                far_second[:, :, start:stop].rearrange("p t (c i) -> p c t i", i=2),
-                ALU.max,
+                far_excess[t][:], h[1, t][:].indirect(entries_of(pos2_t, KEPT, PAIRS)), far_first[t][:], ALU.subtract
             )
 
-        def quantize_z(b, start, stop):
-            nc.vector.quantize_mx(
-                out=z_codes[b][:, start:stop].bitcast(FP8X4),
-                scales=z_planes[b][:, start:stop],
-                in_=z_bf16[b][:, start * PACK : stop * PACK],
-            )
+        def relu_far(t):
+            far_rise[t] = keep.tile([P, PAIRS - KEPT], F32, name=f"far_rise_{t}")
+            relu_beside(far_rise[t][:], far_excess[t][:])
 
-        def multiply_z(b, c, bank, start, stop, width):
-            for m in range(start, stop, width):
-                nc.tensor.matmul_mx(
-                    out=bank[:, m - start : m - start + width],
-                    lhsT=w2_codes[:, b, 2 * c * P : 2 * (c + 1) * P].bitcast(FP4X4),
-                    lhsT_scale=w2_planes[:, b, c * P : (c + 1) * P],
-                    rhs=z_codes[b][:, m : m + width].bitcast(FP8X4),
-                    rhs_scale=z_planes[b][:, m : m + width],
-                    start=(b == 0 and m == start),
-                    stop=(b == 1 and m == stop - width),
-                )
+
+        z_codes = [keep.tile([P, PAIRS], U32, name=f"z_codes_{b}", align_bytes=64) for b in range(2)]
+        z_planes = []
+
+        def quantize_z(b, start, stop, src):
+            nc.vector.quantize_mx(out=z_codes[b][:, start:stop].bitcast(FP8X4), scales=z_planes[b][:, start:stop], in_=src)
+
+        def multiply_z(b, c, bank, first, start, stop, opens, closes):
+            nc.tensor.matmul_mx(
+                out=bank[:, start - first : stop - first],
+                lhsT=w2_codes[:, b, 2 * c * P : 2 * (c + 1) * P].bitcast(FP4X4),
+                lhsT_scale=w2_planes[:, b, c * P : (c + 1) * P],
+                rhs=z_codes[b][:, start:stop].bitcast(FP8X4),
+                rhs_scale=z_planes[b][:, start:stop],
+                start=opens,
+                stop=closes,
+            )
 
         round_near(1)
         make_h(0, 0, f"w1_raw_1_{P}")
@@ -302,94 +323,155 @@ def tile_list_passage_document_coarsening_kernel(
         quantize_near(2, "near_plane_2")
         first_excess = laid.tile([P, 1, PAIRS], F32, name="first_excess", offset=FIRST_EXCESS_AT)
         pick_near(0, first_excess[:, 0, :], 1)
+        relu_near(0, first_excess[:, 0, :])
         make_h(0, 1)
         round_near(3)
         quantize_near(3, "near_plane_3")
         later_excess = laid.tile([P, PACK - 1, PAIRS], F32, name="later_excess", offset=LATER_EXCESS_AT)
         pick_near(1, later_excess[:, 0, :], 1)
+        relu_near(1, later_excess[:, 0, :])
         make_h(0, 2)
         pick_near(2, later_excess[:, 1, :], 2)
+        relu_near(2, later_excess[:, 1, :])
         round_far(0)
         quantize_far(0)
         make_h(0, 3)
         pick_near(3, later_excess[:, 2, :], 2)
         round_far(1)
+        relu_near(3, later_excess[:, 2, :], f"w1_raw_1_{K_PASS}")
         quantize_far(1)
         make_h(1, 0)
         make_h(1, 1)
-        far_first = keep.tile([P, PACK, PAIRS], F32, name="far_first")
-        pick_far(0)
-        rise = {}
-
-        def relu_near(half, tag):
-            rise[half] = keep.tile([P, PACK, 2 * P], F32, name=f"rise_{half}", tag=tag, align_bytes=64)
-            two_blocks = slice(2 * half * P, 2 * (half + 1) * P)
-            for dst, src in ((rise[half][:, 0:1, :], first_excess), (rise[half][:, 1:PACK, :], later_excess)):
-                if half == 0:
-                    nc.scalar.activation(dst, src[:, :, two_blocks], ACT.Relu)
-                else:
-                    nc.gpsimd.tensor_scalar(dst, src[:, :, two_blocks], F32_MAX, 0.0, ALU.min, ALU.max)
-
-        relu_near(0, "far_codes_0")
-        make_h(1, 2)
-        make_h(1, 3)
-        relu_near(1, "far_codes_1")
-
-        def turn(src, j, bank, opens):
-            for t in range(PACK):
-                nc.tensor.matmul(
-                    bank[:, t * P : (t + 1) * P],
-                    lhsT=src[:, t, j * P : (j + 1) * P],
-                    rhs=identity[:],
-                    is_transpose=True,
-                    start=(opens and t == 0),
-                    stop=(not opens and t == PACK - 1),
-                )
-
-        turn_banks = [psum.tile([P, K_PASS], F32, name=f"z_turned_bank_{j}", tag=f"bank_{j}") for j in range(PAIRS // P)]
+        turn_banks = [psum.tile([P, K_PASS], F32, name=f"z_turned_bank_{j}", tag=f"bank_{2 + j}") for j in range(PAIRS // P)]
+        turn_near(0, near_first[:, 0, :], True, False)
+        turn_near(0, near_rise[0][:], False, False)
+        turn_near(1, near_first[:, 1, :], False, False)
+        for t in range(2, PACK):
+            turn_near(t, near_first[:, t, :], False, False)
+            turn_near(t - 1, near_rise[t - 1][:], False, False)
+        for t in range(2):
+            pick_far(t)
+            relu_far(t)
         turned = []
-        for j, bank in enumerate(turn_banks):
-            turn(near_first, j, bank, True)
-            turn(rise[j // 2], j % 2, bank, False)
-            tile = keep.tile([P, K_PASS], BF16, name=f"z_turned_{j}", tag=f"z_turned_{j}", align_bytes=64)
+
+        def round_turned(j):
+            if j == PACK - 1:
+                tile = laid.tile([P, K_PASS], BF16, name=f"z_turned_{j}", offset=LATE_AT, align_bytes=64)
+            else:
+                tile = keep.tile([P, K_PASS], BF16, name=f"z_turned_{j}", align_bytes=64)
             nc.scalar.copy(
                 tile[:].rearrange("m (u p e) -> m u p e", u=2, e=2),
-                bank[:].rearrange("m (p u e) -> m u p e", u=2, e=2),
+                turn_banks[j][:].rearrange("m (p u e) -> m u p e", u=2, e=2),
             )
             turned.append(tile)
-        z_bf16[0] = keep.tile([P, PAIRS * PACK], BF16, name="z_bf16_0", align_bytes=64)
-        for half in range(2):
-            bank = psum.tile([P, 2, 2, P], F32, name=f"z_back_bank_{half}", tag="bank_4")
+
+        def weave(dst, bank, blocks):
+            nc.scalar.copy(
+                dst.bitcast(F32).rearrange("p (j m u) -> p j m u", j=blocks, u=2),
+                bank[:].rearrange("p (j u m) -> p j m u", j=blocks, u=2),
+            )
+
+        def finish_near(half):
+            bank = psum.tile([P, K_PASS], F32, name=f"z_back_bank_{half}", tag=f"bank_{2 + 2 * half}")
             for block in range(2):
                 words = turned[2 * half + block][:].bitcast(F32)
                 for u in range(2):
-                    nc.tensor.transpose(bank[:, block, u, :], words[:, u * P : (u + 1) * P], identity[:])
-            z_words = z_bf16[0][:, half * 2 * K_PASS : (half + 1) * 2 * K_PASS].bitcast(F32)
-            nc.scalar.copy(z_words.rearrange("p (j m u) -> p j m u", j=2, u=2), bank[:].rearrange("p j u m -> p j m u"))
-        for t in range(1, PACK):
-            pick_far(t)
-        quantize_z(0, 0, PAIRS // 2)
-        quantize_z(0, PAIRS // 2, PAIRS)
-        z_bf16[1] = keep.tile([P, PAIRS * PACK], BF16, name="z_bf16_1", tag="z_turned_3", align_bytes=64)
+                    place = 2 * block + u
+                    nc.tensor.transpose(bank[:, place * P : (place + 1) * P], words[:, u * P : (u + 1) * P], identity[:])
+            return bank
 
+        make_h(1, 2)
+        turn_near(PACK - 1, near_rise[PACK - 1][:], False, True)
+        round_turned(0)
+        pick_far(2)
+        relu_far(2)
+        make_h(1, 3)
+        pick_far(3)
+        near_z = keep.tile([P, PAIRS * PACK], BF16, name="near_z", align_bytes=64)
+        for j in range(1, PAIRS // P):
+            round_turned(j)
+        near_back = [finish_near(half) for half in range(2)]
+        weave(near_z[:, : 2 * K_PASS], near_back[0], 2)
 
-        y_banks = {}
-        for c, ranges in enumerate(Y_RANGES):
-            for start, stop, n in ranges:
-                y_banks[c, start] = psum.tile([P, stop - start], F32, name=f"y_bank_{c}_{start}", tag=f"bank_{n}")
-                multiply_z(0, c, y_banks[c, start], start, stop, P if (stop - start) % (2 * P) else 2 * P)
-        max_far(0, Z_CUTS[0])
-        max_far(Z_CUTS[0], Z_CUTS[1])
-        quantize_z(1, 0, Z_CUTS[0])
-        max_far(Z_CUTS[1], PAIRS)
-        quantize_z(1, Z_CUTS[0], Z_CUTS[1])
-        quantize_z(1, Z_CUTS[1], PAIRS)
+        word_banks = {}
+
+        def turn_far(t, src, opens, closes):
+            u, e = divmod(t, 2)
+            for block in range(2):
+                place = (2 * block + e) * P
+                add_turned(
+                    word_banks[u][:, place : place + P],
+                    src[:, block * P : (block + 1) * P],
+                    opens and block == 0,
+                    closes and block == 1,
+                )
+
+        def turn_back(u, tile):
+            nc.scalar.copy(
+                tile[:].rearrange("m (b p e) -> m b p e", b=2, e=2), word_banks[u][:].rearrange("m (b e p) -> m b p e", b=2, e=2)
+            )
+            words = tile[:].bitcast(F32)
+            for block in range(2):
+                place = (2 * block + u) * P
+                nc.tensor.transpose(far_back[:, place : place + P], words[:, block * P : (block + 1) * P], identity[:])
+
+        word_banks[0] = psum.tile([P, K_PASS], F32, name="far_turned_bank_0", tag="bank_3")
+        far_back = psum.tile([P, K_PASS], F32, name="far_back_bank", tag="bank_5")
+        turn_far(0, far_first[0], True, False)
+        turn_far(0, far_rise[0], False, False)
+        turn_far(1, far_first[1], False, False)
+        turn_far(1, far_rise[1], False, True)
+        early_turned = keep.tile([P, K_PASS], BF16, name="early_turned", align_bytes=64)
+        turn_back(0, early_turned)
+        word_banks[1] = psum.tile([P, K_PASS], F32, name="far_turned_bank_1", tag="bank_7")
+        turn_far(2, far_first[2], True, False)
+        turn_far(2, far_rise[2], False, False)
+        turn_far(3, far_first[3], False, False)
+        kept_second = keep.tile([P, PACK, KEPT], F32, name="kept_second", tag="far_first_2")
+        for t in range(PACK - 1):
+            pick_kept(kept_second, t, pos2_t)
+        pick_kept(kept_second, PACK - 1, pos2_t, 0, P)
+        pick_kept(kept_second, PACK - 1, pos2_t, P, KEPT)
+
+        def max_kept(dst, start, stop):
+            nc.vector.tensor_tensor(
+                dst[:].rearrange("p (c i t) -> p c t i", i=2, t=PACK),
+                kept_first[:, :, start:stop].rearrange("p t (c i) -> p c t i", i=2),
+                kept_second[:, :, start:stop].rearrange("p t (c i) -> p c t i", i=2),
+                ALU.max,
+            )
+
+        kept_z = [keep.tile([P, K_PASS], BF16, name="kept_z_0", align_bytes=64)]
+        max_kept(kept_z[0], 0, P)
+        far_rise[3] = laid.tile([P, PAIRS - KEPT], F32, name="far_rise_3", offset=LATE_AT, align_bytes=64)
+        nc.scalar.activation(far_rise[3][:], far_excess[3][:], ACT.Relu)
+        weave(near_z[:, 2 * K_PASS :], near_back[1], 2)
+        turn_far(3, far_rise[3], False, True)
+        last_turned = laid.tile([P, K_PASS], BF16, name="last_turned", offset=LAST_TURNED_AT, align_bytes=64)
+        turn_back(1, last_turned)
+        turned_z = keep.tile([P, 2 * K_PASS], BF16, name="turned_z", align_bytes=64)
+        weave(turned_z[:], far_back, 2)
+        z_planes.append(laid.tile([P, PAIRS], U8, name="z_plane_0", offset=LAST_TURNED_AT - 2 * P, align_bytes=64))
+        z_planes.append(laid.tile([P, PAIRS], U8, name="z_plane_1", offset=LAST_TURNED_AT + 2 * P, align_bytes=64))
+        kept_z.append(laid.tile([P, K_PASS], BF16, name="kept_z_1", offset=LAST_TURNED_AT + 6 * P, align_bytes=64))
+        quantize_z(0, 0, KEPT, near_z[:, : 2 * K_PASS])
+        max_kept(kept_z[1], P, KEPT)
+        quantize_z(0, KEPT, PAIRS, near_z[:, 2 * K_PASS :])
+        quantize_z(1, 0, P, kept_z[0][:])
+        quantize_z(1, P, KEPT, kept_z[1][:])
+        quantize_z(1, KEPT, 3 * P, turned_z[:, :K_PASS])
+        quantize_z(1, 3 * P, PAIRS, turned_z[:, K_PASS:])
+
         y = [keep.tile([P, PAIRS], F32, name=f"y_{c}") for c in range(N // P)]
         for c, ranges in enumerate(Y_RANGES):
             copy_out = nc.vector.tensor_copy if c == 1 else nc.scalar.copy
-            for start, stop, n in ranges:
-                multiply_z(1, c, y_banks[c, start], start, stop, P if (stop - start) % (2 * P) else stop - start)
-                copy_out(y[c][:, start:stop], y_banks[c, start][:])
+            for first, end, n in ranges:
+                bank = psum.tile([P, end - first], F32, name=f"y_bank_{c}_{first}", tag=f"bank_{n}")
+                cuts = [first, KEPT, end] if first < KEPT < end else [first, end]
+                for b in range(2):
+                    for start, stop in zip(cuts, cuts[1:]):
+                        multiply_z(b, c, bank, first, start, stop, b == 0 and start == first, b == 1 and stop == end)
+                copy_out(y[c][:, first:end], bank[:])
 
 
         gate = {}

@@ -38,12 +38,11 @@ FIRST_RANGES = [(0, BANK), (BANK, S - 2 * P), (S - 2 * P, S - P), (S - P, S)]
 KEPT = 2 * P
 Y_RANGES = [
     [(0, KEPT, 0), (KEPT, 3 * P, 2), (3 * P, PAIRS, 6)],
-    [(0, 3 * P, 1), (3 * P, PAIRS, 4)],
+    [(0, KEPT, 1), (KEPT, PAIRS, 4)],
     [(0, PAIRS, 3)],
     [(0, PAIRS, 7)],
 ]
 LATE_AT = 16 * KIB
-LAST_TURNED_AT = 17 * KIB
 
 
 def tile_list_passage_document_coarsening_kernel(
@@ -287,7 +286,7 @@ def tile_list_passage_document_coarsening_kernel(
 
         def pick_far(t):
             far_first[t] = keep.tile([P, PAIRS - KEPT], F32, name=f"far_first_{t}", tag=f"far_first_{t}")
-            far_excess[t] = keep.tile([P, PAIRS - KEPT], F32, name=f"far_excess_{t}")
+            far_excess[t] = keep.tile([P, PAIRS - KEPT], F32, name=f"far_excess_{t}", tag=f"far_excess_{t}")
             nc.vector.tensor_copy(far_first[t][:], h[1, t][:].indirect(entries_of(pos1_t, KEPT, PAIRS)))
             pick_kept(kept_first, t, pos1_t)
             nc.vector.tensor_tensor(
@@ -391,7 +390,12 @@ def tile_list_passage_document_coarsening_kernel(
         for j in range(1, PAIRS // P):
             round_turned(j)
         near_back = [finish_near(half) for half in range(2)]
-        weave(near_z[:, : 2 * K_PASS], near_back[0], 2)
+        z_planes.extend(keep.tile([P, PAIRS], U8, name=f"z_plane_{b}", align_bytes=64) for b in range(2))
+        for half in range(2):
+            weave(near_z[:, half * 2 * K_PASS : (half + 1) * 2 * K_PASS], near_back[half], 2)
+            quantize_z(0, half * 2 * P, (half + 1) * 2 * P, near_z[:, half * 2 * K_PASS : (half + 1) * 2 * K_PASS])
+        far_rise[3] = laid.tile([P, PAIRS - KEPT], F32, name="far_rise_3", offset=LATE_AT, align_bytes=64)
+        nc.scalar.activation(far_rise[3][:], far_excess[3][:], ACT.Relu)
 
         word_banks = {}
 
@@ -427,7 +431,12 @@ def tile_list_passage_document_coarsening_kernel(
         turn_far(2, far_first[2], True, False)
         turn_far(2, far_rise[2], False, False)
         turn_far(3, far_first[3], False, False)
-        kept_second = keep.tile([P, PACK, KEPT], F32, name="kept_second", tag="far_first_2")
+        turn_far(3, far_rise[3], False, True)
+        last_turned = keep.tile([P, K_PASS], BF16, name="last_turned", align_bytes=64)
+        turn_back(1, last_turned)
+        turned_z = keep.tile([P, 2 * K_PASS], BF16, name="turned_z", align_bytes=64)
+        weave(turned_z[:], far_back, 2)
+        kept_second = keep.tile([P, PACK, KEPT], F32, name="kept_second", tag="far_excess_3")
         for t in range(PACK - 1):
             pick_kept(kept_second, t, pos2_t)
         pick_kept(kept_second, PACK - 1, pos2_t, 0, P)
@@ -441,31 +450,18 @@ def tile_list_passage_document_coarsening_kernel(
                 ALU.max,
             )
 
-        kept_z = [keep.tile([P, K_PASS], BF16, name="kept_z_0", align_bytes=64)]
-        max_kept(kept_z[0], 0, P)
-        far_rise[3] = laid.tile([P, PAIRS - KEPT], F32, name="far_rise_3", offset=LATE_AT, align_bytes=64)
-        nc.scalar.activation(far_rise[3][:], far_excess[3][:], ACT.Relu)
-        weave(near_z[:, 2 * K_PASS :], near_back[1], 2)
-        turn_far(3, far_rise[3], False, True)
-        last_turned = laid.tile([P, K_PASS], BF16, name="last_turned", offset=LAST_TURNED_AT, align_bytes=64)
-        turn_back(1, last_turned)
-        turned_z = keep.tile([P, 2 * K_PASS], BF16, name="turned_z", align_bytes=64)
-        weave(turned_z[:], far_back, 2)
-        z_planes.append(laid.tile([P, PAIRS], U8, name="z_plane_0", offset=LAST_TURNED_AT - 2 * P, align_bytes=64))
-        z_planes.append(laid.tile([P, PAIRS], U8, name="z_plane_1", offset=LAST_TURNED_AT + 2 * P, align_bytes=64))
-        kept_z.append(laid.tile([P, K_PASS], BF16, name="kept_z_1", offset=LAST_TURNED_AT + 6 * P, align_bytes=64))
-        quantize_z(0, 0, KEPT, near_z[:, : 2 * K_PASS])
-        max_kept(kept_z[1], P, KEPT)
-        quantize_z(0, KEPT, PAIRS, near_z[:, 2 * K_PASS :])
-        quantize_z(1, 0, P, kept_z[0][:])
-        quantize_z(1, P, KEPT, kept_z[1][:])
+        kept_z = [keep.tile([P, K_PASS], BF16, name=f"kept_z_{n}", align_bytes=64) for n in range(2)]
+        for n in range(2):
+            max_kept(kept_z[n], n * P, (n + 1) * P)
+        for n in range(2):
+            quantize_z(1, n * P, (n + 1) * P, kept_z[n][:])
         quantize_z(1, KEPT, 3 * P, turned_z[:, :K_PASS])
         quantize_z(1, 3 * P, PAIRS, turned_z[:, K_PASS:])
 
         y = [keep.tile([P, PAIRS], F32, name=f"y_{c}") for c in range(N // P)]
         for c, ranges in enumerate(Y_RANGES):
-            copy_out = nc.vector.tensor_copy if c == 1 else nc.scalar.copy
             for first, end, n in ranges:
+                copy_out = nc.vector.tensor_copy if (c, first) == (1, 0) else nc.scalar.copy
                 bank = psum.tile([P, end - first], F32, name=f"y_bank_{c}_{first}", tag=f"bank_{n}")
                 cuts = [first, KEPT, end] if first < KEPT < end else [first, end]
                 for b in range(2):

@@ -37,12 +37,11 @@ HALVES = [(0, BANK), (BANK, S)]
 FIRST_RANGES = [(0, BANK), (BANK, S - 2 * P), (S - 2 * P, S - P), (S - P, S)]
 KEPT = 2 * P
 Y_RANGES = [
-    [(0, KEPT, 0), (KEPT, 3 * P, 2), (3 * P, PAIRS, 6)],
-    [(0, KEPT, 1), (KEPT, PAIRS, 4)],
-    [(0, PAIRS, 3)],
-    [(0, PAIRS, 7)],
+    [(0, KEPT, 2), (KEPT, 3 * P, 1), (3 * P, PAIRS, 6)],
+    [(0, KEPT, 5), (KEPT, PAIRS, 3)],
+    [(0, KEPT, 0), (KEPT, PAIRS, 7)],
+    [(0, PAIRS, 4)],
 ]
-LATE_AT = 16 * KIB
 
 
 def tile_list_passage_document_coarsening_kernel(
@@ -152,7 +151,7 @@ def tile_list_passage_document_coarsening_kernel(
             nc.vector.quantize_mx(out=near_codes[t][:].bitcast(FP8X4), scales=near_planes[t][:], in_=near_bf16[t][:])
 
         def round_far(u):
-            far_bf16[u] = keep.tile([P, 4 * K_PASS], BF16, name=f"far_bf16_{u}", align_bytes=64)
+            far_bf16[u] = keep.tile([P, 4 * K_PASS], BF16, name=f"far_bf16_{u}", tag=f"far_bf16_{u}", align_bytes=64)
             for a in range(2):
                 nc.scalar.copy(
                     far_bf16[u][:, 2 * a * K_PASS : 2 * (a + 1) * K_PASS].rearrange("p (t m j) -> p m j t", t=2, j=PACK),
@@ -279,13 +278,14 @@ def tile_list_passage_document_coarsening_kernel(
         far_first = {}
         far_excess = {}
         far_rise = {}
-        kept_first = keep.tile([P, PACK, KEPT], F32, name="kept_first")
+        slots = keep.tile([P, (PACK + 1) * KEPT], F32, name="slots", align_bytes=64)
+        kept_first = slots[:, : PACK * KEPT].rearrange("p (t c) -> p t c", t=PACK)
 
         def pick_kept(dst, t, list_tile, start=0, stop=KEPT):
             nc.vector.tensor_copy(dst[:, t, start:stop], h[1, t][:].indirect(entries_of(list_tile, start, stop)))
 
         def pick_far(t):
-            far_first[t] = keep.tile([P, PAIRS - KEPT], F32, name=f"far_first_{t}", tag=f"far_first_{t}")
+            far_first[t] = keep.tile([P, PAIRS - KEPT], F32, name=f"far_first_{t}")
             far_excess[t] = keep.tile([P, PAIRS - KEPT], F32, name=f"far_excess_{t}", tag=f"far_excess_{t}")
             nc.vector.tensor_copy(far_first[t][:], h[1, t][:].indirect(entries_of(pos1_t, KEPT, PAIRS)))
             pick_kept(kept_first, t, pos1_t)
@@ -331,14 +331,14 @@ def tile_list_passage_document_coarsening_kernel(
         relu_near(1, later_excess[:, 0, :])
         make_h(0, 2)
         pick_near(2, later_excess[:, 1, :], 2)
-        relu_near(2, later_excess[:, 1, :])
         round_far(0)
         quantize_far(0)
+        relu_near(2, later_excess[:, 1, :], "far_bf16_0")
         make_h(0, 3)
         pick_near(3, later_excess[:, 2, :], 2)
         round_far(1)
-        relu_near(3, later_excess[:, 2, :], f"w1_raw_1_{K_PASS}")
         quantize_far(1)
+        relu_near(3, later_excess[:, 2, :], "far_bf16_1")
         make_h(1, 0)
         make_h(1, 1)
         turn_banks = [psum.tile([P, K_PASS], F32, name=f"z_turned_bank_{j}", tag=f"bank_{2 + j}") for j in range(PAIRS // P)]
@@ -354,10 +354,7 @@ def tile_list_passage_document_coarsening_kernel(
         turned = []
 
         def round_turned(j):
-            if j == PACK - 1:
-                tile = laid.tile([P, K_PASS], BF16, name=f"z_turned_{j}", offset=LATE_AT, align_bytes=64)
-            else:
-                tile = keep.tile([P, K_PASS], BF16, name=f"z_turned_{j}", align_bytes=64)
+            tile = keep.tile([P, K_PASS], BF16, name=f"z_turned_{j}", tag=f"z_turned_{j}", align_bytes=64)
             nc.scalar.copy(
                 tile[:].rearrange("m (u p e) -> m u p e", u=2, e=2),
                 turn_banks[j][:].rearrange("m (p u e) -> m u p e", u=2, e=2),
@@ -379,66 +376,85 @@ def tile_list_passage_document_coarsening_kernel(
                     nc.tensor.transpose(bank[:, place * P : (place + 1) * P], words[:, u * P : (u + 1) * P], identity[:])
             return bank
 
+        word_banks = {}
+
+        def turn_far(t, blocks, opens, closes):
+            u, e = divmod(t, 2)
+            for block, src in enumerate(blocks):
+                if u == 0:
+                    place = (2 * block + e) * P
+                    add_turned(word_banks[0][:, place : place + P], src, opens and block == 0, closes and block == 1)
+                else:
+                    add_turned(word_banks[1][block][:, e * P : (e + 1) * P], src, opens, closes)
+
+        def blocks_of(tile):
+            return [tile[:, block * P : (block + 1) * P] for block in range(2)]
+
+        def turn_back(u, tile, bank, blocks):
+            count = len(blocks)
+            nc.scalar.copy(
+                tile[:].rearrange("m (b p e) -> m b p e", b=count, e=2), bank[:].rearrange("m (b e p) -> m b p e", b=count, e=2)
+            )
+            words = tile[:].bitcast(F32)
+            for place, block in enumerate(blocks):
+                nc.tensor.transpose(far_back[block][:, u * P : (u + 1) * P], words[:, place * P : (place + 1) * P], identity[:])
+
+        z_planes.extend(keep.tile([P, PAIRS], U8, name=f"z_plane_{b}", align_bytes=64) for b in range(2))
         make_h(1, 2)
         turn_near(PACK - 1, near_rise[PACK - 1][:], False, True)
         round_turned(0)
-        pick_far(2)
-        relu_far(2)
+        round_turned(1)
         make_h(1, 3)
-        pick_far(3)
-        near_z = keep.tile([P, PAIRS * PACK], BF16, name="near_z", align_bytes=64)
-        for j in range(1, PAIRS // P):
-            round_turned(j)
-        near_back = [finish_near(half) for half in range(2)]
-        z_planes.extend(keep.tile([P, PAIRS], U8, name=f"z_plane_{b}", align_bytes=64) for b in range(2))
-        for half in range(2):
-            weave(near_z[:, half * 2 * K_PASS : (half + 1) * 2 * K_PASS], near_back[half], 2)
-            quantize_z(0, half * 2 * P, (half + 1) * 2 * P, near_z[:, half * 2 * K_PASS : (half + 1) * 2 * K_PASS])
-        far_rise[3] = laid.tile([P, PAIRS - KEPT], F32, name="far_rise_3", offset=LATE_AT, align_bytes=64)
-        nc.scalar.activation(far_rise[3][:], far_excess[3][:], ACT.Relu)
+        pick_far(2)
+        staged = slots[:, (PACK - 1) * KEPT :].bitcast(BF16)
+        weave(staged, finish_near(0), 2)
+        far_first[3] = keep.tile([P, PAIRS - KEPT], F32, name="far_first_3", tag="far_first_3", align_bytes=64)
+        nc.vector.tensor_copy(far_first[3][:], h[1, 3][:].indirect(entries_of(pos1_t, KEPT, PAIRS)))
+        for block in (1, 0):
+            quantize_z(0, block * P, (block + 1) * P, staged[:, block * K_PASS : (block + 1) * K_PASS])
+        last_excess = slots[:, PACK * KEPT :]
+        nc.vector.tensor_tensor(last_excess, h[1, 3][:].indirect(entries_of(pos2_t, KEPT, PAIRS)), far_first[3][:], ALU.subtract)
+        far_rise[3] = keep.tile([P, PAIRS - KEPT], F32, name="far_rise_3")
+        relu_beside(far_rise[3][:], last_excess)
+        pick_kept(kept_first, PACK - 1, pos1_t)
 
-        word_banks = {}
-
-        def turn_far(t, src, opens, closes):
-            u, e = divmod(t, 2)
-            for block in range(2):
-                place = (2 * block + e) * P
-                add_turned(
-                    word_banks[u][:, place : place + P],
-                    src[:, block * P : (block + 1) * P],
-                    opens and block == 0,
-                    closes and block == 1,
-                )
-
-        def turn_back(u, tile):
-            nc.scalar.copy(
-                tile[:].rearrange("m (b p e) -> m b p e", b=2, e=2), word_banks[u][:].rearrange("m (b e p) -> m b p e", b=2, e=2)
-            )
-            words = tile[:].bitcast(F32)
-            for block in range(2):
-                place = (2 * block + u) * P
-                nc.tensor.transpose(far_back[:, place : place + P], words[:, block * P : (block + 1) * P], identity[:])
-
-        word_banks[0] = psum.tile([P, K_PASS], F32, name="far_turned_bank_0", tag="bank_3")
-        far_back = psum.tile([P, K_PASS], F32, name="far_back_bank", tag="bank_5")
-        turn_far(0, far_first[0], True, False)
-        turn_far(0, far_rise[0], False, False)
-        turn_far(1, far_first[1], False, False)
-        turn_far(1, far_rise[1], False, True)
+        word_banks[0] = psum.tile([P, K_PASS], F32, name="far_turned_bank_0", tag="bank_0")
+        word_banks[1] = [
+            psum.tile([P, 2 * P], F32, name=f"far_turned_bank_1_{block}", tag=f"bank_{1 + 2 * block}") for block in range(2)
+        ]
+        far_back = [psum.tile([P, 2 * P], F32, name=f"far_back_bank_{block}", tag=f"bank_{6 + block}") for block in range(2)]
+        turn_far(0, blocks_of(far_first[0]), True, False)
+        turn_far(0, blocks_of(far_rise[0]), False, False)
+        turn_far(1, blocks_of(far_first[1]), False, False)
+        turn_far(1, blocks_of(far_rise[1]), False, True)
+        round_turned(2)
+        round_turned(3)
+        near_back = finish_near(1)
+        turn_far(2, blocks_of(far_first[2]), True, False)
+        turn_far(3, blocks_of(far_first[3]), False, False)
         early_turned = keep.tile([P, K_PASS], BF16, name="early_turned", align_bytes=64)
-        turn_back(0, early_turned)
-        word_banks[1] = psum.tile([P, K_PASS], F32, name="far_turned_bank_1", tag="bank_7")
-        turn_far(2, far_first[2], True, False)
-        turn_far(2, far_rise[2], False, False)
-        turn_far(3, far_first[3], False, False)
-        turn_far(3, far_rise[3], False, True)
-        last_turned = keep.tile([P, K_PASS], BF16, name="last_turned", align_bytes=64)
-        turn_back(1, last_turned)
+        turn_back(0, early_turned, word_banks[0], [0, 1])
+        late_slots = keep.tile([P, PACK * KEPT], F32, name="late_slots", tag="far_first_3", align_bytes=64)
+        kept_second = late_slots[:].rearrange("p (t c) -> p t c", t=PACK)
+        near_z = late_slots[:, 2 * KEPT :].bitcast(BF16)
+        weave(near_z, near_back, 2)
+        far_rise[2] = keep.tile([P, PAIRS - KEPT], F32, name="far_rise_2")
+        nc.scalar.activation(far_rise[2][:], far_excess[2][:], ACT.Relu)
+        turn_far(2, blocks_of(far_rise[2]), False, False)
+        turn_far(3, blocks_of(far_rise[3]), False, True)
+        for block in range(2):
+            last_turned = keep.tile([P, 2 * P], BF16, name=f"last_turned_{block}", align_bytes=64)
+            turn_back(1, last_turned, word_banks[1][block], [block])
         turned_z = keep.tile([P, 2 * K_PASS], BF16, name="turned_z", align_bytes=64)
-        weave(turned_z[:], far_back, 2)
-        kept_second = keep.tile([P, PACK, KEPT], F32, name="kept_second", tag="far_excess_3")
-        for t in range(PACK - 1):
+        for block in range(2):
+            weave(turned_z[:, block * K_PASS : (block + 1) * K_PASS], far_back[block], 1)
+
+        for t in range(2):
             pick_kept(kept_second, t, pos2_t)
+        for block in range(2):
+            start = KEPT + block * P
+            quantize_z(0, start, start + P, near_z[:, block * K_PASS : (block + 1) * K_PASS])
+        pick_kept(kept_second, 2, pos2_t)
         pick_kept(kept_second, PACK - 1, pos2_t, 0, P)
         pick_kept(kept_second, PACK - 1, pos2_t, P, KEPT)
 
@@ -464,8 +480,8 @@ def tile_list_passage_document_coarsening_kernel(
                 copy_out = nc.vector.tensor_copy if (c, first) == (1, 0) else nc.scalar.copy
                 bank = psum.tile([P, end - first], F32, name=f"y_bank_{c}_{first}", tag=f"bank_{n}")
                 cuts = [first, KEPT, end] if first < KEPT < end else [first, end]
-                for b in range(2):
-                    for start, stop in zip(cuts, cuts[1:]):
+                for start, stop in zip(cuts, cuts[1:]):
+                    for b in range(2):
                         multiply_z(b, c, bank, first, start, stop, b == 0 and start == first, b == 1 and stop == end)
                 copy_out(y[c][:, first:end], bank[:])
 

@@ -37,11 +37,15 @@ HALVES = [(0, BANK), (BANK, S)]
 FIRST_RANGES = [(0, BANK), (BANK, S - 2 * P), (S - 2 * P, S - P), (S - P, S)]
 KEPT = 2 * P
 Y_RANGES = [
-    [(0, KEPT, 2), (KEPT, 3 * P, 1), (3 * P, PAIRS, 6)],
-    [(0, KEPT, 5), (KEPT, PAIRS, 3)],
-    [(0, KEPT, 0), (KEPT, PAIRS, 7)],
-    [(0, PAIRS, 4)],
+    [(0, KEPT, 2), (KEPT, 3 * P, 4), (3 * P, PAIRS, 0)],
+    [(0, KEPT, 7), (KEPT, PAIRS, 5)],
+    [(0, KEPT, 6), (KEPT, PAIRS, 1)],
+    [(0, PAIRS, 3)],
 ]
+FAR_BANKS = [0, 4, 6, 0]
+LAST_STAGE_AT = 20 * KIB
+LAST_RISE_AT = LAST_STAGE_AT - 3 * KIB // 2
+TURNED_AT = [LAST_RISE_AT + 2 * KIB, LAST_RISE_AT + 4 * KIB]
 
 
 def tile_list_passage_document_coarsening_kernel(
@@ -130,6 +134,7 @@ def tile_list_passage_document_coarsening_kernel(
         near_bf16 = {}
         near_codes = {}
         near_planes = {}
+        stages = {}
         far_bf16 = {}
         far_codes = {}
         far_planes = {}
@@ -150,18 +155,31 @@ def tile_list_passage_document_coarsening_kernel(
             near_planes[t] = keep.tile([P, 2 * P], U8, name=f"near_plane_{t}", tag=plane_tag, align_bytes=64)
             nc.vector.quantize_mx(out=near_codes[t][:].bitcast(FP8X4), scales=near_planes[t][:], in_=near_bf16[t][:])
 
-        def round_far(u):
-            far_bf16[u] = keep.tile([P, 4 * K_PASS], BF16, name=f"far_bf16_{u}", tag=f"far_bf16_{u}", align_bytes=64)
-            for a in range(2):
-                nc.scalar.copy(
-                    far_bf16[u][:, 2 * a * K_PASS : 2 * (a + 1) * K_PASS].rearrange("p (t m j) -> p m j t", t=2, j=PACK),
-                    far_raw[a][:].rearrange("p j (m t) -> p m j t", t=PACK)[:, :, :, 2 * u : 2 * u + 2],
+        def round_far(u, a):
+            name = f"far_stage_{u}_{a}"
+            if (u, a) == (1, 1):
+                stages[u, a] = laid.tile([P, 2 * PAIRS], F32, name=name, offset=LAST_STAGE_AT, align_bytes=64)
+            else:
+                stages[u, a] = keep.tile([P, 2 * PAIRS], F32, name=name, align_bytes=64)
+            far_bf16[u, a] = stages[u, a][:, PAIRS // 2 : 3 * PAIRS // 2].bitcast(BF16)
+            nc.scalar.copy(
+                far_bf16[u, a].rearrange("p (t m j) -> p m j t", t=2, j=PACK),
+                far_raw[a][:].rearrange("p j (m t) -> p m j t", t=PACK)[:, :, :, 2 * u : 2 * u + 2],
+            )
+
+        def quantize_far(u, a, parts):
+            width = 2 * P // parts
+            for n in range(parts):
+                cols = slice(2 * a * P + n * width, 2 * a * P + (n + 1) * width)
+                nc.vector.quantize_mx(
+                    out=far_codes[u][:, cols].bitcast(FP8X4),
+                    scales=far_planes[u][:, cols],
+                    in_=far_bf16[u, a][:, n * width * PACK : (n + 1) * width * PACK],
                 )
 
-        def quantize_far(u):
-            far_codes[u] = keep.tile([P, 4 * P], U32, name=f"far_codes_{u}", tag=f"far_codes_{u}", align_bytes=64)
+        for u in range(2):
+            far_codes[u] = keep.tile([P, 4 * P], U32, name=f"far_codes_{u}", align_bytes=64)
             far_planes[u] = keep.tile([P, 4 * P], U8, name=f"far_plane_{u}", align_bytes=64)
-            nc.vector.quantize_mx(out=far_codes[u][:].bitcast(FP8X4), scales=far_planes[u][:], in_=far_bf16[u][:])
 
 
         v_scales = keep.tile([P, S], U8, name="v_scales", align_bytes=64)
@@ -206,7 +224,7 @@ def tile_list_passage_document_coarsening_kernel(
                 codes, planes = far_codes[u], far_planes[u]
                 first_col = [(2 * a + e) * P for a in range(2)]
             ranges = FIRST_RANGES if (b, t) == (0, 0) else HALVES
-            first_bank = 2 * t if b == 0 else 6 * (t % 2)
+            first_bank = 2 * t if b == 0 else FAR_BANKS[t]
             bank_numbers = [first_bank, first_bank + 1, 7, 6]
             banks = [
                 psum.tile([P, stop - start], F32, name=f"h_bank_{b}_{t}_{n}", tag=f"bank_{bank_numbers[n]}")
@@ -244,19 +262,13 @@ def tile_list_passage_document_coarsening_kernel(
                 copy_out = nc.scalar.copy if n < len(HALVES) else nc.vector.tensor_copy
                 copy_out(h[b, t][:, start:stop], bank[:])
 
-        near_first = keep.tile([P, PACK, PAIRS], F32, name="near_first")
+        near_first = {t: keep.tile([P, PAIRS], F32, name=f"near_first_{t}")[:] for t in range(PACK - 1)}
 
-        def pick_near(t, excess, parts):
-            pieces = [(n * PAIRS // parts, (n + 1) * PAIRS // parts) for n in range(parts)]
-            for start, stop in pieces:
-                nc.vector.tensor_copy(near_first[:, t, start:stop], h[0, t][:].indirect(entries_of(pos1_t, start, stop)))
-            for start, stop in pieces:
-                nc.vector.tensor_tensor(
-                    excess[:, start:stop],
-                    h[0, t][:].indirect(entries_of(pos2_t, start, stop)),
-                    near_first[:, t, start:stop],
-                    ALU.subtract,
-                )
+        def pick_first(t):
+            nc.vector.tensor_copy(near_first[t], h[0, t][:].indirect(pos1_t[:]))
+
+        def pick_excess(t, excess):
+            nc.vector.tensor_tensor(excess, h[0, t][:].indirect(pos2_t[:]), near_first[t], ALU.subtract)
 
         def relu_beside(dst, src):
             nc.gpsimd.tensor_scalar(dst, src, F32_MAX, 0.0, ALU.min, ALU.max)
@@ -266,27 +278,37 @@ def tile_list_passage_document_coarsening_kernel(
 
         near_rise = {}
 
-        def relu_near(t, excess, tag=None):
-            name = f"near_rise_{t}"
-            near_rise[t] = keep.tile([P, PAIRS], F32, name=name, tag=tag or name, align_bytes=64)
-            relu_beside(near_rise[t][:], excess)
+        def relu_near(t, excess, dst=None):
+            near_rise[t] = keep.tile([P, PAIRS], F32, name=f"near_rise_{t}")[:] if dst is None else dst
+            relu_beside(near_rise[t], excess)
 
-        def turn_near(t, src, opens, closes):
-            for j, bank in enumerate(turn_banks):
-                add_turned(bank[:, t * P : (t + 1) * P], src[:, j * P : (j + 1) * P], opens, closes)
+        def turn_near(pair, first_bank):
+            banks = [
+                psum.tile([P, K_PASS], F32, name=f"near_turned_bank_{pair}_{n}", tag=f"bank_{first_bank + n}") for n in range(2)
+            ]
+            for e in range(2):
+                t = 2 * pair + e
+                for term, src in enumerate((near_first[t], near_rise[t])):
+                    for j in range(PAIRS // P):
+                        n, block = divmod(j, 2)
+                        place = (2 * block + e) * P
+                        ends = (e, term, block)
+                        add_turned(
+                            banks[n][:, place : place + P], src[:, j * P : (j + 1) * P], ends == (0, 0, 0), ends == (1, 1, 1)
+                        )
+            return banks
 
         far_first = {}
         far_excess = {}
         far_rise = {}
-        slots = keep.tile([P, (PACK + 1) * KEPT], F32, name="slots", align_bytes=64)
-        kept_first = slots[:, : PACK * KEPT].rearrange("p (t c) -> p t c", t=PACK)
+        kept_first = keep.tile([P, PACK, KEPT], F32, name="kept_first")
 
         def pick_kept(dst, t, list_tile, start=0, stop=KEPT):
             nc.vector.tensor_copy(dst[:, t, start:stop], h[1, t][:].indirect(entries_of(list_tile, start, stop)))
 
         def pick_far(t):
             far_first[t] = keep.tile([P, PAIRS - KEPT], F32, name=f"far_first_{t}")
-            far_excess[t] = keep.tile([P, PAIRS - KEPT], F32, name=f"far_excess_{t}", tag=f"far_excess_{t}")
+            far_excess[t] = keep.tile([P, PAIRS - KEPT], F32, name=f"far_excess_{t}", tag=f"far_excess_{t}", align_bytes=64)
             nc.vector.tensor_copy(far_first[t][:], h[1, t][:].indirect(entries_of(pos1_t, KEPT, PAIRS)))
             pick_kept(kept_first, t, pos1_t)
             nc.vector.tensor_tensor(
@@ -320,46 +342,49 @@ def tile_list_passage_document_coarsening_kernel(
         quantize_near(1, "near_plane_0")
         round_near(2)
         quantize_near(2, "near_plane_2")
-        first_excess = laid.tile([P, 1, PAIRS], F32, name="first_excess", offset=FIRST_EXCESS_AT)
-        pick_near(0, first_excess[:, 0, :], 1)
-        relu_near(0, first_excess[:, 0, :])
+        first_excess = laid.tile([P, PAIRS], F32, name="first_excess", offset=FIRST_EXCESS_AT)
+        pick_first(0)
+        pick_excess(0, first_excess[:])
+        relu_near(0, first_excess[:])
         make_h(0, 1)
         round_near(3)
         quantize_near(3, "near_plane_3")
-        later_excess = laid.tile([P, PACK - 1, PAIRS], F32, name="later_excess", offset=LATER_EXCESS_AT)
-        pick_near(1, later_excess[:, 0, :], 1)
-        relu_near(1, later_excess[:, 0, :])
+        later_excess = laid.tile([P, PAIRS], F32, name="later_excess", offset=LATER_EXCESS_AT)
+        pick_first(1)
+        pick_excess(1, later_excess[:])
+        relu_near(1, later_excess[:])
         make_h(0, 2)
-        pick_near(2, later_excess[:, 1, :], 2)
-        round_far(0)
-        quantize_far(0)
-        relu_near(2, later_excess[:, 1, :], "far_bf16_0")
+        round_far(0, 0)
+        pick_first(2)
+        quantize_far(0, 0, 2)
+        pick_excess(2, stages[0, 0][:, :PAIRS])
+        round_far(0, 1)
+        quantize_far(0, 1, 2)
+        relu_near(2, stages[0, 0][:, :PAIRS], stages[0, 1][:, PAIRS:])
         make_h(0, 3)
-        pick_near(3, later_excess[:, 2, :], 2)
-        round_far(1)
-        quantize_far(1)
-        relu_near(3, later_excess[:, 2, :], "far_bf16_1")
+        round_far(1, 0)
+        near_first[3] = stages[0, 1][:, :PAIRS]
+        pick_first(3)
+        quantize_far(1, 0, 1)
+        last_near_excess = keep.tile([P, PAIRS], F32, name="last_near_excess", tag=f"w1_raw_0_{K_PASS}", align_bytes=64)
+        pick_excess(3, last_near_excess[:])
+        round_far(1, 1)
+        quantize_far(1, 1, 1)
+        last_rise = laid.tile([P, PAIRS], F32, name="near_rise_3", offset=LAST_RISE_AT, align_bytes=64)
+        relu_near(3, last_near_excess[:], last_rise[:])
         make_h(1, 0)
         make_h(1, 1)
-        turn_banks = [psum.tile([P, K_PASS], F32, name=f"z_turned_bank_{j}", tag=f"bank_{2 + j}") for j in range(PAIRS // P)]
-        turn_near(0, near_first[:, 0, :], True, False)
-        turn_near(0, near_rise[0][:], False, False)
-        turn_near(1, near_first[:, 1, :], False, False)
-        for t in range(2, PACK):
-            turn_near(t, near_first[:, t, :], False, False)
-            turn_near(t - 1, near_rise[t - 1][:], False, False)
+        early_banks = turn_near(0, 2)
         for t in range(2):
             pick_far(t)
             relu_far(t)
-        turned = []
+        turned = [laid.tile([P, 2 * K_PASS], BF16, name=f"z_turned_{n}", offset=TURNED_AT[n], align_bytes=64) for n in range(2)]
 
-        def round_turned(j):
-            tile = keep.tile([P, K_PASS], BF16, name=f"z_turned_{j}", tag=f"z_turned_{j}", align_bytes=64)
+        def round_turned(pair, n, bank):
             nc.scalar.copy(
-                tile[:].rearrange("m (u p e) -> m u p e", u=2, e=2),
-                turn_banks[j][:].rearrange("m (p u e) -> m u p e", u=2, e=2),
+                turned[n][:].rearrange("m (j u g p e) -> m g j u p e", j=2, u=2, g=2, e=2)[:, pair],
+                bank[:].rearrange("m (j p u e) -> m j u p e", j=2, u=2, e=2),
             )
-            turned.append(tile)
 
         def weave(dst, bank, blocks):
             nc.scalar.copy(
@@ -368,12 +393,10 @@ def tile_list_passage_document_coarsening_kernel(
             )
 
         def finish_near(half):
-            bank = psum.tile([P, K_PASS], F32, name=f"z_back_bank_{half}", tag=f"bank_{2 + 2 * half}")
-            for block in range(2):
-                words = turned[2 * half + block][:].bitcast(F32)
-                for u in range(2):
-                    place = 2 * block + u
-                    nc.tensor.transpose(bank[:, place * P : (place + 1) * P], words[:, u * P : (u + 1) * P], identity[:])
+            bank = psum.tile([P, K_PASS], F32, name=f"z_back_bank_{half}", tag=f"bank_{2 + half}")
+            words = turned[half][:].bitcast(F32)
+            for place in range(PACK):
+                nc.tensor.transpose(bank[:, place * P : (place + 1) * P], words[:, place * P : (place + 1) * P], identity[:])
             return bank
 
         word_banks = {}
@@ -401,47 +424,31 @@ def tile_list_passage_document_coarsening_kernel(
 
         z_planes.extend(keep.tile([P, PAIRS], U8, name=f"z_plane_{b}", align_bytes=64) for b in range(2))
         make_h(1, 2)
-        turn_near(PACK - 1, near_rise[PACK - 1][:], False, True)
-        round_turned(0)
-        round_turned(1)
         make_h(1, 3)
-        pick_far(2)
-        staged = slots[:, (PACK - 1) * KEPT :].bitcast(BF16)
-        weave(staged, finish_near(0), 2)
-        far_first[3] = keep.tile([P, PAIRS - KEPT], F32, name="far_first_3", tag="far_first_3", align_bytes=64)
-        nc.vector.tensor_copy(far_first[3][:], h[1, 3][:].indirect(entries_of(pos1_t, KEPT, PAIRS)))
-        for block in (1, 0):
-            quantize_z(0, block * P, (block + 1) * P, staged[:, block * K_PASS : (block + 1) * K_PASS])
-        last_excess = slots[:, PACK * KEPT :]
-        nc.vector.tensor_tensor(last_excess, h[1, 3][:].indirect(entries_of(pos2_t, KEPT, PAIRS)), far_first[3][:], ALU.subtract)
-        far_rise[3] = keep.tile([P, PAIRS - KEPT], F32, name="far_rise_3")
-        relu_beside(far_rise[3][:], last_excess)
-        pick_kept(kept_first, PACK - 1, pos1_t)
+        late_banks = turn_near(1, 4)
+        for t in range(2, PACK):
+            pick_far(t)
+            relu_far(t)
+        for pair, banks in enumerate((early_banks, late_banks)):
+            for n, bank in enumerate(banks):
+                round_turned(pair, n, bank)
+        near_back = [finish_near(half) for half in range(2)]
 
-        word_banks[0] = psum.tile([P, K_PASS], F32, name="far_turned_bank_0", tag="bank_0")
+        word_banks[0] = psum.tile([P, K_PASS], F32, name="far_turned_bank_0", tag="bank_6")
         word_banks[1] = [
-            psum.tile([P, 2 * P], F32, name=f"far_turned_bank_1_{block}", tag=f"bank_{1 + 2 * block}") for block in range(2)
+            psum.tile([P, 2 * P], F32, name=f"far_turned_bank_1_{block}", tag=f"bank_{4 + block}") for block in range(2)
         ]
-        far_back = [psum.tile([P, 2 * P], F32, name=f"far_back_bank_{block}", tag=f"bank_{6 + block}") for block in range(2)]
-        turn_far(0, blocks_of(far_first[0]), True, False)
-        turn_far(0, blocks_of(far_rise[0]), False, False)
-        turn_far(1, blocks_of(far_first[1]), False, False)
-        turn_far(1, blocks_of(far_rise[1]), False, True)
-        round_turned(2)
-        round_turned(3)
-        near_back = finish_near(1)
-        turn_far(2, blocks_of(far_first[2]), True, False)
-        turn_far(3, blocks_of(far_first[3]), False, False)
+        far_back = [psum.tile([P, 2 * P], F32, name=f"far_back_bank_{block}", tag=f"bank_{block}") for block in range(2)]
+        for t in range(PACK):
+            turn_far(t, blocks_of(far_first[t]), t % 2 == 0, False)
+            turn_far(t, blocks_of(far_rise[t]), False, t % 2 == 1)
+        late_slots = laid.tile([P, PACK * KEPT], F32, name="late_slots", offset=LAST_RISE_AT, align_bytes=64)
+        kept_second = late_slots[:].rearrange("p (t c) -> p t c", t=PACK)
+        near_z = [late_slots[:, 2 * KEPT :].bitcast(BF16), keep.tile([P, 2 * K_PASS], BF16, name="near_z", align_bytes=64)[:]]
+        for half in range(2):
+            weave(near_z[half], near_back[half], 2)
         early_turned = keep.tile([P, K_PASS], BF16, name="early_turned", align_bytes=64)
         turn_back(0, early_turned, word_banks[0], [0, 1])
-        late_slots = keep.tile([P, PACK * KEPT], F32, name="late_slots", tag="far_first_3", align_bytes=64)
-        kept_second = late_slots[:].rearrange("p (t c) -> p t c", t=PACK)
-        near_z = late_slots[:, 2 * KEPT :].bitcast(BF16)
-        weave(near_z, near_back, 2)
-        far_rise[2] = keep.tile([P, PAIRS - KEPT], F32, name="far_rise_2")
-        nc.scalar.activation(far_rise[2][:], far_excess[2][:], ACT.Relu)
-        turn_far(2, blocks_of(far_rise[2]), False, False)
-        turn_far(3, blocks_of(far_rise[3]), False, True)
         for block in range(2):
             last_turned = keep.tile([P, 2 * P], BF16, name=f"last_turned_{block}", align_bytes=64)
             turn_back(1, last_turned, word_banks[1][block], [block])
@@ -451,9 +458,8 @@ def tile_list_passage_document_coarsening_kernel(
 
         for t in range(2):
             pick_kept(kept_second, t, pos2_t)
-        for block in range(2):
-            start = KEPT + block * P
-            quantize_z(0, start, start + P, near_z[:, block * K_PASS : (block + 1) * K_PASS])
+        for half in range(2):
+            quantize_z(0, half * KEPT, (half + 1) * KEPT, near_z[half])
         pick_kept(kept_second, 2, pos2_t)
         pick_kept(kept_second, PACK - 1, pos2_t, 0, P)
         pick_kept(kept_second, PACK - 1, pos2_t, P, KEPT)

@@ -39,7 +39,7 @@ KEPT = 2 * P
 Y_RANGES = [
     [(0, KEPT, 2), (KEPT, 3 * P, 4), (3 * P, PAIRS, 0)],
     [(0, KEPT, 7), (KEPT, PAIRS, 5)],
-    [(0, KEPT, 6), (KEPT, PAIRS, 1)],
+    [(0, PAIRS, 6)],
     [(0, PAIRS, 3)],
 ]
 FAR_BANKS = [0, 4, 6, 0]
@@ -146,7 +146,7 @@ def tile_list_passage_document_coarsening_kernel(
             )
 
         def round_near(t):
-            near_bf16[t] = keep.tile([P, 2 * K_PASS], BF16, name=f"near_bf16_{t}", align_bytes=64)
+            near_bf16[t] = keep.tile([P, 2 * K_PASS], BF16, name=f"near_bf16_{t}", tag=f"near_bf16_{t}", align_bytes=64)
             for a in range(2):
                 round_pass(near_bf16[t][:, a * K_PASS : (a + 1) * K_PASS], t, a)
 
@@ -278,8 +278,8 @@ def tile_list_passage_document_coarsening_kernel(
 
         near_rise = {}
 
-        def relu_near(t, excess, dst=None):
-            near_rise[t] = keep.tile([P, PAIRS], F32, name=f"near_rise_{t}")[:] if dst is None else dst
+        def relu_near(t, excess, dst):
+            near_rise[t] = dst
             relu_beside(near_rise[t], excess)
 
         def turn_near(pair, first_bank):
@@ -316,7 +316,7 @@ def tile_list_passage_document_coarsening_kernel(
             )
 
         def relu_far(t):
-            far_rise[t] = keep.tile([P, PAIRS - KEPT], F32, name=f"far_rise_{t}")
+            far_rise[t] = keep.tile([P, PAIRS - KEPT], F32, name=f"far_rise_{t}", tag=f"far_rise_{t}", align_bytes=64)
             relu_beside(far_rise[t][:], far_excess[t][:])
 
 
@@ -345,14 +345,14 @@ def tile_list_passage_document_coarsening_kernel(
         first_excess = laid.tile([P, PAIRS], F32, name="first_excess", offset=FIRST_EXCESS_AT)
         pick_first(0)
         pick_excess(0, first_excess[:])
-        relu_near(0, first_excess[:])
         make_h(0, 1)
         round_near(3)
         quantize_near(3, "near_plane_3")
+        first_rise = keep.tile([P, PAIRS], F32, name="first_rise", tag="near_bf16_3", align_bytes=64)
+        relu_near(0, first_excess[:], first_rise[:])
         later_excess = laid.tile([P, PAIRS], F32, name="later_excess", offset=LATER_EXCESS_AT)
         pick_first(1)
         pick_excess(1, later_excess[:])
-        relu_near(1, later_excess[:])
         make_h(0, 2)
         round_far(0, 0)
         pick_first(2)
@@ -360,7 +360,6 @@ def tile_list_passage_document_coarsening_kernel(
         pick_excess(2, stages[0, 0][:, :PAIRS])
         round_far(0, 1)
         quantize_far(0, 1, 2)
-        relu_near(2, stages[0, 0][:, :PAIRS], stages[0, 1][:, PAIRS:])
         make_h(0, 3)
         round_far(1, 0)
         near_first[3] = stages[0, 1][:, :PAIRS]
@@ -370,8 +369,11 @@ def tile_list_passage_document_coarsening_kernel(
         pick_excess(3, last_near_excess[:])
         round_far(1, 1)
         quantize_far(1, 1, 1)
-        last_rise = laid.tile([P, PAIRS], F32, name="near_rise_3", offset=LAST_RISE_AT, align_bytes=64)
-        relu_near(3, last_near_excess[:], last_rise[:])
+        held_rise = laid.tile([P, PAIRS], F32, name="held_rise", offset=LAST_RISE_AT, align_bytes=64)
+        relu_near(1, later_excess[:], held_rise[:])
+        next_rise = laid.tile([P, PAIRS], F32, name="next_rise", offset=LATER_EXCESS_AT)
+        relu_near(2, stages[0, 0][:, :PAIRS], next_rise[:])
+        relu_near(3, last_near_excess[:], stages[0, 0][:, :PAIRS])
         make_h(1, 0)
         make_h(1, 1)
         early_banks = turn_near(0, 2)
@@ -422,7 +424,6 @@ def tile_list_passage_document_coarsening_kernel(
             for place, block in enumerate(blocks):
                 nc.tensor.transpose(far_back[block][:, u * P : (u + 1) * P], words[:, place * P : (place + 1) * P], identity[:])
 
-        z_planes.extend(keep.tile([P, PAIRS], U8, name=f"z_plane_{b}", align_bytes=64) for b in range(2))
         make_h(1, 2)
         make_h(1, 3)
         late_banks = turn_near(1, 4)
@@ -442,9 +443,9 @@ def tile_list_passage_document_coarsening_kernel(
         for t in range(PACK):
             turn_far(t, blocks_of(far_first[t]), t % 2 == 0, False)
             turn_far(t, blocks_of(far_rise[t]), False, t % 2 == 1)
-        late_slots = laid.tile([P, PACK * KEPT], F32, name="late_slots", offset=LAST_RISE_AT, align_bytes=64)
-        kept_second = late_slots[:].rearrange("p (t c) -> p t c", t=PACK)
-        near_z = [late_slots[:, 2 * KEPT :].bitcast(BF16), keep.tile([P, 2 * K_PASS], BF16, name="near_z", align_bytes=64)[:]]
+        late_slots = laid.tile([P, (PACK + 1) * KEPT], F32, name="late_slots", offset=LAST_RISE_AT - KIB, align_bytes=64)
+        kept_second = late_slots[:, : PACK * KEPT].rearrange("p (t c) -> p t c", t=PACK)
+        near_z = [late_slots[:, 3 * KEPT :].bitcast(BF16), keep.tile([P, 2 * K_PASS], BF16, name="near_z", align_bytes=64)[:]]
         for half in range(2):
             weave(near_z[half], near_back[half], 2)
         early_turned = keep.tile([P, K_PASS], BF16, name="early_turned", align_bytes=64)
@@ -456,11 +457,12 @@ def tile_list_passage_document_coarsening_kernel(
         for block in range(2):
             weave(turned_z[:, block * K_PASS : (block + 1) * K_PASS], far_back[block], 1)
 
-        for t in range(2):
+        for t in range(PACK - 1):
             pick_kept(kept_second, t, pos2_t)
+        z_planes.append(keep.tile([P, PAIRS], U8, name="z_plane_0", tag="far_rise_3", align_bytes=64))
+        z_planes.append(keep.tile([P, PAIRS], U8, name="z_plane_1", align_bytes=64))
         for half in range(2):
             quantize_z(0, half * KEPT, (half + 1) * KEPT, near_z[half])
-        pick_kept(kept_second, 2, pos2_t)
         pick_kept(kept_second, PACK - 1, pos2_t, 0, P)
         pick_kept(kept_second, PACK - 1, pos2_t, P, KEPT)
 
@@ -486,9 +488,10 @@ def tile_list_passage_document_coarsening_kernel(
                 copy_out = nc.vector.tensor_copy if (c, first) == (1, 0) else nc.scalar.copy
                 bank = psum.tile([P, end - first], F32, name=f"y_bank_{c}_{first}", tag=f"bank_{n}")
                 cuts = [first, KEPT, end] if first < KEPT < end else [first, end]
-                for start, stop in zip(cuts, cuts[1:]):
-                    for b in range(2):
-                        multiply_z(b, c, bank, first, start, stop, b == 0 and start == first, b == 1 and stop == end)
+                pieces = list(zip(cuts, cuts[1:]))
+                passes = [(0, piece) for piece in pieces] + [(1, piece) for piece in reversed(pieces)]
+                for place, (b, (start, stop)) in enumerate(passes):
+                    multiply_z(b, c, bank, first, start, stop, place == 0, place == len(passes) - 1)
                 copy_out(y[c][:, first:end], bank[:])
 
 

@@ -25,6 +25,7 @@ GROUP = 16
 QUADRANTS = 4
 F32_MAX = 3.4028234663852886e38
 KIB = 1024
+DMA_ALIGN = 256
 
 RAW_AT = {(1, 2 * P): 3 * KIB, (1, 3 * P): 9 * KIB}
 H_AT = {(0, 1): 0, (0, 2): 6 * KIB}
@@ -32,7 +33,7 @@ FIRST_EXCESS_AT = 4 * KIB
 LATER_EXCESS_AT = 10 * KIB
 
 LOWER = BANK + P
-UPPER_PIECES = [(start, start + P) for start in range(LOWER, S, P)]
+UPPER_PIECES = [(LOWER, S - P), (S - P, S)]
 HALVES = [(0, BANK), (BANK, S)]
 FIRST_RANGES = [(0, BANK), (BANK, S - 2 * P), (S - 2 * P, S - P), (S - P, S)]
 KEPT = 2 * P
@@ -69,19 +70,19 @@ def tile_list_passage_document_coarsening_kernel(
         def load_w1(a, start, width):
             name = f"w1_raw_{a}_{start}"
             if (a, start) in RAW_AT:
-                tile = laid.tile([P, PACK, width], F32, name=name, offset=RAW_AT[a, start])
+                tile = laid.tile([P, PACK, width], F32, name=name, offset=RAW_AT[a, start], align_bytes=DMA_ALIGN)
             else:
-                tile = keep.tile([P, PACK, width], F32, name=name, tag=name, align_bytes=64)
+                tile = keep.tile([P, PACK, width], F32, name=name, tag=name, align_bytes=DMA_ALIGN)
             rows = w1[a * K_PASS : (a + 1) * K_PASS, start : start + width]
             nc.sync.dma_start(tile[:], rows.rearrange("(p j) c -> p j c", j=PACK))
             return tile
 
         def load_table(a):
-            words = keep.tile([P, T], U32, name=f"table_{a}")
+            words = keep.tile([P, T], U32, name=f"table_{a}", align_bytes=DMA_ALIGN)
             nc.sync.dma_start(words[:].bitcast(I32), tab_words[a].rearrange("p t i -> p (t i)").bitcast(I32))
             return words
 
-        table_scales = keep.tile([P, T], U8, name="table_scales")
+        table_scales = keep.tile([P, T], U8, name="table_scales", align_bytes=DMA_ALIGN)
         w2_planes = keep.tile([P, 2, N], U8, name="w2_planes", align_bytes=64)
         warm_in = keep.tile([P, 1], F32, name="warm_in")
         warm_out = keep.tile([P, 1], F32, name="warm_out")
@@ -199,7 +200,7 @@ def tile_list_passage_document_coarsening_kernel(
         quantize_first(0)
         nc.vector.tensor_copy(v_lower[:], table[1][:].indirect(entries_of(offs_t, 0, LOWER)))
         quantize_first(1)
-        v_upper = keep.tile([P, S - LOWER], U32, name="v_upper", tag="w1_raw_1_0", align_bytes=64)
+        v_upper = keep.tile([P, S - LOWER], U32, name="v_upper", tag="w1_raw_1_0", align_bytes=DMA_ALIGN)
         for start, stop in UPPER_PIECES:
             nc.vector.tensor_copy(
                 v_upper[:, start - LOWER : stop - LOWER], table[1][:].indirect(entries_of(offs_t, start, stop))
@@ -257,7 +258,7 @@ def tile_list_passage_document_coarsening_kernel(
             if (b, t) in H_AT:
                 h[b, t] = laid.tile([P, S], F32, name=name, offset=H_AT[b, t])
             else:
-                h[b, t] = keep.tile([P, S], F32, name=name, tag=tag or name, align_bytes=64)
+                h[b, t] = keep.tile([P, S], F32, name=name, tag=tag or name, align_bytes=DMA_ALIGN)
             for n, (bank, (start, stop)) in enumerate(banks):
                 copy_out = nc.scalar.copy if n < len(HALVES) else nc.vector.tensor_copy
                 copy_out(h[b, t][:, start:stop], bank[:])
@@ -365,7 +366,7 @@ def tile_list_passage_document_coarsening_kernel(
         near_first[3] = stages[0, 1][:, :PAIRS]
         pick_first(3)
         quantize_far(1, 0, 1)
-        last_near_excess = keep.tile([P, PAIRS], F32, name="last_near_excess", tag=f"w1_raw_0_{K_PASS}", align_bytes=64)
+        last_near_excess = keep.tile([P, PAIRS], F32, name="last_near_excess", tag=f"w1_raw_0_{K_PASS}", align_bytes=DMA_ALIGN)
         pick_excess(3, last_near_excess[:])
         round_far(1, 1)
         quantize_far(1, 1, 1)
@@ -501,29 +502,37 @@ def tile_list_passage_document_coarsening_kernel(
         def doc_pieces(c):
             return [(0, DOCS // 2), (DOCS // 2, DOCS)] if c == N // P - 1 else [(0, DOCS)]
 
-        def pick_y(c):
-            right = keep.tile([P, DOCS], F32, name=f"right_{c}", tag=f"right_{c}")
+        stay = {}
+
+        def pick_right(c):
+            right = keep.tile([P, DOCS], F32, name=f"right_{c}", tag=f"right_{c}", align_bytes=DMA_ALIGN)
             nc.vector.tensor_copy(right[:], y[c][:].indirect(pos4_t[:]))
-            stay = keep.tile([P, DOCS], F32, name=f"stay_{c}")
+            stay[c] = keep.tile([P, DOCS], F32, name=f"stay_{c}")
             gate[c] = keep.tile([P, DOCS], F32, name=f"gate_{c}")
-            nc.scalar.activation(stay[:], right[:], ACT.Sigmoid, scale=-1.0)
-            nc.scalar.activation(gate[c][:], right[:], ACT.Sigmoid)
             kept[c] = keep.tile([P, DOCS], F32, name=f"kept_{c}")
-            for start, stop in doc_pieces(c):
-                nc.vector.tensor_tensor(
-                    kept[c][:, start:stop], y[c][:].indirect(entries_of(pos3_t, start, stop)), stay[:, start:stop], ALU.mult
-                )
+            sigmoids = [(stay[c], -1.0), (gate[c], 1.0)]
+            for dst, sign in reversed(sigmoids) if c == N // P - 1 else sigmoids:
+                nc.scalar.activation(dst[:], right[:], ACT.Sigmoid, scale=sign)
+
+        def pick_left(c, start, stop):
+            nc.vector.tensor_tensor(
+                kept[c][:, start:stop], y[c][:].indirect(entries_of(pos3_t, start, stop)), stay[c][:, start:stop], ALU.mult
+            )
 
         def store_doc(c):
-            doc = keep.tile([P, DOCS], F32, name=f"doc_{c}", tag=f"right_{c + 1}")
+            doc = keep.tile([P, DOCS], F32, name=f"doc_{c}", tag=f"right_{c + 1}", align_bytes=DMA_ALIGN)
             for start, stop in doc_pieces(c):
                 nc.vector.scalar_tensor_tensor(
                     doc[:, start:stop], gate[c][:, start:stop], w_col[:, c : c + 1], kept[c][:, start:stop], ALU.mult, ALU.add
                 )
                 nc.sync.dma_start(out[c * P : (c + 1) * P, start:stop], doc[:, start:stop])
 
-        pick_y(0)
-        for c in range(1, N // P):
-            pick_y(c)
-            store_doc(c - 1)
+        for c in range(N // P):
+            pick_right(c)
+            first_piece, *other_pieces = doc_pieces(c)
+            pick_left(c, *first_piece)
+            if c > 0:
+                store_doc(c - 1)
+            for piece in other_pieces:
+                pick_left(c, *piece)
         store_doc(N // P - 1)

@@ -114,9 +114,9 @@ def tile_list_passage_document_coarsening_kernel(
         load_near(1, [0])
         load_near(0, [1])
         load_near(1, [1])
-        load_near(0, [2, 3])
-        load_near(1, [2])
-        load_near(1, [3])
+        for t in range(2, PACK):
+            for a in range(2):
+                load_near(a, [t])
         far_raw = [load_w1(a, K_PASS, K_PASS) for a in range(2)]
         w2_codes = keep.tile([P, 2, 2 * N], U8, name="w2_codes", align_bytes=64)
         nc.sync.dma_start(w2_codes[:].bitcast(I32), w2_words.rearrange("a p c -> p a c").bitcast(I32))
@@ -430,7 +430,7 @@ def tile_list_passage_document_coarsening_kernel(
         late_banks = turn_near(1, 4)
         for t in range(2, PACK):
             pick_far(t)
-            relu_far(t)
+        relu_far(2)
         for pair, banks in enumerate((early_banks, late_banks)):
             for n, bank in enumerate(banks):
                 round_turned(pair, n, bank)
@@ -441,14 +441,16 @@ def tile_list_passage_document_coarsening_kernel(
             psum.tile([P, 2 * P], F32, name=f"far_turned_bank_1_{block}", tag=f"bank_{4 + block}") for block in range(2)
         ]
         far_back = [psum.tile([P, 2 * P], F32, name=f"far_back_bank_{block}", tag=f"bank_{block}") for block in range(2)]
-        for t in range(PACK):
-            turn_far(t, blocks_of(far_first[t]), t % 2 == 0, False)
-            turn_far(t, blocks_of(far_rise[t]), False, t % 2 == 1)
         late_slots = laid.tile([P, (PACK + 1) * KEPT], F32, name="late_slots", offset=LAST_RISE_AT - KIB, align_bytes=64)
         kept_second = late_slots[:, : PACK * KEPT].rearrange("p (t c) -> p t c", t=PACK)
         near_z = [late_slots[:, 3 * KEPT :].bitcast(BF16), keep.tile([P, 2 * K_PASS], BF16, name="near_z", align_bytes=64)[:]]
         for half in range(2):
             weave(near_z[half], near_back[half], 2)
+        far_rise[3] = laid.tile([P, PAIRS - KEPT], F32, name="far_rise_3", offset=TURNED_AT[1], align_bytes=64)
+        nc.scalar.activation(far_rise[3][:], far_excess[3][:], ACT.Relu)
+        for t in range(PACK):
+            turn_far(t, blocks_of(far_first[t]), t % 2 == 0, False)
+            turn_far(t, blocks_of(far_rise[t]), False, t % 2 == 1)
         early_turned = keep.tile([P, K_PASS], BF16, name="early_turned", align_bytes=64)
         turn_back(0, early_turned, word_banks[0], [0, 1])
         for block in range(2):
@@ -460,7 +462,7 @@ def tile_list_passage_document_coarsening_kernel(
 
         for t in range(PACK - 1):
             pick_kept(kept_second, t, pos2_t)
-        z_planes.append(keep.tile([P, PAIRS], U8, name="z_plane_0", tag="far_rise_3", align_bytes=64))
+        z_planes.append(laid.tile([P, PAIRS], U8, name="z_plane_0", offset=TURNED_AT[1], align_bytes=64))
         z_planes.append(keep.tile([P, PAIRS], U8, name="z_plane_1", align_bytes=64))
         for half in range(2):
             quantize_z(0, half * KEPT, (half + 1) * KEPT, near_z[half])

@@ -252,7 +252,7 @@ def tile_list_passage_document_coarsening_kernel(
                     )
             return list(zip(banks, ranges))
 
-        def make_h(b, t, tag=None):
+        def make_h(b, t, tag=None, between=None):
             banks = multiply_h(b, t)
             name = f"h_{b}_{t}"
             if (b, t) in H_AT:
@@ -262,6 +262,8 @@ def tile_list_passage_document_coarsening_kernel(
             for n, (bank, (start, stop)) in enumerate(banks):
                 copy_out = nc.scalar.copy if n < len(HALVES) else nc.vector.tensor_copy
                 copy_out(h[b, t][:, start:stop], bank[:])
+                if n == 0 and between is not None:
+                    round_far(*between)
 
         near_first = {t: keep.tile([P, PAIRS], F32, name=f"near_first_{t}")[:] for t in range(PACK - 1)}
 
@@ -287,16 +289,17 @@ def tile_list_passage_document_coarsening_kernel(
             banks = [
                 psum.tile([P, K_PASS], F32, name=f"near_turned_bank_{pair}_{n}", tag=f"bank_{first_bank + n}") for n in range(2)
             ]
-            for e in range(2):
-                t = 2 * pair + e
-                for term, src in enumerate((near_first[t], near_rise[t])):
-                    for j in range(PAIRS // P):
-                        n, block = divmod(j, 2)
-                        place = (2 * block + e) * P
-                        ends = (e, term, block)
-                        add_turned(
-                            banks[n][:, place : place + P], src[:, j * P : (j + 1) * P], ends == (0, 0, 0), ends == (1, 1, 1)
-                        )
+            for n, bank in enumerate(banks):
+                for e in range(2):
+                    t = 2 * pair + e
+                    for term, src in enumerate((near_first[t], near_rise[t])):
+                        for block in range(2):
+                            j = 2 * n + block
+                            place = (2 * block + e) * P
+                            ends = (e, term, block)
+                            add_turned(
+                                bank[:, place : place + P], src[:, j * P : (j + 1) * P], ends == (0, 0, 0), ends == (1, 1, 1)
+                            )
             return banks
 
         far_first = {}
@@ -339,8 +342,8 @@ def tile_list_passage_document_coarsening_kernel(
             )
 
         round_near(1)
+        quantize_near(1, "near_plane_1")
         make_h(0, 0, f"w1_raw_1_{P}")
-        quantize_near(1, "near_plane_0")
         round_near(2)
         quantize_near(2, "near_plane_2")
         first_excess = laid.tile([P, PAIRS], F32, name="first_excess", offset=FIRST_EXCESS_AT)
@@ -359,9 +362,8 @@ def tile_list_passage_document_coarsening_kernel(
         pick_first(2)
         quantize_far(0, 0, 2)
         pick_excess(2, stages[0, 0][:, :PAIRS])
-        round_far(0, 1)
+        make_h(0, 3, between=(0, 1))
         quantize_far(0, 1, 2)
-        make_h(0, 3)
         round_far(1, 0)
         near_first[3] = stages[0, 1][:, :PAIRS]
         pick_first(3)

from contextlib import ExitStack

import concourse.mybir as mybir
from concourse.masks import make_identity

K, T, S, PAIRS, DOCS, H, N = 1024, 2048, 1024, 512, 256, 1024, 512
FLOPS = 2 * K * H * S + 2 * H * N * PAIRS

F32 = mybir.dt.float32
BF16 = mybir.dt.bfloat16
I32 = mybir.dt.int32
U32 = mybir.dt.uint32
U16 = mybir.dt.uint16
U8 = mybir.dt.uint8
FP8X4 = mybir.dt.float8_e4m3fn_x4
FP4X4 = mybir.dt.float4_e2m1fn_x4
ALU = mybir.AluOpType
ACT = mybir.ActivationFunctionType

P = 128
PACK = 4
K_PASS = P * PACK
BANK = 512
GROUP = 16
QUADRANTS = 4
F32_MAX = 3.4028234663852886e38
KIB = 1024
DMA_ALIGN = 256

RAW_AT = {(1, 2 * P): 3 * KIB, (1, 3 * P): 9 * KIB}
H_AT = {(0, 1): 0, (0, 2): 6 * KIB}
FIRST_EXCESS_AT = 4 * KIB
LATER_EXCESS_AT = 10 * KIB

LOWER = BANK + P
UPPER_PIECES = [(LOWER, S - P), (S - P, S)]
HALVES = [(0, BANK), (BANK, S)]
FIRST_RANGES = [(0, BANK), (BANK, S - 2 * P), (S - 2 * P, S - P), (S - P, S)]
KEPT = 2 * P
Y_RANGES = [
    [(0, KEPT, 2), (KEPT, 3 * P, 4), (3 * P, PAIRS, 0)],
    [(0, KEPT, 7), (KEPT, PAIRS, 5)],
    [(0, PAIRS, 6)],
    [(0, PAIRS, 3)],
]
FAR_BANKS = [0, 4, 6, 0]
LAST_STAGE_AT = 20 * KIB
LAST_RISE_AT = LAST_STAGE_AT - 3 * KIB // 2
TURNED_AT = [LAST_RISE_AT + 2 * KIB, LAST_RISE_AT + 4 * KIB]


def tile_list_passage_document_coarsening_kernel(
    tc, tab_words, tab_scales, offs, w1, pos1, pos2, w2_words, w2_scales, pos3, pos4, w, out
):
    nc = tc.nc
    with ExitStack() as ctx:
        keep = ctx.enter_context(tc.tile_pool(name="keep", bufs=1))
        laid = ctx.enter_context(tc.tile_pool(name="laid", bufs=1))
        psum = ctx.enter_context(tc.psum_pool(name="psum", bufs=1))


        def load_list(name, src, entries):
            tile = keep.tile([P, entries // GROUP], U16, name=name)
            nc.sync.dma_start(tile[:], src)
            return tile

        def entries_of(list_tile, start, stop):
            return list_tile[:, start // GROUP : stop // GROUP]

        def load_w1(a, start, width):
            name = f"w1_raw_{a}_{start}"
            if (a, start) in RAW_AT:
                tile = laid.tile([P, PACK, width], F32, name=name, offset=RAW_AT[a, start], align_bytes=DMA_ALIGN)
            else:
                tile = keep.tile([P, PACK, width], F32, name=name, tag=name, align_bytes=DMA_ALIGN)
            rows = w1[a * K_PASS : (a + 1) * K_PASS, start : start + width]
            nc.sync.dma_start(tile[:], rows.rearrange("(p j) c -> p j c", j=PACK))
            return tile

        def load_table(a):
            words = keep.tile([P, T], U32, name=f"table_{a}", align_bytes=DMA_ALIGN)
            nc.sync.dma_start(words[:].bitcast(I32), tab_words[a].rearrange("p t i -> p (t i)").bitcast(I32))
            return words

        table_scales = keep.tile([P, T], U8, name="table_scales", align_bytes=DMA_ALIGN)
        w2_planes = keep.tile([P, 2, N], U8, name="w2_planes", align_bytes=64)
        warm_in = keep.tile([P, 1], F32, name="warm_in")
        warm_out = keep.tile([P, 1], F32, name="warm_out")
        nc.vector.memset(table_scales[:].bitcast(I32), 0)
        nc.vector.memset(warm_in[:], 0.0)
        nc.vector.memset(w2_planes[:].bitcast(I32), 0)
        identity = keep.tile([P, P], F32, name="identity")
        nc.vector.memset(identity[:], 0.0)
        make_identity(nc, identity[:], nomemset=True)

        offs_t = load_list("offs_t", offs, S)
        nc.scalar.activation(warm_out[:], warm_in[:], ACT.Sigmoid)
        near_raw = {}

        def load_near(a, tiles):
            chunk = load_w1(a, tiles[0] * P, len(tiles) * P)
            for place, t in enumerate(tiles):
                near_raw[t, a] = chunk[:, :, place * P : (place + 1) * P]

        pos1_t = load_list("pos1_t", pos1, PAIRS)
        pos2_t = load_list("pos2_t", pos2, PAIRS)
        for q in range(QUADRANTS):
            nc.sync.dma_start(
                table_scales[32 * q : 32 * q + 8, :].bitcast(I32), tab_scales[:, 4 * q : 4 * q + 4, :].bitcast(I32)
            )
        table = [load_table(0)]
        load_near(0, [0])
        table.append(load_table(1))
        load_near(1, [0])
        load_near(0, [1])
        load_near(1, [1])
        for t in range(2, PACK):
            for a in range(2):
                load_near(a, [t])
        far_raw = [load_w1(a, K_PASS, K_PASS) for a in range(2)]
        w2_codes = keep.tile([P, 2, 2 * N], U8, name="w2_codes", align_bytes=64)
        nc.sync.dma_start(w2_codes[:].bitcast(I32), w2_words.rearrange("a p c -> p a c").bitcast(I32))
        for q in range(QUADRANTS):
            nc.sync.dma_start(
                w2_planes[32 * q : 32 * q + 4, :, :].bitcast(I32),
                w2_scales[:, 4 * q : 4 * q + 4, :].rearrange("a r c -> r a c").bitcast(I32),
            )
        pos3_t = load_list("pos3_t", pos3, DOCS)
        pos4_t = load_list("pos4_t", pos4, DOCS)
        w_col = keep.tile([P, N // P], F32, name="w_col")
        with nc.allow_non_contiguous_dma(reason="one value of w for each partition"):
            nc.sync.dma_start(w_col[:], w.rearrange("(c p) -> p c", p=P))


        near_bf16 = {}
        near_codes = {}
        near_planes = {}
        stages = {}
        far_bf16 = {}
        far_codes = {}
        far_planes = {}

        def round_pass(dst, t, a):
            nc.scalar.copy(
                dst.rearrange("p (c i j) -> p c j i", i=4, j=PACK),
                near_raw[t, a].rearrange("p j (c i) -> p c j i", i=4),
            )

        def round_near(t):
            near_bf16[t] = keep.tile([P, 2 * K_PASS], BF16, name=f"near_bf16_{t}", tag=f"near_bf16_{t}", align_bytes=64)
            for a in range(2):
                round_pass(near_bf16[t][:, a * K_PASS : (a + 1) * K_PASS], t, a)

        def quantize_near(t, plane_tag):
            near_codes[t] = keep.tile([P, 2 * P], U32, name=f"near_codes_{t}", align_bytes=64)
            near_planes[t] = keep.tile([P, 2 * P], U8, name=f"near_plane_{t}", tag=plane_tag, align_bytes=64)
            nc.vector.quantize_mx(out=near_codes[t][:].bitcast(FP8X4), scales=near_planes[t][:], in_=near_bf16[t][:])

        def round_far(u, a):
            name = f"far_stage_{u}_{a}"
            if (u, a) == (1, 1):
                stages[u, a] = laid.tile([P, 2 * PAIRS], F32, name=name, offset=LAST_STAGE_AT, align_bytes=64)
            else:
                stages[u, a] = keep.tile([P, 2 * PAIRS], F32, name=name, align_bytes=64)
            far_bf16[u, a] = stages[u, a][:, PAIRS // 2 : 3 * PAIRS // 2].bitcast(BF16)
            nc.scalar.copy(
                far_bf16[u, a].rearrange("p (t m j) -> p m j t", t=2, j=PACK),
                far_raw[a][:].rearrange("p j (m t) -> p m j t", t=PACK)[:, :, :, 2 * u : 2 * u + 2],
            )

        def quantize_far(u, a, parts):
            width = 2 * P // parts
            for n in range(parts):
                cols = slice(2 * a * P + n * width, 2 * a * P + (n + 1) * width)
                nc.vector.quantize_mx(
                    out=far_codes[u][:, cols].bitcast(FP8X4),
                    scales=far_planes[u][:, cols],
                    in_=far_bf16[u, a][:, n * width * PACK : (n + 1) * width * PACK],
                )

        for u in range(2):
            far_codes[u] = keep.tile([P, 4 * P], U32, name=f"far_codes_{u}", align_bytes=64)
            far_planes[u] = keep.tile([P, 4 * P], U8, name=f"far_plane_{u}", align_bytes=64)


        v_scales = keep.tile([P, S], U8, name="v_scales", align_bytes=64)
        v_first = keep.tile([P, S], U32, name="v_first", align_bytes=64)
        v_lower = keep.tile([P, LOWER], U32, name="v_lower", align_bytes=64)
        near_codes[0] = keep.tile([P, 2 * P], U32, name="near_codes_0", align_bytes=64)
        near_planes[0] = keep.tile([P, 2 * P], U8, name="near_plane_0", tag="near_plane_0", align_bytes=64)

        def quantize_first(a):
            stage = keep.tile([P, K_PASS], BF16, name=f"first_bf16_{a}", align_bytes=64)
            round_pass(stage[:], 0, a)
            cols = slice(a * P, (a + 1) * P)
            nc.vector.quantize_mx(out=near_codes[0][:, cols].bitcast(FP8X4), scales=near_planes[0][:, cols], in_=stage[:])

        nc.vector.tensor_copy(v_scales[:], table_scales[:].indirect(offs_t[:]))
        nc.vector.tensor_copy(v_first[:], table[0][:].indirect(offs_t[:]))
        quantize_first(0)
        nc.vector.tensor_copy(v_lower[:], table[1][:].indirect(entries_of(offs_t, 0, LOWER)))
        quantize_first(1)
        v_upper = keep.tile([P, S - LOWER], U32, name="v_upper", tag="w1_raw_1_0", align_bytes=DMA_ALIGN)
        for start, stop in UPPER_PIECES:
            nc.vector.tensor_copy(
                v_upper[:, start - LOWER : stop - LOWER], table[1][:].indirect(entries_of(offs_t, start, stop))
            )

        def v_codes(a, start, stop):
            if a == 0:
                return v_first[:, start:stop]
            if start < LOWER:
                return v_lower[:, start:stop]
            return v_upper[:, start - LOWER : stop - LOWER]


        h = {}

        def multiply_h(b, t):
            if b == 0:
                codes, planes = near_codes[t], near_planes[t]
                first_col = [a * P for a in range(2)]
            else:
                u, e = divmod(t, 2)
                codes, planes = far_codes[u], far_planes[u]
                first_col = [(2 * a + e) * P for a in range(2)]
            ranges = FIRST_RANGES if (b, t) == (0, 0) else HALVES
            first_bank = 2 * t if b == 0 else FAR_BANKS[t]
            bank_numbers = [first_bank, first_bank + 1, 7, 6]
            banks = [
                psum.tile([P, stop - start], F32, name=f"h_bank_{b}_{t}_{n}", tag=f"bank_{bank_numbers[n]}")
                for n, (start, stop) in enumerate(ranges)
            ]
            order = [(a, n) for n in range(len(ranges)) for a in range(2)]
            if (b, t) == (0, 0):
                order = sorted(order)
            for a, n in order:
                weights = slice(first_col[a], first_col[a] + P)
                begin, end = ranges[n]
                cuts = [begin, end]
                if a == 1 and begin < LOWER < end:
                    cuts = sorted({begin, LOWER, min(LOWER + 2 * P, end), end})
                for start, stop in zip(cuts, cuts[1:]):
                    nc.tensor.matmul_mx(
                        out=banks[n][:, start - begin : stop - begin],
                        lhsT=codes[:, weights].bitcast(FP8X4),
                        lhsT_scale=planes[:, weights],
                        rhs=v_codes(a, start, stop).bitcast(FP8X4),
                        rhs_scale=v_scales[4 * a : P, start:stop],
                        start=(a == 0),
                        stop=(a == 1 and stop == end),
                    )
            return list(zip(banks, ranges))

        def make_h(b, t, tag=None, between=None):
            banks = multiply_h(b, t)
            name = f"h_{b}_{t}"
            if (b, t) in H_AT:
                h[b, t] = laid.tile([P, S], F32, name=name, offset=H_AT[b, t])
            else:
                h[b, t] = keep.tile([P, S], F32, name=name, tag=tag or name, align_bytes=DMA_ALIGN)
            for n, (bank, (start, stop)) in enumerate(banks):
                copy_out = nc.scalar.copy if n < len(HALVES) else nc.vector.tensor_copy
                copy_out(h[b, t][:, start:stop], bank[:])
                if n == 0 and between is not None:
                    round_far(*between)

        near_first = {t: keep.tile([P, PAIRS], F32, name=f"near_first_{t}")[:] for t in range(PACK - 1)}

        def pick_first(t):
            nc.vector.tensor_copy(near_first[t], h[0, t][:].indirect(pos1_t[:]))

        def pick_excess(t, excess):
            nc.vector.tensor_tensor(excess, h[0, t][:].indirect(pos2_t[:]), near_first[t], ALU.subtract)

        def relu_beside(dst, src):
            nc.gpsimd.tensor_scalar(dst, src, F32_MAX, 0.0, ALU.min, ALU.max)

        def add_turned(dst, src, start, stop):
            nc.tensor.matmul(dst, lhsT=src, rhs=identity[:], is_transpose=True, start=start, stop=stop)

        near_rise = {}

        def relu_near(t, excess, dst):
            near_rise[t] = dst
            relu_beside(near_rise[t], excess)

        def turn_near(pair, first_bank):
            banks = [
                psum.tile([P, K_PASS], F32, name=f"near_turned_bank_{pair}_{n}", tag=f"bank_{first_bank + n}") for n in range(2)
            ]
            for n, bank in enumerate(banks):
                for e in range(2):
                    t = 2 * pair + e
                    for term, src in enumerate((near_first[t], near_rise[t])):
                        for block in range(2):
                            j = 2 * n + block
                            place = (2 * block + e) * P
                            ends = (e, term, block)
                            add_turned(
                                bank[:, place : place + P], src[:, j * P : (j + 1) * P], ends == (0, 0, 0), ends == (1, 1, 1)
                            )
            return banks

        far_first = {}
        far_excess = {}
        far_rise = {}
        kept_first = keep.tile([P, PACK, KEPT], F32, name="kept_first")

        def pick_kept(dst, t, list_tile, start=0, stop=KEPT):
            nc.vector.tensor_copy(dst[:, t, start:stop], h[1, t][:].indirect(entries_of(list_tile, start, stop)))

        def pick_far(t):
            far_first[t] = keep.tile([P, PAIRS - KEPT], F32, name=f"far_first_{t}")
            far_excess[t] = keep.tile([P, PAIRS - KEPT], F32, name=f"far_excess_{t}", tag=f"far_excess_{t}", align_bytes=64)
            nc.vector.tensor_copy(far_first[t][:], h[1, t][:].indirect(entries_of(pos1_t, KEPT, PAIRS)))
            pick_kept(kept_first, t, pos1_t)
            nc.vector.tensor_tensor(
                far_excess[t][:], h[1, t][:].indirect(entries_of(pos2_t, KEPT, PAIRS)), far_first[t][:], ALU.subtract
            )

        def relu_far(t):
            far_rise[t] = keep.tile([P, PAIRS - KEPT], F32, name=f"far_rise_{t}", tag=f"far_rise_{t}", align_bytes=64)
            relu_beside(far_rise[t][:], far_excess[t][:])


        z_codes = [keep.tile([P, PAIRS], U32, name=f"z_codes_{b}", align_bytes=64) for b in range(2)]
        z_planes = []

        def quantize_z(b, start, stop, src):
            nc.vector.quantize_mx(out=z_codes[b][:, start:stop].bitcast(FP8X4), scales=z_planes[b][:, start:stop], in_=src)

        def multiply_z(b, c, bank, first, start, stop, opens, closes):
            nc.tensor.matmul_mx(
                out=bank[:, start - first : stop - first],
                lhsT=w2_codes[:, b, 2 * c * P : 2 * (c + 1) * P].bitcast(FP4X4),
                lhsT_scale=w2_planes[:, b, c * P : (c + 1) * P],
                rhs=z_codes[b][:, start:stop].bitcast(FP8X4),
                rhs_scale=z_planes[b][:, start:stop],
                start=opens,
                stop=closes,
            )

        round_near(1)
        quantize_near(1, "near_plane_1")
        make_h(0, 0, f"w1_raw_1_{P}")
        round_near(2)
        quantize_near(2, "near_plane_2")
        first_excess = laid.tile([P, PAIRS], F32, name="first_excess", offset=FIRST_EXCESS_AT)
        pick_first(0)
        pick_excess(0, first_excess[:])
        make_h(0, 1)
        round_near(3)
        quantize_near(3, "near_plane_3")
        first_rise = keep.tile([P, PAIRS], F32, name="first_rise", tag="near_bf16_3", align_bytes=64)
        relu_near(0, first_excess[:], first_rise[:])
        later_excess = laid.tile([P, PAIRS], F32, name="later_excess", offset=LATER_EXCESS_AT)
        pick_first(1)
        pick_excess(1, later_excess[:])
        make_h(0, 2)
        round_far(0, 0)
        pick_first(2)
        quantize_far(0, 0, 2)
        pick_excess(2, stages[0, 0][:, :PAIRS])
        make_h(0, 3, between=(0, 1))
        quantize_far(0, 1, 2)
        round_far(1, 0)
        near_first[3] = stages[0, 1][:, :PAIRS]
        pick_first(3)
        quantize_far(1, 0, 1)
        last_near_excess = keep.tile([P, PAIRS], F32, name="last_near_excess", tag=f"w1_raw_0_{K_PASS}", align_bytes=DMA_ALIGN)
        pick_excess(3, last_near_excess[:])
        round_far(1, 1)
        quantize_far(1, 1, 1)
        held_rise = laid.tile([P, PAIRS], F32, name="held_rise", offset=LAST_RISE_AT, align_bytes=64)
        relu_near(1, later_excess[:], held_rise[:])
        next_rise = laid.tile([P, PAIRS], F32, name="next_rise", offset=LATER_EXCESS_AT)
        relu_near(2, stages[0, 0][:, :PAIRS], next_rise[:])
        relu_near(3, last_near_excess[:], stages[0, 0][:, :PAIRS])
        make_h(1, 0)
        make_h(1, 1)
        early_banks = turn_near(0, 2)
        for t in range(2):
            pick_far(t)
            relu_far(t)
        turned = [laid.tile([P, 2 * K_PASS], BF16, name=f"z_turned_{n}", offset=TURNED_AT[n], align_bytes=64) for n in range(2)]

        def round_turned(pair, n, bank):
            nc.scalar.copy(
                turned[n][:].rearrange("m (j u g p e) -> m g j u p e", j=2, u=2, g=2, e=2)[:, pair],
                bank[:].rearrange("m (j p u e) -> m j u p e", j=2, u=2, e=2),
            )

        def weave(dst, bank, blocks):
            nc.scalar.copy(
                dst.bitcast(F32).rearrange("p (j m u) -> p j m u", j=blocks, u=2),
                bank[:].rearrange("p (j u m) -> p j m u", j=blocks, u=2),
            )

        def finish_near(half):
            bank = psum.tile([P, K_PASS], F32, name=f"z_back_bank_{half}", tag=f"bank_{2 + half}")
            words = turned[half][:].bitcast(F32)
            for place in range(PACK):
                nc.tensor.transpose(bank[:, place * P : (place + 1) * P], words[:, place * P : (place + 1) * P], identity[:])
            return bank

        word_banks = {}

        def turn_far(t, blocks, opens, closes):
            u, e = divmod(t, 2)
            for block, src in enumerate(blocks):
                if u == 0:
                    place = (2 * block + e) * P
                    add_turned(word_banks[0][:, place : place + P], src, opens and block == 0, closes and block == 1)
                else:
                    add_turned(word_banks[1][block][:, e * P : (e + 1) * P], src, opens, closes)

        def blocks_of(tile):
            return [tile[:, block * P : (block + 1) * P] for block in range(2)]

        def turn_back(u, tile, bank, blocks):
            count = len(blocks)
            nc.scalar.copy(
                tile[:].rearrange("m (b p e) -> m b p e", b=count, e=2), bank[:].rearrange("m (b e p) -> m b p e", b=count, e=2)
            )
            words = tile[:].bitcast(F32)
            for place, block in enumerate(blocks):
                nc.tensor.transpose(far_back[block][:, u * P : (u + 1) * P], words[:, place * P : (place + 1) * P], identity[:])

        make_h(1, 2)
        make_h(1, 3)
        late_banks = turn_near(1, 4)
        for t in range(2, PACK):
            pick_far(t)
        relu_far(2)
        for pair, banks in enumerate((early_banks, late_banks)):
            for n, bank in enumerate(banks):
                round_turned(pair, n, bank)
        near_back = [finish_near(half) for half in range(2)]

        word_banks[0] = psum.tile([P, K_PASS], F32, name="far_turned_bank_0", tag="bank_6")
        word_banks[1] = [
            psum.tile([P, 2 * P], F32, name=f"far_turned_bank_1_{block}", tag=f"bank_{4 + block}") for block in range(2)
        ]
        far_back = [psum.tile([P, 2 * P], F32, name=f"far_back_bank_{block}", tag=f"bank_{block}") for block in range(2)]
        late_slots = laid.tile([P, (PACK + 1) * KEPT], F32, name="late_slots", offset=LAST_RISE_AT - KIB, align_bytes=64)
        kept_second = late_slots[:, : PACK * KEPT].rearrange("p (t c) -> p t c", t=PACK)
        near_z = [late_slots[:, 3 * KEPT :].bitcast(BF16), keep.tile([P, 2 * K_PASS], BF16, name="near_z", align_bytes=64)[:]]
        for half in range(2):
            weave(near_z[half], near_back[half], 2)
        far_rise[3] = laid.tile([P, PAIRS - KEPT], F32, name="far_rise_3", offset=TURNED_AT[1], align_bytes=64)
        nc.scalar.activation(far_rise[3][:], far_excess[3][:], ACT.Relu)
        for t in range(PACK):
            turn_far(t, blocks_of(far_first[t]), t % 2 == 0, False)
            turn_far(t, blocks_of(far_rise[t]), False, t % 2 == 1)
        early_turned = keep.tile([P, K_PASS], BF16, name="early_turned", align_bytes=64)
        turn_back(0, early_turned, word_banks[0], [0, 1])
        for block in range(2):
            last_turned = keep.tile([P, 2 * P], BF16, name=f"last_turned_{block}", align_bytes=64)
            turn_back(1, last_turned, word_banks[1][block], [block])
        turned_z = keep.tile([P, 2 * K_PASS], BF16, name="turned_z", align_bytes=64)
        for block in range(2):
            weave(turned_z[:, block * K_PASS : (block + 1) * K_PASS], far_back[block], 1)

        for t in range(PACK - 1):
            pick_kept(kept_second, t, pos2_t)
        z_planes.append(laid.tile([P, PAIRS], U8, name="z_plane_0", offset=TURNED_AT[1], align_bytes=64))
        z_planes.append(keep.tile([P, PAIRS], U8, name="z_plane_1", align_bytes=64))
        for half in range(2):
            quantize_z(0, half * KEPT, (half + 1) * KEPT, near_z[half])
        pick_kept(kept_second, PACK - 1, pos2_t, 0, P)
        pick_kept(kept_second, PACK - 1, pos2_t, P, KEPT)

        def max_kept(dst, start, stop):
            nc.vector.tensor_tensor(
                dst[:].rearrange("p (c i t) -> p c t i", i=2, t=PACK),
                kept_first[:, :, start:stop].rearrange("p t (c i) -> p c t i", i=2),
                kept_second[:, :, start:stop].rearrange("p t (c i) -> p c t i", i=2),
                ALU.max,
            )

        kept_z = [keep.tile([P, K_PASS], BF16, name=f"kept_z_{n}", align_bytes=64) for n in range(2)]
        for n in range(2):
            max_kept(kept_z[n], n * P, (n + 1) * P)
        for n in range(2):
            quantize_z(1, n * P, (n + 1) * P, kept_z[n][:])
        quantize_z(1, KEPT, 3 * P, turned_z[:, :K_PASS])
        quantize_z(1, 3 * P, PAIRS, turned_z[:, K_PASS:])

        y = [keep.tile([P, PAIRS], F32, name=f"y_{c}") for c in range(N // P)]
        for c, ranges in enumerate(Y_RANGES):
            for first, end, n in ranges:
                copy_out = nc.vector.tensor_copy if (c, first) == (1, 0) else nc.scalar.copy
                bank = psum.tile([P, end - first], F32, name=f"y_bank_{c}_{first}", tag=f"bank_{n}")
                cuts = [first, KEPT, end] if first < KEPT < end else [first, end]
                pieces = list(zip(cuts, cuts[1:]))
                passes = [(0, piece) for piece in pieces] + [(1, piece) for piece in reversed(pieces)]
                for place, (b, (start, stop)) in enumerate(passes):
                    multiply_z(b, c, bank, first, start, stop, place == 0, place == len(passes) - 1)
                copy_out(y[c][:, first:end], bank[:])


        gate = {}
        kept = {}

        def doc_pieces(c):
            return [(0, DOCS // 2), (DOCS // 2, DOCS)] if c == N // P - 1 else [(0, DOCS)]

        stay = {}

        def pick_right(c):
            right = keep.tile([P, DOCS], F32, name=f"right_{c}", tag=f"right_{c}", align_bytes=DMA_ALIGN)
            nc.vector.tensor_copy(right[:], y[c][:].indirect(pos4_t[:]))
            stay[c] = keep.tile([P, DOCS], F32, name=f"stay_{c}")
            gate[c] = keep.tile([P, DOCS], F32, name=f"gate_{c}")
            kept[c] = keep.tile([P, DOCS], F32, name=f"kept_{c}")
            sigmoids = [(stay[c], -1.0), (gate[c], 1.0)]
            for dst, sign in reversed(sigmoids) if c == N // P - 1 else sigmoids:
                nc.scalar.activation(dst[:], right[:], ACT.Sigmoid, scale=sign)

        def pick_left(c, start, stop):
            nc.vector.tensor_tensor(
                kept[c][:, start:stop], y[c][:].indirect(entries_of(pos3_t, start, stop)), stay[c][:, start:stop], ALU.mult
            )

        def store_doc(c):
            doc = keep.tile([P, DOCS], F32, name=f"doc_{c}", tag=f"right_{c + 1}", align_bytes=DMA_ALIGN)
            for start, stop in doc_pieces(c):
                nc.vector.scalar_tensor_tensor(
                    doc[:, start:stop], gate[c][:, start:stop], w_col[:, c : c + 1], kept[c][:, start:stop], ALU.mult, ALU.add
                )
                nc.sync.dma_start(out[c * P : (c + 1) * P, start:stop], doc[:, start:stop])

        for c in range(N // P):
            pick_right(c)
            first_piece, *other_pieces = doc_pieces(c)
            pick_left(c, *first_piece)
            if c > 0:
                store_doc(c - 1)
            for piece in other_pieces:
                pick_left(c, *piece)
        store_doc(N // P - 1)
